import numpy as np, ml_dtypes
CORES = [16,18,20,22]
N = 4
BF = ml_dtypes.bfloat16
def gentries(a):
    return np.ascontiguousarray(a.reshape(8, 16, -1).transpose(0, 2, 1)).reshape(8, -1)
def gtable(e):
    e = np.asarray(e); return np.ascontiguousarray(e.reshape(8, -1, 16).transpose(0, 2, 1)).reshape(128, -1).astype(np.int32)
F, A, GI, D, E, RO = 3072, 3072, 2, 1024, 128, 3
L = GI + RO - 1
R = 16 // N
NE = [F] + [A] * GI + [D] * (RO - 1)
ST = [sum(NE[:e]) + e * E for e in range(L + 1)]
PO = [0] + [sum(NE[1:e]) for e in range(1, L + 1)]
W = ST[L] + NE[L]; M = GI * A + (RO - 1) * D
def cols(e):
    o = np.concatenate([np.arange(ST[k], ST[k] + NE[k]) for k in range(e)]); g = np.concatenate([np.arange(ST[k] + NE[k], ST[k] + NE[k] + E) for k in range(e)])
    return o, g
def parts(rng):
    h = rng.integers(0, 65536, (N, 8, 16, F)); t = rng.integers(0, 65536, (8, 16))
    s = np.zeros((N, 8, GI * A), np.int64); d = np.zeros((N, 8, M), np.int64); m = np.zeros((N, 8, L * E), np.int64)
    for e in range(1, L + 1):
        o, g = cols(e); p, n = PO[e], NE[e]
        if e <= GI: s[:, :, p:p + n] = rng.choice(o, (N, 8, n))
        d[:, :, p:p + n] = np.where(rng.random((N, 8, n)) < 0.25, rng.choice(g, (N, 8, n)), rng.choice(o, (N, 8, n)))
    for e in range(L): m[:, :, e * E:(e + 1) * E] = rng.integers(0, NE[e], (N, 8, E))
    return h, t, s, d, m
def pack(h, t, s, d, m):
    return {"trait": np.ascontiguousarray(h.reshape(N, 128, F)).astype(np.int32), "aim0": np.tile(t.reshape(1, 128, 1), (N, 1, 1)).astype(np.int32),
            "sire": np.stack([gtable(a) for a in s]), "dam": np.stack([gtable(a) for a in d]), "mg": np.stack([gtable(a) for a in m])}
def setup_inputs(rng):
    return pack(*parts(rng))
def plant(rng, h, t, s, d, m, g, j, up):
    t[g] = rng.integers(0, 1000, 16); low = rng.integers(1000, 5000, 14)
    for q in range(N):
        c = 1 + rng.permutation(F - 1); x, y, z, a0, a1, b = [int(v) for v in c[:6]]; rest = c[6:]
        w = rng.integers(20000, 55000, (16, F)); w[0] = rng.integers(60000, 65536, F); w[1] = rng.integers(2000, 40000, F)
        w[:2, [x, y, z, b]] = rng.integers(2000, 40000, (2, 4)); w[1, b] = rng.integers(60000, 65536); w[0, x] = 1000; w[1, y] = 1000
        w[2:, y] = rng.integers(1000, 5000, 14) + 5000 * (q % 2); w[2:, x] = w[2:, y] + 40000; w[2:, z] = rng.integers(60000, 65536, 14)
        w[2:, a0] = low; w[2:, a1] = low + up; w[2:, b] = low + 40000; h[q, g] = w
        col = a1
        for e in range(1, GI):
            k = int(rng.integers(0, A)); s[q, g, PO[e] + k] = a0; d[q, g, PO[e] + k] = col; col = ST[e] + k
        o = rng.choice(rest, A); k = rng.permutation(A)[:4]; o[k[:3]] = (x, y, z); p = PO[GI]
        s[q, g, p:p + A] = o; d[q, g, p:p + A] = o; s[q, g, p + k[3]] = a0; d[q, g, p + k[3]] = col
        v = rng.choice(rest, D); v[int(rng.integers(1, D - 1))] = ST[GI] + k[3]; v[j] = b
        d[q, g, PO[GI + 1]:PO[GI + 1] + D] = v; m[q, g, (GI + 1) * E] = j
def setup_inputs_ends(rng):
    h, t, s, d, m = parts(rng); t = rng.choice(np.array([0, 1, 32767, 65534, 65535]), (8, 16))
    for e in range(1, L + 1):
        o, g = cols(e); p, n = PO[e], NE[e]
        if e <= GI: s[:, 4:, p:p + n] = rng.choice(np.array([0, F - 1, o[-1]]), (N, 4, n))
        d[:, 4:, p:p + n] = rng.choice(np.array([0, F - 1, F, F + E - 1, o[-1], g[-1]]), (N, 4, n))
    for e in range(L): m[:, 4:, e * E:(e + 1) * E] = rng.choice(np.array([0, NE[e] - 1]), (N, 4, E))
    h[:, :4, :, 7] = t[:4]; h[:, :4, :, 9] = np.where(t[:4] < 32768, 65535, 0); a, z = (GI - 1) * A, GI * A - 1
    for g in range(4):
        x, y = (7, 9) if g < 2 else (9, 7)
        s[:, g, z] = x; d[:, g, z] = x; s[:, g, a] = y; d[:, g, a] = y
    plant(rng, h, t, s, d, m, 6, D - 1, 1); plant(rng, h, t, s, d, m, 7, 0, 0)
    return pack(h, t, s, d, m)
def setup_inputs_ghosts(rng):
    h, t, s, d, m = parts(rng)
    for e in range(1, L + 1):
        o, g = cols(e); p, n = PO[e], NE[e]
        d[:, 0::2, p:p + n] = rng.choice(g, (N, 4, n)); d[:, 1, p:p + n] = rng.choice(o, (N, n))
        d[:, 6, p:p + n] = rng.integers(ST[e] - E, ST[e], (N, n))
        if e > GI: d[:, 3, p:p + n] = rng.integers(ST[e - 1], ST[e - 1] + NE[e - 1], (N, n))
    d[:, 3, :GI * A] = s[:, 3]
    for e in range(L):
        m[:, 5, e * E:(e + 1) * E] = rng.integers(0, NE[e], (N, 1)); m[:, 7, e * E:(e + 1) * E] = NE[e] - 1
    return pack(h, t, s, d, m)
def setup_inputs_lines(rng):
    h, t, s, d, m = parts(rng); t[5] = rng.integers(0, 65536)
    for e in range(1, L + 1):
        p, n = PO[e], NE[e]; lo, hi = ST[e - 1], ST[e - 1] + NE[e - 1]
        if e <= GI:
            s[:, 0:2, p:p + n] = rng.integers(lo, hi, (N, 2, n)); s[:, 2:4, p:p + n] = rng.integers(0, F, (N, 2, n))
            s[:, 4, p:p + n] = np.where(rng.random((N, n)) < 0.9, rng.integers(lo, hi, (N, 1)), rng.integers(lo, hi, (N, n)))
            d[:, 7, p:p + n] = rng.integers(1, ST[e], (N, 1))
        d[:, 0::4, p:p + n] = rng.integers(lo, hi, (N, 2, n)); d[:, 1::4, p:p + n] = rng.integers(0, F, (N, 2, n))
        for g, k in ((2, 1), (3, 2), (6, 3)):
            y = min(k, e - 1); d[:, g, p:p + n] = rng.integers(ST[y], ST[y] + NE[y], (N, n))
    return pack(h, t, s, d, m)
def setup_inputs_spread(rng):
    h, t, s, d, m = parts(rng)
    h = np.minimum((np.exp2(17 * rng.random((N, 8, 1, F))) * rng.random((N, 8, 16, F))).astype(np.int64), 65535)
    t = np.minimum(np.exp2(16 * rng.random((8, 16))).astype(np.int64), 65535)
    for e in range(1, L + 1):
        o, g = cols(e); p, n = PO[e], NE[e]; o = rng.permutation(o); g = rng.permutation(g)
        if e <= GI: s[:, :, p:p + n] = o[(len(o) * rng.random((N, 8, n)) ** 4).astype(np.int64)]
        d[:, :, p:p + n] = np.where(rng.random((N, 8, n)) < 0.5, g[(len(g) * rng.random((N, 8, n)) ** 3).astype(np.int64)], o[(len(o) * rng.random((N, 8, n)) ** 3).astype(np.int64)])
    for e in range(L): m[:, :, e * E:(e + 1) * E] = (NE[e] * rng.random((N, 8, E)) ** 3).astype(np.int64)
    return pack(h, t, s, d, m)
def setup_inputs_ties(rng):
    h, t, s, d, m = parts(rng)
    h[:, 0] = 5; t[0] = rng.choice(np.array([3, 4, 1000, 60000]), 16)
    t[0, 14] = 5; h[:, 0, 14, 0] = 60000; t[0, 15] = 0; h[:, 0, 15] = 65535
    s[:, 0] = np.where(s[:, 0] == 0, 1, s[:, 0]); d[:, 0] = np.where(d[:, 0] == 0, 1, d[:, 0]); m[:, 0, :E] = np.where(m[:, 0, :E] == 0, 1, m[:, 0, :E])
    h[:, 1:3] = rng.choice(np.array([0, 1, 32768, 65535]), (N, 2, 16, F)); t[1:3] = rng.choice(np.array([0, 1, 32768, 65535]), (2, 16))
    h[:, 3:5, 8:] = h[:, 3:5, :8]; t[3:5, 8:] = t[3:5, :8]
    h[:, 5] = 65535 * rng.integers(0, 2, (N, 16, F)); t[5] = 65535 * rng.integers(0, 2, 16)
    h[:, 6] = h[:, 6][:, :, np.arange(F) % 16]
    t[7] = 32768; h[:, 7] = 32768 + 20000 * (2 * rng.integers(0, 2, (N, 16, F)) - 1)
    return pack(h, t, s, d, m)
def check_inputs(d):
    bad = []
    for k in ("trait", "aim0"):
        if np.min(d[k]) < 0 or np.max(d[k]) > 65535: bad.append("range of " + k)
    if np.any(d["aim0"] != d["aim0"][:1]): bad.append("aim0 alike on all ranks")
    s = np.stack([gentries(a) for a in d["sire"]]); w = np.stack([gentries(a) for a in d["dam"]]); m = np.stack([gentries(a) for a in d["mg"]])
    for e in range(1, GI + 1):
        if not np.all(np.isin(s[:, :, PO[e]:PO[e] + NE[e]], cols(e)[0])): bad.append("sires of generation " + str(e))
    for e in range(1, L + 1):
        x = w[:, :, PO[e]:PO[e] + NE[e]]
        if np.min(x) < 0 or np.max(x) >= ST[e]: bad.append("dams of generation " + str(e))
    for e in range(L):
        x = m[:, :, e * E:(e + 1) * E]
        if np.min(x) < 0 or np.max(x) >= NE[e]: bad.append("emigrants of generation " + str(e))
    return bad
def pick(w, ix):
    return np.take_along_axis(w, ix[:, :, None, :], 3)
def reference(trait, aim0, sire, dam, mg):
    h = trait.astype(np.int64).reshape(N, 8, 16, F); t = aim0.astype(np.int64).reshape(N, 8, 16, 1)
    sl = np.zeros((N, 8, M), np.int64); sl[:, :, :GI * A] = np.stack([gentries(a) for a in sire])
    dl = np.stack([gentries(a) for a in dam]).astype(np.int64); ml = np.stack([gentries(a) for a in mg]).astype(np.int64)
    top = np.zeros((N, 8, W), np.int64); top[:, :, :F] = np.arange(F)
    for e in range(1, GI + 1): top[:, :, ST[e]:ST[e] + NE[e]] = np.take_along_axis(top, sl[:, :, PO[e]:PO[e] + NE[e]], 2)
    f = np.zeros((N, 8, 16, W)); aims = []
    for rnd in range(1, RO + 1):
        new = GI + rnd - 1
        for e in range(new + 1):
            a, n, p = ST[e], NE[e], PO[e]
            if e == 0: f[:, :, :, :F] = 65535 - np.abs(h - t)
            else: f[:, :, :, a:a + n] = (pick(f, sl[:, :, p:p + n]) + pick(f, dl[:, :, p:p + n])) * 0.5
            if e < L: f[:, :, :, a + n:a + n + E] = np.roll(pick(f[:, :, :, a:a + n], ml[:, :, e * E:(e + 1) * E]), 1, axis=0)
        if rnd == RO: break
        a, n = ST[new], NE[new]; x = f[:, :, :, a:a + n]
        best = a + np.argmax(x, axis=3); least = a + np.argmin(x, axis=3)
        b, p = ST[new + 1], PO[new + 1]
        row = np.argmin(pick(f, dl[:, :, p:p + D]), axis=2)
        sl[:, :, p:p + D] = np.take_along_axis(best, row, 2)
        old = np.take_along_axis(h, np.take_along_axis(top, least, 2)[:, :, :, None], 3)[:, :, :, 0]
        top[:, :, b:b + D] = np.take_along_axis(top, sl[:, :, p:p + D], 2)
        t1 = np.stack([old[m // R, :, m] for m in range(16)], axis=1)
        t = np.tile(t1.reshape(1, 8, 16, 1), (N, 1, 1, 1)); aims.append(t.reshape(N, 128))
    made = np.concatenate([f[:, :, :, ST[e]:ST[e] + NE[e]] for e in range(GI + 1, L + 1)], axis=3)
    return {"yf": made.reshape(N, 128, (RO - 1) * D).astype(np.float32), "ys": np.stack([gtable(a) for a in sl[:, :, GI * A:]]).astype(np.float32), "yt": np.stack(aims, axis=2).astype(np.float32)}

@@ -1,0 +1,620 @@
+from concourse.bass import DstId, RemoteDMATransfer
+from concourse.mybir import AluOpType, AxisListType, ActivationFunctionType
+
+ALU = AluOpType
+AF = ActivationFunctionType
+F32, I32, U16, B16 = "float32", "int32", "uint16", "bfloat16"
+Z0 = 8
+OWN1 = Z0 + 6272
+G1 = Z0 + 6272
+E1 = Z0 + 6400
+G2X = Z0 + 6400
+X3 = Z0 + 6528
+G3X = Z0 + 7552
+TW = Z0 + 7680
+WW = 3080
+KP = 512
+VD = 1024
+CUT = 2048
+
+
+def _sb(n, d=F32):
+    return ("sbuf", [128, n], d)
+
+
+SCRATCH = {
+    "sireI": _sb(384, I32), "damI": _sb(528, I32), "mgI": _sb(32, I32), "aimI": _sb(1, I32),
+    "trI": _sb(3072, I32), "W": _sb(WW, I32),
+    "y1": _sb(3200), "FH": _sb(3200), "tabA": _sb(TW), "tabB": _sb(TW),
+    "tmp": _sb(3072), "tmp2": _sb(1024), "D2": _sb(2048), "DT": _sb(1024), "KS": _sb(1024), "CF": _sb(2304),
+    "T3": _sb(1024), "T4": _sb(1024), "key": _sb(1024), "G3": _sb(1024),
+    "yo": _sb(2048), "sf": _sb(2048), "sy": _sb(1024), "seg": _sb(1024), "zero": _sb(512),
+    "io": _sb(512), "dmj": _sb(512), "mk": _sb(512), "msc": _sb(512), "junk": _sb(3072, B16),
+    "Y": _sb(143), "Gm": _sb(128), "blk": _sb(128), "bs1": _sb(128), "bd1": _sb(128), "bs2": _sb(128), "bd2": _sb(128),
+    "ident": _sb(128), "idm": _sb(128), "id8": _sb(128), "ZS": _sb(143), "ZD": _sb(143),
+    "w1": _sb(512), "w2": _sb(144), "w3": _sb(128),
+    "R00": _sb(128, B16), "R01": _sb(128, B16), "R10": _sb(128, B16), "R11": _sb(128, B16),
+    "pI": _sb(8, I32), "cc": _sb(32), "dmo": _sb(16), "dmh": _sb(16),
+    "sire16": _sb(384, U16), "dam16": _sb(384, U16), "mg16": _sb(32, U16), "ms16": _sb(32, U16),
+    "pos16": _sb(144, U16), "US16": _sb(128, U16), "UD16": _sb(128, U16), "row16": _sb(128, U16), "sm16": _sb(64, U16),
+    "EI": _sb(144, I32), "AI": _sb(144, I32), "EF": _sb(144), "EG": _sb(144), "EM": _sb(144),
+    "pp": _sb(144), "qq": _sb(144), "is2": _sb(144), "mn": _sb(128), "x1": _sb(128),
+    "gs": _sb(1152), "gt": _sb(768), "ri": _sb(64, I32), "rb": _sb(64, I32), "rbf": _sb(64, B16),
+    "bT": _sb(32), "bR": _sb(32), "bg": _sb(16), "bm": _sb(32), "bsc": _sb(32), "Ub": _sb(16), "ub1": _sb(16), "HB": _sb(16),
+    "cl": _sb(64), "ci": _sb(64, I32), "lk": _sb(128), "land1": _sb(16), "land2": _sb(16),
+    "off16": _sb(16, U16), "i16": _sb(16), "nm": _sb(256), "bg2": _sb(16), "bm2": _sb(16), "yt16": _sb(16),
+    "yso": _sb(128), "yto": _sb(2),
+}
+del SCRATCH["DT"], SCRATCH["KS"]
+BANKS = ("pC", "pS", "pD", "pM", "pY", "pA", "pB", "pE")
+for _b in BANKS:
+    SCRATCH[_b] = ("psum", [128, 512], F32)
+SEMAPHORES = ["qV", "qA", "qP", "qG", "sent", "l_sire", "l_sire2", "l_dam0", "l_dam1", "l_dam2", "l_mg", "l_aim",
+              "l_t0", "l_t1", "l_t2", "l_t3", "l_w", "l_w2", "l_tr", "o_ys", "o_yt", "o_f3", "o_f4a", "o_f4b", "o_f4c",
+              "a_g0", "a_g11", "a_g12", "a_g13", "a_g21", "a_g22", "a_g23", "a_g32", "a_g33", "a_aim1", "a_aim2"]
+
+
+def rank_program(g, core, T, topo):
+    rank = T.rank_of(core)
+    if rank is None:
+        return
+    N = len(T.cores)
+    nxt = T.cores[(rank + 1) % N]
+    Q = {"V": g.vector, "A": g.scalar, "P": g.tensor, "G": g, "S": g.sync}
+    SEM = {"V": "qV", "A": "qA", "P": "qP", "G": "qG"}
+    cnt = {"V": 0, "A": 0, "P": 0, "G": 0}
+    known = {e: {} for e in Q}
+    recs = {}
+    clocks = {}
+    total = {}
+
+    def need(e, reads, writes, acc=False):
+        req = {}
+        for kind, regs in ((0, reads), (1, writes)):
+            for b, c0, c1 in regs:
+                for o0, o1, ow, sem, val, oe in recs.get(b, []):
+                    if o1 <= c0 or o0 >= c1 or (kind == 0 and not ow) or (oe == e and acc):
+                        continue
+                    req[sem] = max(req.get(sem, 0), val)
+        live = {s: v for s, v in req.items() if known[e].get(s, 0) < v}
+        for s in sorted(live):
+            if any(o != s and clocks.get((o, live[o]), {}).get(s, 0) >= live[s] for o in live):
+                continue
+            Q[e].wait_ge(T.sem[s], live[s])
+        for s, v in live.items():
+            known[e][s] = max(known[e].get(s, 0), v)
+            for o, w in clocks.get((s, v), {}).items():
+                known[e][o] = max(known[e].get(o, 0), w)
+
+    def note(e, reads, writes, sem, val):
+        clocks[(sem, val)] = dict(known[e]) if e in known else {}
+        total[sem] = val
+        for b, c0, c1 in writes:
+            keep = [r for r in recs.get(b, []) if not (c0 <= r[0] and r[1] <= c1)]
+            keep.append((c0, c1, True, sem, val, e))
+            recs[b] = keep
+        for b, c0, c1 in reads:
+            keep = [r for r in recs.get(b, []) if not (not r[2] and r[5] == e and c0 <= r[0] and r[1] <= c1)]
+            keep.append((c0, c1, False, sem, val, e))
+            recs[b] = keep
+
+    def reg(x):
+        return (x[0], 0, 512) if x[0] in BANKS else (x[0], x[1], x[2])
+
+    def ap(x):
+        if len(x) == 4:
+            return T[x[0]][:, x[1]:x[2]:x[3]]
+        return T[x[0]][:, x[1]:x[2]]
+
+    def op(e, fn, reads, writes, acc=False):
+        rd, wr = [reg(x) for x in reads], [reg(x) for x in writes]
+        need(e, rd, wr, acc)
+        cnt[e] += 1
+        fn().then_inc(T.sem[SEM[e]], 1)
+        note(e, rd, wr, SEM[e], cnt[e])
+
+    def src(x):
+        if len(x) == 2:
+            return ap(x[0]).indirect(ap(x[1])), [x[0], x[1]]
+        return ap(x), [x]
+
+    def copy(out, a):
+        s, rd = src(a)
+        op("V", lambda: g.vector.tensor_copy(ap(out), s), rd, [out])
+
+    def tt(out, a, b, alu):
+        s, rd = src(a)
+        op("V", lambda: g.vector.tensor_tensor(ap(out), s, ap(b), alu), rd + [b], [out])
+
+    def ts(out, a, s1, o1, s2=None, o2=None):
+        s, rd = src(a)
+        v1 = ap(s1) if isinstance(s1, tuple) else s1
+        v2 = ap(s2) if isinstance(s2, tuple) else s2
+        rd = rd + [x for x in (s1, s2) if isinstance(x, tuple)]
+        if o2 is None:
+            op("V", lambda: g.vector.tensor_scalar(ap(out), s, v1, None, o1), rd, [out])
+        else:
+            op("V", lambda: g.vector.tensor_scalar(ap(out), s, v1, v2, o1, o2), rd, [out])
+
+    def red(out, a, alu=ALU.add):
+        op("V", lambda: g.vector.tensor_reduce(ap(out), ap(a), AxisListType.X, alu), [a], [out])
+
+    def fill(a, v):
+        op("V", lambda: g.vector.memset(ap(a), v), [], [a])
+
+    def turn(out, a):
+        op("V", lambda: g.vector.transpose(ap(out), ap(a)), [a], [out])
+
+    def scan(out, d0, d1, init, o0, o1):
+        iv = ap(init) if isinstance(init, tuple) else init
+        rd = [d0, d1] + ([init] if isinstance(init, tuple) else [])
+        op("V", lambda: g.vector.tensor_tensor_scan(ap(out), ap(d0), ap(d1), iv, o0, o1), rd, [out])
+
+    def act(out, a, func, bias=0.0, scale=1.0, accum=None):
+        s, rd = src(a)
+        bv = ap(bias) if isinstance(bias, tuple) else bias
+        sv = ap(scale) if isinstance(scale, tuple) else scale
+        rd = rd + [x for x in (bias, scale) if isinstance(x, tuple)]
+        if accum is None:
+            op("A", lambda: g.scalar.activation(ap(out), s, func, bias=bv, scale=sv), rd, [out])
+        else:
+            op("A", lambda: g.scalar.activation(ap(out), s, func, bias=bv, scale=sv, accum_out=ap(accum)), rd, [out, accum])
+
+    def mm(out, lhsT, rhs, start=True, stop=True):
+        op("P", lambda: g.tensor.matmul(ap(out), ap(lhsT), ap(rhs), start, stop), [lhsT, rhs], [out], acc=True)
+
+    def iota(out, pattern, base, cm):
+        if out[0] in ("pI", "W"):
+            op("G", lambda: g.iota(ap(out), pattern, base, cm), [], [out])
+        else:
+            op("G", lambda: g.iota(ap(out), pattern, base, cm, allow_small_or_imprecise_dtypes=True), [], [out])
+
+    def dma(e, pairs, sem, reads, writes):
+        need(e, reads, writes)
+        for o, i in pairs:
+            Q[e].dma_start(o, i).then_inc(T.sem[sem], 16)
+        note("D" + sem, reads, writes, sem, 16 * len(pairs))
+
+    engs = [e for e in topo.engines(core, nxt) if all(e in topo.engines(core, c) for c in T.cores if c != core)]
+    mask = sum(1 << e for e in engs)
+    sent = [0]
+
+    def ship(buf, a, b, out, oa, ob, sem):
+        need("G", [(buf, a, b)], [])
+        rid, pid, _ = topo.addr(nxt)
+        g.remote_dma(out_ap=T[out][:, oa:ob], in_ap=T[buf][:, a:b], remote_sem=T.sem[sem], local_sem=T.sem.sent,
+                     pid=pid, routing_id=rid, dma_engine_mask=mask)
+        sent[0] += len(engs)
+        note("R", [], [(out, oa, ob)], sem, len(engs))
+
+    def share_aim(land, sem):
+        need("G", [(land, 4 * rank, 4 * rank + 1)], [])
+        others = [c for c in T.cores if c != core]
+        ids = [DstId(rid=topo.addr(c)[0], pnc=topo.addr(c)[1]) for c in others]
+        a = T[land][:, 4 * rank:4 * rank + 1]
+        g.remote_dma_fused([RemoteDMATransfer(dst_ids=ids, dma_engine_mask=mask, remote_sem=T.sem[sem], srcs=[a],
+                                              dsts=[a for c in others])], local_sem=T.sem.sent)
+        sent[0] += len(engs)
+        for k in range(N):
+            if k != rank:
+                note("R", [], [(land, 4 * k, 4 * k + 1)], sem, len(engs) * (N - 1))
+
+    dma("A", [(T.damI[:, 384:512], T.dam[:, 384:512])], "l_dam1", [], [("damI", 384, 512)])
+    dma("S", [(T.mgI[:], T.mg[:])], "l_mg", [], [("mgI", 0, 32)])
+    dma("S", [(T.aimI[:], T.aim0[:])], "l_aim", [], [("aimI", 0, 1)])
+    dma("A", [(T.trI[:, 0:768], T.trait[:, 0:768])], "l_t0", [], [("trI", 0, 768)])
+    dma("A", [(T.trI[:, 768:1536], T.trait[:, 768:1536])], "l_t1", [], [("trI", 768, 1536)])
+    dma("A", [(T.trI[:, 1536:2304], T.trait[:, 1536:2304])], "l_t2", [], [("trI", 1536, 2304)])
+    dma("A", [(T.trI[:, 2304:3072], T.trait[:, 2304:3072])], "l_t3", [], [("trI", 2304, 3072)])
+    dma("S", [(T.sireI[:, 0:192], T.sire[:, 0:192])], "l_sire", [("trI", 768, 1536)], [("sireI", 0, 192)])
+    dma("S", [(T.damI[:, 0:192], T.dam[:, 0:192])], "l_dam0", [], [("damI", 0, 192)])
+    iota(("pI", 0, 1), [[0, 1]], 0, 1)
+    iota(("Gm", 0, 128), [[16, 8], [0, 16]], 0, 0)
+    iota(("Y", 0, 143), [[1, 143]], 0, -1)
+    iota(("io", 0, 512), [[0, 32], [1, 16]], 0, 0)
+    iota(("W", 800, WW), [[0, WW - 800]], 0, 0)
+    iota(("zero", 0, 512), [[0, 512]], 0, 0)
+    iota(("tabA", 0, Z0), [[0, Z0]], 0, 0)
+    iota(("tabB", 0, Z0), [[0, Z0]], 0, 0)
+    fill(("W", 0, 800), 0)
+    own = [4 * rank + k for k in range(4)]
+    d1, s2, d2 = [(4 * rank + 4 + k) % 16 for k in range(3)]
+    wp = [(T.W[own[0]:128:16, 8:WW], T.sire[:, 0:192])]
+    wp.append((T.W[d1:128:16, 8:WW], T.dam[:, 0:192]))
+    wp.append((T.W[s2:128:16, 8:WW], T.sire[:, 192:384]))
+    wp.append((T.W[d2:128:16, 8:WW], T.dam[:, 192:384]))
+    dma("S", wp, "l_w", [], [("W", 8, WW)])
+    dma("S", [(T.sireI[:, 192:384], T.sire[:, 192:384])], "l_sire2", [], [("sireI", 192, 384)])
+    dma("S", [(T.damI[:, 192:384], T.dam[:, 192:384])], "l_dam2", [], [("damI", 192, 384)])
+
+    PM, PG, OWN, KB, PS1, PD1, PS2, PD2, Y0, Y1, T1, HOWN, NS2, ND2, NY0, NY1 = [("cc", k, k + 1) for k in range(16)]
+    ts(("pI", 1, 2), ("pI", 0, 1), 15, ALU.bitwise_and)
+    ts(("pI", 3, 4), ("pI", 0, 1), 16, ALU.bitwise_and, 4, ALU.logical_shift_right)
+    copy(PM, ("pI", 1, 2))
+    ts(("pI", 2, 3), ("pI", 1, 2), 2, ALU.logical_shift_right)
+    copy(Y1, ("pI", 3, 4))
+    tt(PG, ("pI", 0, 1), PM, ALU.subtract)
+    ts(OWN, ("pI", 2, 3), float(rank), ALU.is_equal)
+    ts(HOWN, ("pI", 2, 3), float(rank), ALU.is_equal, 0.5, ALU.mult)
+    for col, r in ((PS1, own[0]), (PD1, d1), (PS2, s2), (PD2, d2)):
+        ts(col, PM, float(r), ALU.is_equal)
+    for col, r in ((NS2, s2), (ND2, d2)):
+        ts(col, PM, float(r), ALU.is_equal, -1.0, ALU.mult)
+    ts(KB, PM, -1.0 / 64, ALU.mult, 15.0 / 64, ALU.add)
+    ts(Y0, Y1, -1.0, ALU.mult, 1.0, ALU.add)
+    ts(NY1, Y1, -1.0, ALU.mult)
+    ts(NY0, Y1, -1.0, ALU.add)
+    act(("w3", 0, 128), ("Gm", 0, 128), AF.Abs, PG, -1.0)
+    act(("blk", 0, 128), ("w3", 0, 128), AF.Relu, 1.0, -1.0)
+    for b, col in (("bs1", PS1), ("bd1", PD1), ("bs2", PS2), ("bd2", PD2)):
+        act((b, 0, 128), ("blk", 0, 128), AF.Identity, 0.0, col)
+    for zb, k, m, nm in (("ZS", 15 - s2, PS2, NS2), ("ZD", 15 - d2, PD2, ND2)):
+        act(("w2", 0, 143), ("Y", 0, 143), AF.Abs, float(-k))
+        act((zb, 0, 143), ("w2", 0, 143), AF.Relu, m, nm)
+    act(("w1", 0, 512), ("io", 0, 512), AF.Abs, PM, -1.0)
+    act(("dmj", 0, 512), ("w1", 0, 512), AF.Relu, 1.0, -1.0)
+    act(("seg", 0, 512), ("io", 0, 512), AF.Sign)
+    act(("w3", 0, 128), ("Y", 0, 128), AF.Abs)
+    act(("ident", 0, 128), ("w3", 0, 128), AF.Relu, 1.0, -1.0)
+    act(("idm", 0, 128), ("ident", 0, 128), AF.Identity, 0.0, -6400.0)
+    act(("id8", 0, 128), ("ident", 0, 128), AF.Identity, 0.0, -float(Z0))
+    copy(("mg16", 0, 32), ("mgI", 0, 32))
+    ts(("damI", 512, 520), ("mgI", 16, 24), 6400.0, ALU.add)
+    ts(("damI", 520, 528), ("mgI", 8, 16), 6400.0, ALU.add)
+    A144 = (0, 144)
+    ts(("EI",) + A144, ("damI", 384, 528), -6400.0, ALU.add, 0.0, ALU.max)
+    ts(("AI",) + A144, ("EI",) + A144, 15, ALU.bitwise_and)
+    ts(("EF",) + A144, ("AI",) + A144, 3071.0, ALU.mult, 128.0, ALU.add)
+    tt(("EG",) + A144, ("EF",) + A144, ("EI",) + A144, ALU.add)
+    ts(("pp",) + A144, ("damI", 384, 528), 6400.0, ALU.is_ge)
+    ts(("qq",) + A144, ("damI", 384, 528), 9472.0, ALU.is_ge)
+    tt(("is2",) + A144, ("pp",) + A144, ("qq",) + A144, ALU.subtract)
+    tt(("EM",) + A144, ("EG",) + A144, ("is2",) + A144, ALU.mult)
+    ts(("pos16",) + A144, ("EM",) + A144, 0.0625, ALU.mult)
+    copy(T1, ("aimI", 0, 1))
+
+    def y_chunk(k):
+        a, b = 768 * k, 768 * k + 768
+        ts(("y1", a, b), ("trI", a, b), T1, ALU.subtract)
+
+    def f(n):
+        return (n, 0, 128)
+
+    y_chunk(0)
+    y_chunk(1)
+    y_chunk(2)
+    ts(("gs", 0, 128), (("trI", 0, 3072), ("mg16", 0, 8)), T1, ALU.subtract)
+    ship("gs", 0, 128, "y1", 3072, 3200, "a_g0")
+    y_chunk(3)
+    copy(("sire16", 0, 192), ("sireI", 0, 192))
+    copy(("dam16", 0, 192), ("damI", 0, 192))
+    dma("S", [(T.trI[r:128:16, 0:3072], T.sire[:, 192:384]) for r in own], "l_tr", [], [("trI", 0, 3072)])
+    for k in range(4):
+        act(("FH", 768 * k, 768 * k + 768), ("y1", 768 * k, 768 * k + 768), AF.Abs, 0.0, 0.5)
+
+    c = ("damI", 384, 512)
+    ts(f("mn"), c, 6400.0, ALU.min)
+    ts(f("x1"), c, -9472.0, ALU.add, 0.0, ALU.max)
+    ts(("tabA", Z0, Z0 + VD), ("FH", 0, VD), 2.0, ALU.mult)
+    copy(("CF", 2048, 2304), (("W", 0, WW), ("pos16", 128, 144)))
+    mm(("pC", 0, 128), ("bs1", 0, 128), ("CF", 2176, 2304))
+    mm(("pC", 128, 256), ("bd1", 0, 128), ("CF", 2176, 2304))
+    mm(("pC", 256, 384), ("bs2", 0, 128), ("CF", 2048, 2176))
+    mm(("pC", 384, 512), ("bd2", 0, 128), ("CF", 2048, 2176))
+    copy(("CF", 0, 1024), (("W", 0, WW), ("pos16", 0, 64)))
+    tt(("mk", 0, 512), ("pC", 0, 512), ("dmj", 0, 512), ALU.mult)
+    scan(("msc", 0, 512), ("seg", 0, 512), ("mk", 0, 512), 0.0, ALU.mult, ALU.add)
+    copy(("ms16", 0, 32), ("msc", 15, 512, 16))
+    MS1, MD1, MS2, MD2 = [("ms16", 8 * k, 8 * k + 8) for k in range(4)]
+
+    def to_list(pb, z, flat, f0, o0, more=()):
+        for i in range(16):
+            mm((pb, o0, o0 + 64), (z, 15 - i, 143 - i), (flat, f0 + i, f0 + 1024, 16), i == 0, i == 15 and not more)
+        for k, (w, x) in enumerate(more):
+            mm((pb, o0, o0 + 64), (w, 0, 128), (x, o0, o0 + 64), False, k == len(more) - 1)
+
+    def list_s(h):
+        to_list("pS", "ZS", "CF", 1024 * h, 64 * h, (("ident", "mn"), ("idm", "pp"), ("id8", "qq")))
+
+    def list_d(h):
+        to_list("pD", "ZD", "CF", 1024 * h, 64 * h, (("ident", "mn"), ("ident", "x1"), ("idm", "is2")))
+
+    def u_lists(h):
+        v = lambda n: (n, 64 * h, 64 * h + 64)
+        ts(v("US16"), v("pS"), float(Z0), ALU.add)
+        copy(v("UD16"), v("pD"))
+
+    list_s(0)
+    list_d(0)
+
+    PART = [0]
+    for n in (512, 768, 896, 896):
+        PART.append(PART[-1] + n)
+
+    def sires1(k):
+        a, b = PART[k], PART[k + 1]
+        act(("tmp", a, b), (("FH", 0, 3072), ("sire16", a // 16, b // 16)), AF.Identity)
+
+    def dams1(tab, k):
+        a, b = PART[k], PART[k + 1]
+        tt((tab, Z0 + 3200 + a, Z0 + 3200 + b), (("FH", 0, 3200), ("dam16", a // 16, b // 16)), ("tmp", a, b), ALU.add)
+
+    def ghosts1_act(r):
+        act(("gt", 128 * r - 128, 128 * r), (("FH", 0, 3072), MS1), AF.Identity)
+
+    def ghosts1(r, tab):
+        o = 128 * r
+        tt(("gs", o, o + 128), (("FH", 0, 3200), MD1), ("gt", o - 128, o), ALU.add)
+        ship("gs", o, o + 128, tab, G1, G1 + 128, "a_g1%d" % r)
+
+    def ghosts2_act(r, tab):
+        act(("gt", 384 + 128 * (r - 1), 384 + 128 * r), ((tab, Z0, OWN1), MS2), AF.Identity)
+
+    def ghosts2(r, tab):
+        o = 384 + 128 * r
+        tt(("gs", o, o + 128), ((tab, Z0, E1), MD2), ("gt", 384 + 128 * (r - 1), 384 + 128 * r), ALU.add)
+        ship("gs", o, o + 128, tab, G2X, G2X + 128, "a_g2%d" % r)
+
+    def double3(tab):
+        act((tab, X3, X3 + 1024), ("G3", 0, 1024), AF.Identity, 0.0, 0.5)
+
+    def ghosts3(r, tab):
+        o = 896 + 128 * (r - 2)
+        ts(("gs", o, o + 128), (("G3", 0, 1024), ("mg16", 24, 32)), 0.5, ALU.mult)
+        ship("gs", o, o + 128, tab, G3X, G3X + 128, "a_g3%d" % r)
+
+    tab = "tabA"
+    sires1(0)
+    sires1(1)
+    sires1(2)
+    act(("FH", 3072, 3200), ("y1", 3072, 3200), AF.Abs, 0.0, 0.5)
+    dams1(tab, 0)
+    act(("dmo", 0, 16), ("dmj", 0, 16), AF.Identity, 0.0, OWN)
+    act(("dmh", 0, 16), ("dmj", 0, 16), AF.Identity, 0.0, HOWN)
+    act(("i16", 0, 16), ("io", 0, 16), AF.Identity, 0.0, 0.0625)
+    act(("nm", 0, 256), ("dmj", 0, 256), AF.Identity, 1.0e9, -1.0e9)
+    ghosts1_act(1)
+    ghosts1(1, tab)
+    dams1(tab, 1)
+    sires1(3)
+    act((tab, Z0 + VD, Z0 + 3200), ("y1", VD, 3200), AF.Abs)
+    dams1(tab, 2)
+    dams1(tab, 3)
+    REST = [(CUT + 512 * k, CUT + 512 * k + 512, pb) for k, pb in enumerate(("pA", "pB"))]
+    HALF = [(0, CUT // 2), (CUT // 2, CUT)]
+    copy(("sire16", 192, 384), ("sireI", 192, 384))
+    copy(("dam16", 192, 384), ("damI", 192, 384))
+    for a, b in HALF:
+        act(("tmp", a, b), ((tab, Z0, OWN1), ("sire16", 192 + a // 16, 192 + b // 16)), AF.Identity)
+    ghosts2_act(1, tab)
+    for a, b, pb in REST:
+        act(("tmp", a, b), ((tab, Z0, OWN1), ("sire16", 192 + a // 16, 192 + b // 16)), AF.Identity)
+        mm((pb, 0, 512), ("ident", 0, 128), ("tmp", a, b), True, False)
+    for a, b, pb in REST:
+        act(("tmp2", a - CUT, b - CUT), ((tab, Z0, E1), ("dam16", 192 + a // 16, 192 + b // 16)), AF.Identity)
+        mm((pb, 0, 512), ("ident", 0, 128), ("tmp2", a - CUT, b - CUT), False, True)
+    copy(("CF", 1024, 2048), (("W", 0, WW), ("pos16", 64, 128)))
+    dma("S", [(T.W[q:128:16, 8:WW], T.sire[:, 0:192]) for q in own[1:]], "l_w2", [], [("W", 8, WW)])
+    for a, b in HALF:
+        tt(("D2", a, b), ((tab, Z0, E1), ("dam16", 192 + a // 16, 192 + b // 16)), ("tmp", a, b), ALU.add)
+    ghosts2(1, tab)
+    u_lists(0)
+    act(("T3", 0, 1024), ((tab, 0, E1), ("US16", 0, 64)), AF.Identity, KB)
+    act(("T4", 0, KP), ((tab, Z0, X3), ("UD16", 0, KP // 16)), AF.Identity)
+    mm(("pC", 0, KP), ("ident", 0, 128), ("T3", 0, KP), True, False)
+    mm(("pC", 0, KP), ("ident", 0, 128), ("T4", 0, KP), False, True)
+    JL, JB = [("cl", k, k + 1) for k in (0, 1)], [("cl", k, k + 1) for k in (2, 3)]
+    scan(("tmp", 0, CUT), ("D2", 0, CUT), ("D2", 0, CUT), 0.0, ALU.max, ALU.max)
+    scan(("FH", 0, CUT), ("D2", 0, CUT), ("D2", 0, CUT), 1.0e9, ALU.min, ALU.min)
+    K, K2, LAST = ("cl", 8, 9), ("cl", 9, 10), ("tmp", 3071, 3072)
+    for out, alu in (("tmp", ALU.max), ("FH", ALU.min)):
+        for n, (a, b, pb) in enumerate(REST):
+            scan((out, a, b), (pb, 0, 512), ("zero", 0, 512), (out, a - 1, a), alu, ALU.add)
+            if out == "FH" and n == 0:
+                act(("junk", 0, 192), ("tmp", 15, 3072, 16), AF.Sign, LAST, -1.0, K)
+                ts(("off16", 0, 16), ("i16", 0, 16), K, ALU.add, 16.0, ALU.mult)
+                tt(("mk", 0, 256), (("tmp", 0, 3072), ("off16", 0, 16)), ("nm", 0, 256), ALU.max)
+                act(("junk", 0, 256), ("mk", 0, 256), AF.Sign, LAST, -1.0, K2)
+    act(("seg", 512, 1024), ("io", 0, 512), AF.Sign)
+    for k in (-1, 0, 1):
+        act(("w3", 0, 128), ("Y", 0, 128), AF.Abs, float(-16 * k))
+        for y, m, nm in ((0, Y0, NY0), (1, Y1, NY1)):
+            if 0 <= y + k < 2:
+                act(("R%d%d" % (y, y + k), 0, 128), ("w3", 0, 128), AF.Relu, m, nm)
+    ts(JL[0], K, 16.0, ALU.mult, K2, ALU.add)
+    act(("junk", 0, 3072), ("FH", 0, 3072), AF.Sign, ("FH", 3071, 3072), -1.0, JB[0])
+
+    def founder_a(s, n):
+        b = lambda k: ("cl", n + k, n + k + 1)
+        ib = lambda k: ("ci", n + k, n + k + 1)
+        ts(ib(0), s, -3200.0, ALU.add, 0.0, ALU.max)
+        ts(b(0), s, 3200.0, ALU.is_lt, s, ALU.mult)
+        ts(ib(1), ib(0), 15, ALU.bitwise_and)
+        ts(b(1), ib(0), 0.0625, ALU.mult)
+        ts(b(2), s, 3200.0, ALU.is_ge)
+        ts(("sm16", n, n + 1), ib(1), 191.9375, ALU.mult, b(1), ALU.add)
+        return ("sm16", n, n + 1)
+
+    def founder_b(n):
+        ts(("sm16", n + 2, n + 3), ("cl", n + 3, n + 4), ("cl", n + 2, n + 3), ALU.mult, ("cl", n, n + 1), ALU.add)
+        return ("sm16", n + 2, n + 3)
+
+    def chain1(land):
+        J = JL[0]
+        ts(("ci", 16, 17), J, 240.0, ALU.add)
+        ts(("cl", 16, 17), J, 0.0625, ALU.mult, 15.0, ALU.add)
+        ts(("ci", 17, 18), ("ci", 16, 17), 15, ALU.bitwise_and)
+        ts(("sm16", 16, 17), ("ci", 17, 18), 191.9375, ALU.mult, ("cl", 16, 17), ALU.add)
+        tt(("lk", 0, 16), (("trI", 0, 3072), ("sm16", 16, 17)), ("dmo", 0, 16), ALU.mult)
+        red(("cl", 17, 18), ("lk", 0, 16))
+        tt(("lk", 16, 32), (("W", 8, WW), founder_a(("cl", 17, 18), 20)), ("dmo", 0, 16), ALU.mult)
+        red(("cl", 23, 24), ("lk", 16, 32))
+        tt(("lk", 32, 48), (("y1", 0, 3072), founder_b(20)), ("dmh", 0, 16), ALU.mult)
+        red((land, 4 * rank, 4 * rank + 1), ("lk", 32, 48))
+
+    def best_lines_a():
+        copy(("bg2", 0, 16), (("W", 8, WW), founder_a(("bsc", 15, 16), 32)))
+        mm(("pM", 288, 304), ("bs1", 0, 128), ("bg2", 0, 16))
+
+    def best_lines_b():
+        tt(("bm2", 0, 16), ("pM", 288, 304), ("dmj", 0, 16), ALU.mult)
+        red(("cl", 35, 36), ("bm2", 0, 16))
+        copy(("yt16", 0, 16), (("y1", 0, 3072), founder_b(32)))
+
+    def chain2(land):
+        copy(("sm16", 40, 41), JL[1])
+        tt(("lk", 48, 64), (("sy", 0, 1024), ("sm16", 40, 41)), ("dmh", 0, 16), ALU.mult)
+        red((land, 4 * rank, 4 * rank + 1), ("lk", 48, 64))
+
+    chain1("land1")
+    share_aim("land1", "a_aim1")
+    tt(("key", KP, 1024), ((tab, Z0, X3), ("UD16", KP // 16, 64)), ("T3", KP, 1024), ALU.add)
+
+    def rows_a(k, between):
+        turn(("D2", 1024 + k, 2048), ("key", k, 1024))
+        if k:
+            turn(("D2", 1024, 1024 + k), ("pC", 0, k))
+        between()
+        scan(("D2", 0, 1024), ("seg", 0, 1024), ("D2", 1024, 2048), 0.0, ALU.mult, ALU.max)
+
+    def rows_b():
+        ts(("ri", 0, 64), ("D2", 15, 1024, 16), 64.0, ALU.mult)
+        ts(("rb", 0, 64), ("ri", 0, 64), 15, ALU.bitwise_and)
+        copy(("rbf", 0, 64), ("rb", 0, 64))
+        for y in range(2):
+            for h in range(2):
+                mm(("pM", 32 * y, 32 * y + 32), ("R%d%d" % (y, h), 0, 128), ("rbf", h, 64, 2), h == 0, h == 1)
+
+    def rows_c(c0):
+        for y in range(2):
+            ts(("row16", c0 + y, c0 + 64, 2), ("pM", 32 * y, 32 * y + 32), -1.0, ALU.mult, 15.0, ALU.add)
+
+    def best_a(r):
+        k = 16 * (r - 1)
+        ts(("bR", k, k + 16), ("dmj", 0, 16), JB[r - 1], ALU.mult, -1.0, ALU.mult)
+        mm(("pY", 128 + k, 144 + k), ("blk", 0, 128), ("bR", k, k + 16))
+
+    def best_b(r):
+        k = 16 * (r - 1)
+        copy(("bT", k, k + 16), ("pY", 128 + k, 144 + k))
+
+    def sire_act(r, a=0, b=1024):
+        k = 64 * (r - 1)
+        act(("sf", 16 * k + a, 16 * k + b), (("bT", 16 * (r - 1), 16 * r), ("row16", k + a // 16, k + b // 16)), AF.Identity)
+
+    def sire_cols(r):
+        to_list("pE", "ZS", "sf", 1024 * (r - 1), 64 * (r - 1))
+
+    BH = [("cl", 4, 5), ("cl", 5, 6)]
+
+    def outputs(r, first):
+        ts(("yso", 64 * (r - 1), 64 * r), ("pE", 64 * (r - 1), 64 * r), float(first), ALU.add)
+        ts(("yto", r - 1, r), BH[r - 1], 2.0, ALU.mult, T1, ALU.add)
+
+    def aims(r, land):
+        op("V", lambda: g.vector.tensor_reduce(ap(BH[r - 1]), T[land][:, 0:16:4], AxisListType.X, ALU.add),
+           [(land, 0, 16)], [BH[r - 1]])
+
+    rows_a(KP, lambda: aims(1, "land1"))
+    rows_b()
+    n = 48
+    best_a(1)
+    copy(("ci", n, n + 1), JB[0])
+    ts(("cl", n + 1, n + 2), JB[0], -0.0625, ALU.mult)
+    ts(("ci", n + 2, n + 3), ("ci", n, n + 1), -1.0, ALU.mult)
+    rows_c(0)
+    ts(("ci", n + 1, n + 2), ("ci", n + 2, n + 3), 15, ALU.bitwise_and)
+    ts(("sm16", n, n + 1), ("ci", n + 1, n + 2), 191.9375, ALU.mult, ("cl", n + 1, n + 2), ALU.add)
+    copy(("bg", 0, 16), (("W", 8, WW), ("sm16", n, n + 1)))
+    mm(("pM", 256, 272), ("bs2", 0, 128), ("bg", 0, 16))
+    mm(("pM", 272, 288), ("bd2", 0, 128), ("bg", 0, 16))
+    list_s(1)
+    best_b(1)
+    tt(("bm", 0, 32), ("pM", 256, 288), ("dmj", 0, 32), ALU.mult)
+    scan(("bsc", 0, 32), ("seg", 0, 32), ("bm", 0, 32), 0.0, ALU.mult, ALU.add)
+    copy(("sm16", n + 4, n + 8, 2), ("bsc", 15, 32, 16))
+    BS, BD = ("sm16", n + 4, n + 5), ("sm16", n + 6, n + 7)
+
+    def begin(r, tab):
+        bias = BH[r - 2]
+        for k in range(4):
+            act(("FH", 800 * k, 800 * k + 800), ("y1", 800 * k, 800 * k + 800), AF.Abs, bias, -0.5)
+        nv = 2 if r == 2 else 3
+        for k in range(nv):
+            ts((tab, Z0 + 800 * k, Z0 + 800 * k + 800), ("FH", 800 * k, 800 * k + 800), 2.0, ALU.mult)
+        for k in range(4):
+            sires1(k)
+            dams1(tab, k)
+            if k == 0:
+                ghosts1_act(r)
+                ghosts1(r, tab)
+                if r == 2:
+                    best_lines_a()
+                    list_d(1)
+        act((tab, Z0 + 800 * nv, Z0 + 3200), ("FH", 800 * nv, 3200), AF.Identity, 0.0, 2.0)
+        if r == 3:
+            sire_act(2, 0, 512)
+        ghosts2_act(r, tab)
+        copy(("ub1", 0, 16), ((tab, Z0, OWN1), BS))
+        tt(("Ub", 0, 16), ((tab, Z0, E1), BD), ("ub1", 0, 16), ALU.add)
+        ghosts2(r, tab)
+        if r == 2:
+            best_lines_b()
+        else:
+            outputs(1, 6400)
+        for k in range(2):
+            a, b = 512 * k, 512 * k + 512
+            act(("tmp2", a, b), (("Ub", 0, 16), ("row16", 32 * k, 32 * k + 32)), AF.Identity)
+            tt(("T3", a, b), ((tab, 0, E1), ("US16", 32 * k, 32 * k + 32)), ("tmp2", a, b), ALU.add)
+        if r == 2:
+            u_lists(1)
+            act(("sy", 0, 1024), (("yt16", 0, 16), ("row16", 0, 64)), AF.Identity)
+        else:
+            sire_act(2, 512, 1024)
+            sire_cols(2)
+        act(("T4", 0, 1024), ((tab, 0, E1), ("US16", 64, 128)), AF.Identity, KB if r == 2 else 0.0)
+        tt(("G3", 0, 1024), ((tab, Z0, X3), ("UD16", 0, 64)), ("T3", 0, 1024), ALU.add)
+
+    tab = "tabB"
+    begin(2, tab)
+    ghosts3(2, tab)
+    scan(("tmp", 0, 1024), ("G3", 0, 1024), ("G3", 0, 1024), 0.0, ALU.max, ALU.max)
+    double3(tab)
+    act(("junk", 0, 1024), ("tmp", 0, 1024), AF.Sign, ("tmp", 1023, 1024), -1.0, JL[1])
+    scan(("FH", 0, 1024), ("G3", 0, 1024), ("G3", 0, 1024), 1.0e9, ALU.min, ALU.min)
+    act(("junk", 0, 1024), ("FH", 0, 1024), AF.Sign, ("FH", 1023, 1024), -1.0, JB[1])
+    sire_act(1)
+    chain2("land2")
+    share_aim("land2", "a_aim2")
+    tt(("key", 0, 1024), ((tab, Z0, TW), ("UD16", 64, 128)), ("T4", 0, 1024), ALU.add)
+    rows_a(0, lambda: aims(2, "land2"))
+    rows_b()
+    best_a(2)
+    sire_cols(1)
+    ts(("sm16", 58, 59), JB[1], -1.0, ALU.mult)
+    rows_c(64)
+    best_b(2)
+
+    tab = "tabA"
+    begin(3, tab)
+    double3(tab)
+    ghosts3(3, tab)
+    ts(("HB", 0, 16), (("G3", 0, 1024), ("sm16", 58, 59)), 0.5, ALU.mult)
+    tt(("T3", 0, 1024), (("HB", 0, 16), ("row16", 64, 128)), ("T4", 0, 1024), ALU.add)
+    act(("yo", 0, 1024), ("G3", 0, 1024), AF.Identity, 65535.0, -0.25)
+    dma("S", [(T.yf[:, 0:1024], T.yo[:, 0:1024])], "o_f3", [("yo", 0, 1024)], [])
+    b = 0
+    for k, n in enumerate((384, 384, 256)):
+        a, b = b, b + n
+        tt(("key", a, b), ((tab, Z0, TW), ("UD16", 64 + a // 16, 64 + b // 16)), ("T3", a, b), ALU.add)
+        act(("yo", 1024 + a, 1024 + b), ("key", a, b), AF.Identity, 65535.0, -0.25)
+        dma("S", [(T.yf[:, 1024 + a:1024 + b], T.yo[:, 1024 + a:1024 + b])], "o_f4%s" % "abc"[k], [("yo", 1024 + a, 1024 + b)], [])
+        if k == 1:
+            outputs(2, 9600)
+            dma("S", [(T.ys[:], T.yso[:])], "o_ys", [("yso", 0, 128)], [])
+            dma("S", [(T.yt[:], T.yto[:])], "o_yt", [("yto", 0, 2)], [])
+
+    for s in sorted(total):
+        if known["G"].get(s, 0) < total[s]:
+            g.wait_ge(T.sem[s], total[s])
+    g.wait_ge(T.sem.sent, sent[0])

@@ -13,9 +13,9 @@ X3 = Z0 + 6528
 G3X = Z0 + 7552
 TW = Z0 + 7680
 WW = 3080
-KP = 512
-VD = 1024
-CUT = 2048
+WV = 1700
+D2 = Z0 + 3200
+VD = (1024, 1600, 2400)
 
 
 def _sb(n, d=F32):
@@ -26,31 +26,31 @@ SCRATCH = {
     "sireI": _sb(384, I32), "damI": _sb(528, I32), "mgI": _sb(32, I32), "aimI": _sb(1, I32),
     "trI": _sb(3072, I32), "W": _sb(WW, I32),
     "y1": _sb(3200), "FH": _sb(3200), "tabA": _sb(TW), "tabB": _sb(TW),
-    "tmp": _sb(3072), "tmp2": _sb(1024), "D2": _sb(2048), "DT": _sb(1024), "KS": _sb(1024), "CF": _sb(2304),
-    "T3": _sb(1024), "T4": _sb(1024), "key": _sb(1024), "G3": _sb(1024),
-    "yo": _sb(2048), "sf": _sb(2048), "sy": _sb(1024), "seg": _sb(1024), "zero": _sb(512),
-    "io": _sb(512), "dmj": _sb(512), "mk": _sb(512), "msc": _sb(512), "junk": _sb(3072, B16),
-    "Y": _sb(143), "Gm": _sb(128), "blk": _sb(128), "bs1": _sb(128), "bd1": _sb(128), "bs2": _sb(128), "bd2": _sb(128),
-    "ident": _sb(128), "idm": _sb(128), "id8": _sb(128), "ZS": _sb(143), "ZD": _sb(143),
-    "w1": _sb(512), "w2": _sb(144), "w3": _sb(128),
-    "R00": _sb(128, B16), "R01": _sb(128, B16), "R10": _sb(128, B16), "R11": _sb(128, B16),
+    "tmp": _sb(3072), "tmp2": _sb(1024), "CF": _sb(2304),
+    "T3": _sb(1024), "T4": _sb(1024), "key": _sb(1024), "G3": _sb(1024), "sg": _sb(1024),
+    "yo": _sb(2048), "sf": _sb(1024, B16), "sy": _sb(1024), "seg": _sb(512),
+    "io": _sb(512), "dmj": _sb(512), "mk": _sb(512), "msc": _sb(512), "junk": _sb(512, B16),
+    "blk": _sb(128), "bs1": _sb(128), "bd1": _sb(128), "bs2": _sb(128), "bd2": _sb(128),
+    "ident": _sb(128), "idm": _sb(128), "id8": _sb(128), "ZS": _sb(144), "ZD": _sb(144), "zero": _sb(144), "one": _sb(128),
+    "w1": _sb(512), "w3": _sb(128), "cix": _sb(256), "nmx": _sb(256), "nmn": _sb(256),
+    "zerob": _sb(144, B16), "idb": _sb(128, B16), "perm0": _sb(128, B16), "perm1": _sb(128, B16), "rT": _sb(128, B16),
+    "ZSb": _sb(144, B16), "ZB": _sb(144, B16), "bH": _sb(16, B16),
     "pI": _sb(8, I32), "cc": _sb(32), "dmo": _sb(16), "dmh": _sb(16),
     "sire16": _sb(384, U16), "dam16": _sb(384, U16), "mg16": _sb(32, U16), "ms16": _sb(32, U16),
     "pos16": _sb(144, U16), "US16": _sb(128, U16), "UD16": _sb(128, U16), "row16": _sb(128, U16), "sm16": _sb(64, U16),
     "EI": _sb(144, I32), "AI": _sb(144, I32), "EF": _sb(144), "EG": _sb(144), "EM": _sb(144),
     "pp": _sb(144), "qq": _sb(144), "is2": _sb(144), "mn": _sb(128), "x1": _sb(128),
-    "gs": _sb(1152), "gt": _sb(768), "ri": _sb(64, I32), "rb": _sb(64, I32), "rbf": _sb(64, B16),
+    "gs": _sb(1152), "gt": _sb(384), "ri": _sb(64, I32), "rb": _sb(64, I32), "rbf": _sb(64, B16),
     "bT": _sb(32), "bR": _sb(32), "bg": _sb(16), "bm": _sb(32), "bsc": _sb(32), "Ub": _sb(16), "ub1": _sb(16), "HB": _sb(16),
     "cl": _sb(64), "ci": _sb(64, I32), "lk": _sb(128), "land1": _sb(16), "land2": _sb(16),
-    "off16": _sb(16, U16), "i16": _sb(16), "nm": _sb(256), "bg2": _sb(16), "bm2": _sb(16), "yt16": _sb(16),
+    "off16": _sb(32, U16), "i16": _sb(16), "bg2": _sb(16), "bm2": _sb(16), "yt16": _sb(32),
     "yso": _sb(128), "yto": _sb(2),
 }
-del SCRATCH["DT"], SCRATCH["KS"]
 BANKS = ("pC", "pS", "pD", "pM", "pY", "pA", "pB", "pE")
 for _b in BANKS:
     SCRATCH[_b] = ("psum", [128, 512], F32)
 SEMAPHORES = ["qV", "qA", "qP", "qG", "sent", "l_sire", "l_sire2", "l_dam0", "l_dam1", "l_dam2", "l_mg", "l_aim",
-              "l_t0", "l_t1", "l_t2", "l_t3", "l_w", "l_w2", "l_tr", "o_ys", "o_yt", "o_f3", "o_f4a", "o_f4b", "o_f4c",
+              "l_t0", "l_t1", "l_t2", "l_t3", "l_w", "l_w2", "l_tr", "o_ys", "o_yt", "o_f3a", "o_f3b", "o_f4a", "o_f4b", "o_f4c",
               "a_g0", "a_g11", "a_g12", "a_g13", "a_g21", "a_g22", "a_g23", "a_g32", "a_g33", "a_aim1", "a_aim2"]
 
 
@@ -101,13 +101,14 @@ def rank_program(g, core, T, topo):
     def reg(x):
         return (x[0], 0, 512) if x[0] in BANKS else (x[0], x[1], x[2])
 
-    def ap(x):
+    def ap(x, rows=128):
         if len(x) == 4:
-            return T[x[0]][:, x[1]:x[2]:x[3]]
-        return T[x[0]][:, x[1]:x[2]]
+            return T[x[0]][0:rows, x[1]:x[2]:x[3]]
+        return T[x[0]][0:rows, x[1]:x[2]]
 
     def op(e, fn, reads, writes, acc=False):
         rd, wr = [reg(x) for x in reads], [reg(x) for x in writes]
+        wr = wr + [r for r in rd if r[0] in BANKS]
         need(e, rd, wr, acc)
         cnt[e] += 1
         fn().then_inc(T.sem[SEM[e]], 1)
@@ -142,9 +143,6 @@ def rank_program(g, core, T, topo):
     def fill(a, v):
         op("V", lambda: g.vector.memset(ap(a), v), [], [a])
 
-    def turn(out, a):
-        op("V", lambda: g.vector.transpose(ap(out), ap(a)), [a], [out])
-
     def scan(out, d0, d1, init, o0, o1):
         iv = ap(init) if isinstance(init, tuple) else init
         rd = [d0, d1] + ([init] if isinstance(init, tuple) else [])
@@ -160,8 +158,8 @@ def rank_program(g, core, T, topo):
         else:
             op("A", lambda: g.scalar.activation(ap(out), s, func, bias=bv, scale=sv, accum_out=ap(accum)), rd, [out, accum])
 
-    def mm(out, lhsT, rhs, start=True, stop=True):
-        op("P", lambda: g.tensor.matmul(ap(out), ap(lhsT), ap(rhs), start, stop), [lhsT, rhs], [out], acc=True)
+    def mm(out, lhsT, rhs, start=True, stop=True, k=128, m=128):
+        op("P", lambda: g.tensor.matmul(ap(out, m), ap(lhsT, k), ap(rhs, k), start, stop), [lhsT, rhs], [out], acc=True)
 
     def iota(out, pattern, base, cm):
         if out[0] in ("pI", "W"):
@@ -169,11 +167,30 @@ def rank_program(g, core, T, topo):
         else:
             op("G", lambda: g.iota(ap(out), pattern, base, cm, allow_small_or_imprecise_dtypes=True), [], [out])
 
+    def select(out, a, pattern, cmp, v, base, cm):
+        op("G", lambda: g.affine_select(ap(out), ap(a), pattern, cmp, v, base, cm), [a], [out])
+
+    def mark(out, pattern, base, v=1.0, on="zero"):
+        select(out, (on, 0, out[2]), pattern, ALU.not_equal, v, base, 1)
+
     def dma(e, pairs, sem, reads, writes):
         need(e, reads, writes)
         for o, i in pairs:
             Q[e].dma_start(o, i).then_inc(T.sem[sem], 16)
         note("D" + sem, reads, writes, sem, 16 * len(pairs))
+
+    def weave(main, filler):
+        for _ in main:
+            next(filler, None)
+
+    def run(steps, n=1000):
+        for _ in zip(range(n), steps):
+            pass
+
+    def both(a, b):
+        while next(a, 0) is None:
+            next(b, None)
+            yield
 
     engs = [e for e in topo.engines(core, nxt) if all(e in topo.engines(core, c) for c in T.cores if c != core)]
     mask = sum(1 << e for e in engs)
@@ -187,6 +204,16 @@ def rank_program(g, core, T, topo):
         sent[0] += len(engs)
         note("R", [], [(out, oa, ob)], sem, len(engs))
 
+    def ship_two(a, oa, b, ob, sem):
+        need("G", [a, b], [])
+        rid, pid, _ = topo.addr(nxt)
+        halves = [sum(1 << e for e in engs[k::2]) for k in range(2)]
+        g.remote_dma_fused([RemoteDMATransfer(dst_ids=[DstId(rid=rid, pnc=pid)], dma_engine_mask=m, remote_sem=T.sem[sem],
+                                              srcs=[ap(x)], dsts=[ap(o)]) for m, x, o in zip(halves, (a, b), (oa, ob))],
+                           local_sem=T.sem.sent)
+        sent[0] += len(engs)
+        note("R", [], [oa, ob], sem, len(engs))
+
     def share_aim(land, sem):
         need("G", [(land, 4 * rank, 4 * rank + 1)], [])
         others = [c for c in T.cores if c != core]
@@ -199,133 +226,118 @@ def rank_program(g, core, T, topo):
             if k != rank:
                 note("R", [], [(land, 4 * k, 4 * k + 1)], sem, len(engs) * (N - 1))
 
-    dma("A", [(T.damI[:, 384:512], T.dam[:, 384:512])], "l_dam1", [], [("damI", 384, 512)])
-    dma("S", [(T.mgI[:], T.mg[:])], "l_mg", [], [("mgI", 0, 32)])
     dma("S", [(T.aimI[:], T.aim0[:])], "l_aim", [], [("aimI", 0, 1)])
-    dma("A", [(T.trI[:, 0:768], T.trait[:, 0:768])], "l_t0", [], [("trI", 0, 768)])
-    dma("A", [(T.trI[:, 768:1536], T.trait[:, 768:1536])], "l_t1", [], [("trI", 768, 1536)])
-    dma("A", [(T.trI[:, 1536:2304], T.trait[:, 1536:2304])], "l_t2", [], [("trI", 1536, 2304)])
-    dma("A", [(T.trI[:, 2304:3072], T.trait[:, 2304:3072])], "l_t3", [], [("trI", 2304, 3072)])
-    dma("S", [(T.sireI[:, 0:192], T.sire[:, 0:192])], "l_sire", [("trI", 768, 1536)], [("sireI", 0, 192)])
-    dma("S", [(T.damI[:, 0:192], T.dam[:, 0:192])], "l_dam0", [], [("damI", 0, 192)])
+    dma("A", [(T.mgI[:], T.mg[:])], "l_mg", [], [("mgI", 0, 32)])
+    dma("S", [(T.damI[:, 384:512], T.dam[:, 384:512])], "l_dam1", [], [("damI", 384, 512)])
+    for k in range(4):
+        a, b = 768 * k, 768 * k + 768
+        dma("A", [(T.trI[:, a:b], T.trait[:, a:b])], "l_t%d" % k, [], [("trI", a, b)])
+    PM, OWN, KB, PS2, PD2, T1, HOWN, HT1, NT1, SGN = [("cc", k, k + 1) for k in range(10)]
     iota(("pI", 0, 1), [[0, 1]], 0, 1)
-    iota(("Gm", 0, 128), [[16, 8], [0, 16]], 0, 0)
-    iota(("Y", 0, 143), [[1, 143]], 0, -1)
     iota(("io", 0, 512), [[0, 32], [1, 16]], 0, 0)
-    iota(("W", 800, WW), [[0, WW - 800]], 0, 0)
-    iota(("zero", 0, 512), [[0, 512]], 0, 0)
+    iota(("W", WV, WW), [[0, WW - WV]], 0, 0)
     iota(("tabA", 0, Z0), [[0, Z0]], 0, 0)
     iota(("tabB", 0, Z0), [[0, Z0]], 0, 0)
-    fill(("W", 0, 800), 0)
+    iota(("zero", 0, 144), [[0, 144]], 0, 0)
+    ts(("pI", 1, 2), ("pI", 0, 1), 15, ALU.bitwise_and)
+    fill(("W", 0, WV), 0)
+    copy(PM, ("pI", 1, 2))
+    act(("seg", 0, 512), ("io", 0, 512), AF.Sign)
+    act(("w1", 0, 512), ("io", 0, 512), AF.Abs, PM, -1.0)
+    act(("dmj", 0, 512), ("w1", 0, 512), AF.Relu, 1.0, -1.0)
     own = [4 * rank + k for k in range(4)]
     d1, s2, d2 = [(4 * rank + 4 + k) % 16 for k in range(3)]
     wp = [(T.W[own[0]:128:16, 8:WW], T.sire[:, 0:192])]
     wp.append((T.W[d1:128:16, 8:WW], T.dam[:, 0:192]))
     wp.append((T.W[s2:128:16, 8:WW], T.sire[:, 192:384]))
     wp.append((T.W[d2:128:16, 8:WW], T.dam[:, 192:384]))
+    dma("S", [(T.sireI[:, 0:192], T.sire[:, 0:192])], "l_sire", [("trI", 0, 768)], [("sireI", 0, 192)])
     dma("S", wp, "l_w", [], [("W", 8, WW)])
+    dma("S", [(T.damI[:, 0:192], T.dam[:, 0:192])], "l_dam0", [], [("damI", 0, 192)])
     dma("S", [(T.sireI[:, 192:384], T.sire[:, 192:384])], "l_sire2", [], [("sireI", 192, 384)])
     dma("S", [(T.damI[:, 192:384], T.dam[:, 192:384])], "l_dam2", [], [("damI", 192, 384)])
-
-    PM, PG, OWN, KB, PS1, PD1, PS2, PD2, Y0, Y1, T1, HOWN, NS2, ND2, NY0, NY1 = [("cc", k, k + 1) for k in range(16)]
-    ts(("pI", 1, 2), ("pI", 0, 1), 15, ALU.bitwise_and)
-    ts(("pI", 3, 4), ("pI", 0, 1), 16, ALU.bitwise_and, 4, ALU.logical_shift_right)
-    copy(PM, ("pI", 1, 2))
-    ts(("pI", 2, 3), ("pI", 1, 2), 2, ALU.logical_shift_right)
-    copy(Y1, ("pI", 3, 4))
-    tt(PG, ("pI", 0, 1), PM, ALU.subtract)
-    ts(OWN, ("pI", 2, 3), float(rank), ALU.is_equal)
-    ts(HOWN, ("pI", 2, 3), float(rank), ALU.is_equal, 0.5, ALU.mult)
-    for col, r in ((PS1, own[0]), (PD1, d1), (PS2, s2), (PD2, d2)):
-        ts(col, PM, float(r), ALU.is_equal)
-    for col, r in ((NS2, s2), (ND2, d2)):
-        ts(col, PM, float(r), ALU.is_equal, -1.0, ALU.mult)
-    ts(KB, PM, -1.0 / 64, ALU.mult, 15.0 / 64, ALU.add)
-    ts(Y0, Y1, -1.0, ALU.mult, 1.0, ALU.add)
-    ts(NY1, Y1, -1.0, ALU.mult)
-    ts(NY0, Y1, -1.0, ALU.add)
-    act(("w3", 0, 128), ("Gm", 0, 128), AF.Abs, PG, -1.0)
-    act(("blk", 0, 128), ("w3", 0, 128), AF.Relu, 1.0, -1.0)
-    for b, col in (("bs1", PS1), ("bd1", PD1), ("bs2", PS2), ("bd2", PD2)):
-        act((b, 0, 128), ("blk", 0, 128), AF.Identity, 0.0, col)
-    for zb, k, m, nm in (("ZS", 15 - s2, PS2, NS2), ("ZD", 15 - d2, PD2, ND2)):
-        act(("w2", 0, 143), ("Y", 0, 143), AF.Abs, float(-k))
-        act((zb, 0, 143), ("w2", 0, 143), AF.Relu, m, nm)
-    act(("w1", 0, 512), ("io", 0, 512), AF.Abs, PM, -1.0)
-    act(("dmj", 0, 512), ("w1", 0, 512), AF.Relu, 1.0, -1.0)
-    act(("seg", 0, 512), ("io", 0, 512), AF.Sign)
-    act(("w3", 0, 128), ("Y", 0, 128), AF.Abs)
-    act(("ident", 0, 128), ("w3", 0, 128), AF.Relu, 1.0, -1.0)
-    act(("idm", 0, 128), ("ident", 0, 128), AF.Identity, 0.0, -6400.0)
-    act(("id8", 0, 128), ("ident", 0, 128), AF.Identity, 0.0, -float(Z0))
     copy(("mg16", 0, 32), ("mgI", 0, 32))
-    ts(("damI", 512, 520), ("mgI", 16, 24), 6400.0, ALU.add)
-    ts(("damI", 520, 528), ("mgI", 8, 16), 6400.0, ALU.add)
-    A144 = (0, 144)
-    ts(("EI",) + A144, ("damI", 384, 528), -6400.0, ALU.add, 0.0, ALU.max)
-    ts(("AI",) + A144, ("EI",) + A144, 15, ALU.bitwise_and)
-    ts(("EF",) + A144, ("AI",) + A144, 3071.0, ALU.mult, 128.0, ALU.add)
-    tt(("EG",) + A144, ("EF",) + A144, ("EI",) + A144, ALU.add)
-    ts(("pp",) + A144, ("damI", 384, 528), 6400.0, ALU.is_ge)
-    ts(("qq",) + A144, ("damI", 384, 528), 9472.0, ALU.is_ge)
-    tt(("is2",) + A144, ("pp",) + A144, ("qq",) + A144, ALU.subtract)
-    tt(("EM",) + A144, ("EG",) + A144, ("is2",) + A144, ALU.mult)
-    ts(("pos16",) + A144, ("EM",) + A144, 0.0625, ALU.mult)
     copy(T1, ("aimI", 0, 1))
+    ts(HT1, ("aimI", 0, 1), 0.5, ALU.mult)
+    ts(NT1, ("aimI", 0, 1), -1.0, ALU.mult)
+
+    def places():
+        v = lambda n: (n, 0, 144)
+        c = ("damI", 384, 528)
+        ts(("damI", 512, 520), ("mgI", 16, 24), 6400.0, ALU.add)
+        ts(("damI", 520, 528), ("mgI", 8, 16), 6400.0, ALU.add)
+        ts(("pI", 2, 3), ("pI", 1, 2), 2, ALU.logical_shift_right)
+        ts(PS2, PM, float(s2), ALU.is_equal)
+        ts(PD2, PM, float(d2), ALU.is_equal)
+        ts(v("EI"), c, -6400.0, ALU.add, 0.0, ALU.max)
+        ts(v("pp"), c, 6400.0, ALU.is_ge)
+        ts(v("AI"), v("EI"), 15, ALU.bitwise_and)
+        ts(v("qq"), c, 9472.0, ALU.is_ge)
+        ts(v("EF"), v("AI"), 3071.0, ALU.mult, 128.0, ALU.add)
+        tt(v("is2"), v("pp"), v("qq"), ALU.subtract)
+        tt(v("EG"), v("EF"), v("EI"), ALU.add)
+        ts(("mn", 0, 128), ("damI", 384, 512), 6400.0, ALU.min)
+        tt(v("EM"), v("EG"), v("is2"), ALU.mult)
+        ts(("x1", 0, 128), ("damI", 384, 512), -9472.0, ALU.add, 0.0, ALU.max)
+        ts(v("pos16"), v("EM"), 0.0625, ALU.mult)
+        ts(OWN, ("pI", 2, 3), float(rank), ALU.is_equal)
+        ts(HOWN, ("pI", 2, 3), float(rank), ALU.is_equal, 0.5, ALU.mult)
+        ts(KB, PM, -1.0 / 64, ALU.mult, 15.0 / 64, ALU.add)
+        ts(SGN, PD2, -1.0, ALU.mult, PS2, ALU.add)
 
     def y_chunk(k):
         a, b = 768 * k, 768 * k + 768
         ts(("y1", a, b), ("trI", a, b), T1, ALU.subtract)
+        act(("FH", a, b), ("y1", a, b), AF.Abs, 0.0, 0.5)
 
-    def f(n):
-        return (n, 0, 128)
+    def double(tab, a, b):
+        ts((tab, Z0 + a, Z0 + b), ("FH", a, b), 2.0, ALU.mult)
 
+    def ghosts0():
+        act(("gt", 0, 128), (("trI", 0, 3072), ("mg16", 0, 8)), AF.Abs, HT1, -0.5)
+        act(("gs", 0, 128), (("trI", 0, 3072), ("mg16", 0, 8)), AF.Identity, NT1)
+        ship_two(("gs", 0, 128), ("y1", 3072, 3200), ("gt", 0, 128), ("FH", 3072, 3200), "a_g0")
+
+    tab = "tabA"
     y_chunk(0)
     y_chunk(1)
+    ghosts0()
     y_chunk(2)
-    ts(("gs", 0, 128), (("trI", 0, 3072), ("mg16", 0, 8)), T1, ALU.subtract)
-    ship("gs", 0, 128, "y1", 3072, 3200, "a_g0")
     y_chunk(3)
     copy(("sire16", 0, 192), ("sireI", 0, 192))
-    copy(("dam16", 0, 192), ("damI", 0, 192))
+    places()
     dma("S", [(T.trI[r:128:16, 0:3072], T.sire[:, 192:384]) for r in own], "l_tr", [], [("trI", 0, 3072)])
-    for k in range(4):
-        act(("FH", 768 * k, 768 * k + 768), ("y1", 768 * k, 768 * k + 768), AF.Abs, 0.0, 0.5)
+    for b, r in (("bs1", own[0]), ("bd1", d1), ("bs2", s2), ("bd2", d2)):
+        mark((b, 0, 128), [[-16, 8], [0, 16]], -r)
+    ROW = [[-16, 9], [1000, 16]]
+    mark(("ZS", 0, 144), ROW, -s2 - 15000)
+    mark(("ident", 0, 128), [[-1, 128]], 0)
+    mark(("idm", 0, 128), [[-1, 128]], 0, -6400.0)
+    mark(("id8", 0, 128), [[-1, 128]], 0, -float(Z0))
+    mark(("ZD", 0, 144), ROW, -d2 - 15000)
 
-    c = ("damI", 384, 512)
-    ts(f("mn"), c, 6400.0, ALU.min)
-    ts(f("x1"), c, -9472.0, ALU.add, 0.0, ALU.max)
-    ts(("tabA", Z0, Z0 + VD), ("FH", 0, VD), 2.0, ALU.mult)
-    copy(("CF", 2048, 2304), (("W", 0, WW), ("pos16", 128, 144)))
-    mm(("pC", 0, 128), ("bs1", 0, 128), ("CF", 2176, 2304))
-    mm(("pC", 128, 256), ("bd1", 0, 128), ("CF", 2176, 2304))
-    mm(("pC", 256, 384), ("bs2", 0, 128), ("CF", 2048, 2176))
-    mm(("pC", 384, 512), ("bd2", 0, 128), ("CF", 2048, 2176))
-    copy(("CF", 0, 1024), (("W", 0, WW), ("pos16", 0, 64)))
-    tt(("mk", 0, 512), ("pC", 0, 512), ("dmj", 0, 512), ALU.mult)
-    scan(("msc", 0, 512), ("seg", 0, 512), ("mk", 0, 512), 0.0, ALU.mult, ALU.add)
-    copy(("ms16", 0, 32), ("msc", 15, 512, 16))
-    MS1, MD1, MS2, MD2 = [("ms16", 8 * k, 8 * k + 8) for k in range(4)]
-
-    def to_list(pb, z, flat, f0, o0, more=()):
+    def to_list(pb, o0, z, flat, f0, x0=0, more=()):
         for i in range(16):
             mm((pb, o0, o0 + 64), (z, 15 - i, 143 - i), (flat, f0 + i, f0 + 1024, 16), i == 0, i == 15 and not more)
         for k, (w, x) in enumerate(more):
-            mm((pb, o0, o0 + 64), (w, 0, 128), (x, o0, o0 + 64), False, k == len(more) - 1)
+            mm((pb, o0, o0 + 64), (w, 0, 128), (x, x0, x0 + 64), False, k == len(more) - 1)
+
+    def flat(h):
+        act(("CF", 1024 * h, 1024 * h + 1024), (("W", 0, WW), ("pos16", 64 * h, 64 * h + 64)), AF.Identity)
+
+    SB, DB = (("pS", 0), ("pD", 0)), (("pS", 64), ("pE", 128))
 
     def list_s(h):
-        to_list("pS", "ZS", "CF", 1024 * h, 64 * h, (("ident", "mn"), ("idm", "pp"), ("id8", "qq")))
+        to_list(*SB[h], "ZS", "CF", 1024 * h, 64 * h, (("ident", "mn"), ("idm", "pp"), ("id8", "qq")))
 
     def list_d(h):
-        to_list("pD", "ZD", "CF", 1024 * h, 64 * h, (("ident", "mn"), ("ident", "x1"), ("idm", "is2")))
+        to_list(*DB[h], "ZD", "CF", 1024 * h, 64 * h, (("ident", "mn"), ("ident", "x1"), ("idm", "is2")))
 
-    def u_lists(h):
-        v = lambda n: (n, 64 * h, 64 * h + 64)
-        ts(v("US16"), v("pS"), float(Z0), ALU.add)
-        copy(v("UD16"), v("pD"))
+    def u_s(h):
+        ts(("US16", 64 * h, 64 * h + 64), (SB[h][0], SB[h][1], SB[h][1] + 64), float(Z0), ALU.add)
 
-    list_s(0)
-    list_d(0)
+    def u_d(h):
+        copy(("UD16", 64 * h, 64 * h + 64), (DB[h][0], DB[h][1], DB[h][1] + 64))
 
     PART = [0]
     for n in (512, 768, 896, 896):
@@ -339,280 +351,335 @@ def rank_program(g, core, T, topo):
         a, b = PART[k], PART[k + 1]
         tt((tab, Z0 + 3200 + a, Z0 + 3200 + b), (("FH", 0, 3200), ("dam16", a // 16, b // 16)), ("tmp", a, b), ALU.add)
 
-    def ghosts1_act(r):
-        act(("gt", 128 * r - 128, 128 * r), (("FH", 0, 3072), MS1), AF.Identity)
+    MS1, MD1, MS2, MD2 = [("ms16", 8 * k, 8 * k + 8) for k in range(4)]
 
     def ghosts1(r, tab):
         o = 128 * r
-        tt(("gs", o, o + 128), (("FH", 0, 3200), MD1), ("gt", o - 128, o), ALU.add)
+        copy(("gt", 128, 256), (("FH", 0, 3072), MS1))
+        tt(("gs", o, o + 128), (("FH", 0, 3200), MD1), ("gt", 128, 256), ALU.add)
         ship("gs", o, o + 128, tab, G1, G1 + 128, "a_g1%d" % r)
 
-    def ghosts2_act(r, tab):
-        act(("gt", 384 + 128 * (r - 1), 384 + 128 * r), ((tab, Z0, OWN1), MS2), AF.Identity)
-
-    def ghosts2(r, tab):
+    def ghosts2(r, tab, between=lambda: None):
         o = 384 + 128 * r
-        tt(("gs", o, o + 128), ((tab, Z0, E1), MD2), ("gt", 384 + 128 * (r - 1), 384 + 128 * r), ALU.add)
+        copy(("gt", 256, 384), ((tab, Z0, OWN1), MS2))
+        between()
+        tt(("gs", o, o + 128), ((tab, Z0, E1), MD2), ("gt", 256, 384), ALU.add)
         ship("gs", o, o + 128, tab, G2X, G2X + 128, "a_g2%d" % r)
 
-    def double3(tab):
-        act((tab, X3, X3 + 1024), ("G3", 0, 1024), AF.Identity, 0.0, 0.5)
+    def double3(tab, a=0, b=1024):
+        act((tab, X3 + a, X3 + b), ("G3", a, b), AF.Identity, 0.0, 0.5)
 
     def ghosts3(r, tab):
         o = 896 + 128 * (r - 2)
         ts(("gs", o, o + 128), (("G3", 0, 1024), ("mg16", 24, 32)), 0.5, ALU.mult)
         ship("gs", o, o + 128, tab, G3X, G3X + 128, "a_g3%d" % r)
 
-    tab = "tabA"
     sires1(0)
+    double(tab, 0, VD[0])
+    act(("CF", 2048, 2304), (("W", 0, WW), ("pos16", 128, 144)), AF.Identity)
+    mm(("pC", 0, 128), ("bs1", 0, 128), ("CF", 2176, 2304))
+    mm(("pC", 128, 256), ("bd1", 0, 128), ("CF", 2176, 2304))
+    mm(("pC", 256, 384), ("bs2", 0, 128), ("CF", 2048, 2176))
+    mm(("pC", 384, 512), ("bd2", 0, 128), ("CF", 2048, 2176))
     sires1(1)
+    flat(0)
+    list_s(0)
+    list_d(0)
     sires1(2)
-    act(("FH", 3072, 3200), ("y1", 3072, 3200), AF.Abs, 0.0, 0.5)
-    dams1(tab, 0)
-    act(("dmo", 0, 16), ("dmj", 0, 16), AF.Identity, 0.0, OWN)
-    act(("dmh", 0, 16), ("dmj", 0, 16), AF.Identity, 0.0, HOWN)
-    act(("i16", 0, 16), ("io", 0, 16), AF.Identity, 0.0, 0.0625)
-    act(("nm", 0, 256), ("dmj", 0, 256), AF.Identity, 1.0e9, -1.0e9)
-    ghosts1_act(1)
-    ghosts1(1, tab)
-    dams1(tab, 1)
     sires1(3)
-    act((tab, Z0 + VD, Z0 + 3200), ("y1", VD, 3200), AF.Abs)
+    copy(("dam16", 0, 192), ("damI", 0, 192))
+    dams1(tab, 0)
+    tt(("mk", 0, 512), ("pC", 0, 512), ("dmj", 0, 512), ALU.mult)
+    copy(("sire16", 192, 384), ("sireI", 192, 384))
+    scan(("msc", 0, 512), ("seg", 0, 512), ("mk", 0, 512), 0.0, ALU.mult, ALU.add)
+    copy(("dam16", 192, 384), ("damI", 192, 384))
+    copy(("ms16", 0, 32), ("msc", 15, 512, 16))
+    ghosts1(1, tab)
+    iota(("cix", 0, 256), [[1, 16], [64, 16]], 0, 0)
+    iota(("one", 0, 128), [[0, 128]], 1, 0)
+    select(("w3", 0, 128), ("one", 0, 128), [[-16, 8], [0, 16]], ALU.is_ge, 0.0, 0, 1)
+    select(("blk", 0, 128), ("w3", 0, 128), [[16, 8], [0, 16]], ALU.is_ge, 0.0, 15, -1)
+    dams1(tab, 1)
+    act((tab, Z0 + VD[0], Z0 + 3200), ("y1", VD[0], 3200), AF.Abs)
+    dma("S", [(T.W[q:128:16, 8:WW], T.sire[:, 0:192]) for q in own[1:]], "l_w2", [], [("W", 8, WW)])
     dams1(tab, 2)
     dams1(tab, 3)
-    REST = [(CUT + 512 * k, CUT + 512 * k + 512, pb) for k, pb in enumerate(("pA", "pB"))]
-    HALF = [(0, CUT // 2), (CUT // 2, CUT)]
-    copy(("sire16", 192, 384), ("sireI", 192, 384))
-    copy(("dam16", 192, 384), ("damI", 192, 384))
-    for a, b in HALF:
-        act(("tmp", a, b), ((tab, Z0, OWN1), ("sire16", 192 + a // 16, 192 + b // 16)), AF.Identity)
-    ghosts2_act(1, tab)
-    for a, b, pb in REST:
-        act(("tmp", a, b), ((tab, Z0, OWN1), ("sire16", 192 + a // 16, 192 + b // 16)), AF.Identity)
-        mm((pb, 0, 512), ("ident", 0, 128), ("tmp", a, b), True, False)
-    for a, b, pb in REST:
-        act(("tmp2", a - CUT, b - CUT), ((tab, Z0, E1), ("dam16", 192 + a // 16, 192 + b // 16)), AF.Identity)
-        mm((pb, 0, 512), ("ident", 0, 128), ("tmp2", a - CUT, b - CUT), False, True)
-    copy(("CF", 1024, 2048), (("W", 0, WW), ("pos16", 64, 128)))
-    dma("S", [(T.W[q:128:16, 8:WW], T.sire[:, 0:192]) for q in own[1:]], "l_w2", [], [("W", 8, WW)])
-    for a, b in HALF:
-        tt(("D2", a, b), ((tab, Z0, E1), ("dam16", 192 + a // 16, 192 + b // 16)), ("tmp", a, b), ALU.add)
     ghosts2(1, tab)
-    u_lists(0)
-    act(("T3", 0, 1024), ((tab, 0, E1), ("US16", 0, 64)), AF.Identity, KB)
-    act(("T4", 0, KP), ((tab, Z0, X3), ("UD16", 0, KP // 16)), AF.Identity)
-    mm(("pC", 0, KP), ("ident", 0, 128), ("T3", 0, KP), True, False)
-    mm(("pC", 0, KP), ("ident", 0, 128), ("T4", 0, KP), False, True)
-    JL, JB = [("cl", k, k + 1) for k in (0, 1)], [("cl", k, k + 1) for k in (2, 3)]
-    scan(("tmp", 0, CUT), ("D2", 0, CUT), ("D2", 0, CUT), 0.0, ALU.max, ALU.max)
-    scan(("FH", 0, CUT), ("D2", 0, CUT), ("D2", 0, CUT), 1.0e9, ALU.min, ALU.min)
-    K, K2, LAST = ("cl", 8, 9), ("cl", 9, 10), ("tmp", 3071, 3072)
-    for out, alu in (("tmp", ALU.max), ("FH", ALU.min)):
-        for n, (a, b, pb) in enumerate(REST):
-            scan((out, a, b), (pb, 0, 512), ("zero", 0, 512), (out, a - 1, a), alu, ALU.add)
-            if out == "FH" and n == 0:
-                act(("junk", 0, 192), ("tmp", 15, 3072, 16), AF.Sign, LAST, -1.0, K)
-                ts(("off16", 0, 16), ("i16", 0, 16), K, ALU.add, 16.0, ALU.mult)
-                tt(("mk", 0, 256), (("tmp", 0, 3072), ("off16", 0, 16)), ("nm", 0, 256), ALU.max)
-                act(("junk", 0, 256), ("mk", 0, 256), AF.Sign, LAST, -1.0, K2)
-    act(("seg", 512, 1024), ("io", 0, 512), AF.Sign)
-    for k in (-1, 0, 1):
-        act(("w3", 0, 128), ("Y", 0, 128), AF.Abs, float(-16 * k))
-        for y, m, nm in ((0, Y0, NY0), (1, Y1, NY1)):
-            if 0 <= y + k < 2:
-                act(("R%d%d" % (y, y + k), 0, 128), ("w3", 0, 128), AF.Relu, m, nm)
-    ts(JL[0], K, 16.0, ALU.mult, K2, ALU.add)
-    act(("junk", 0, 3072), ("FH", 0, 3072), AF.Sign, ("FH", 3071, 3072), -1.0, JB[0])
+    iota(("zerob", 0, 144), [[0, 144]], 0, 0)
+    mark(("idb", 0, 128), [[-1, 128]], 0, on="zerob")
+    for h in range(2):
+        mark(("perm%d" % h, 0, 128), [[-1, 8], [1000, 2], [-8, 8]], -1000 * h, on="zerob")
+    mark(("ZSb", 0, 144), ROW, -s2 - 15000, on="zerob")
+    mark(("ZB", 0, 144), ROW, -d2 - 15000, on="ZSb")
+    for a in range(0, 3072, 512):
+        b = a + 512
+        act(("tmp", a, b), ((tab, Z0, OWN1), ("sire16", 192 + a // 16, 192 + b // 16)), AF.Identity)
+        if a == 2560:
+            u_s(0)
+            u_d(0)
+        tt(("tabB", D2 + a, D2 + b), ((tab, Z0, E1), ("dam16", 192 + a // 16, 192 + b // 16)), ("tmp", a, b), ALU.add)
+
+    def keys_s(tab, h):
+        act(("T4", 0, 1024), ((tab, 0, E1), ("US16", 64 * h, 64 * h + 64)), AF.Identity, KB)
+
+    def turn_keys(parts, i0=0, i1=8):
+        for i in range(i0, i1):
+            o = ("pA" if i < 4 else "pB", 128 * (i % 4), 128 * (i % 4) + 128)
+            for k, b in enumerate(parts):
+                mm(o, (b, i, 1024, 8), ("ident", 0, 128), k == 0, k == len(parts) - 1)
+
+    def rows(c0):
+        for k, pb in enumerate(("pA", "pB")):
+            scan(("sg", 512 * k, 512 * k + 512), ("seg", 0, 512), (pb, 0, 512), 0.0, ALU.mult, ALU.max)
+            yield
+        ts(("ri", 0, 64), ("sg", 15, 1024, 16), 64.0, ALU.mult)
+        yield
+        ts(("rb", 0, 64), ("ri", 0, 64), 15, ALU.bitwise_and)
+        yield
+        copy(("rbf", 0, 64), ("rb", 0, 64))
+        mm(("pC", 0, 128), ("rbf", 0, 64), ("idb", 0, 128), m=64)
+        yield
+        op("V", lambda: g.vector.tensor_copy(ap(("rT", 0, 128), 64), ap(("pC", 0, 128), 64)), [("pC", 0, 128)], [("rT", 0, 128)])
+        for h in range(2):
+            mm(("pC", 128, 192), ("perm%d" % h, 0, 128), ("rT", h, 128, 2), h == 0, h == 1, k=64)
+        yield
+        ts(("row16", c0, c0 + 64), ("pC", 128, 192), -1.0, ALU.mult, 15.0, ALU.add)
+        yield
+
+    def running(o, buf, a, n, alu, piece):
+        for k in range(0, n, piece):
+            init = ("tmp", o + k - 1, o + k) if k else (0.0 if alu == ALU.max else 1.0e9)
+            scan(("tmp", o + k, o + k + piece), (buf, a + 2 * k, a + 2 * k + 2 * piece, 2),
+                 (buf, a + 2 * k + 1, a + 2 * k + 2 * piece, 2), init, alu, alu)
+            yield
+
+    def count(o, n, step, out):
+        act(("junk", 0, n // step), ("tmp", o + step - 1, o + n, step), AF.Sign, ("tmp", o + n - 1, o + n), -1.0, out)
+
+    KX, KN, RX, RN, CX, CN = [("cl", k, k + 1) for k in range(8, 14)]
+    JB = [("cl", k, k + 1) for k in (2, 3)]
+    BH = [("cl", 4, 5), ("cl", 5, 6)]
+    WIN2 = ("tabB", D2, D2 + 3072)
 
     def founder_a(s, n):
         b = lambda k: ("cl", n + k, n + k + 1)
         ib = lambda k: ("ci", n + k, n + k + 1)
         ts(ib(0), s, -3200.0, ALU.add, 0.0, ALU.max)
         ts(b(0), s, 3200.0, ALU.is_lt, s, ALU.mult)
+        ts(b(2), s, 3200.0, ALU.is_ge)
         ts(ib(1), ib(0), 15, ALU.bitwise_and)
         ts(b(1), ib(0), 0.0625, ALU.mult)
-        ts(b(2), s, 3200.0, ALU.is_ge)
+        yield
         ts(("sm16", n, n + 1), ib(1), 191.9375, ALU.mult, b(1), ALU.add)
-        return ("sm16", n, n + 1)
+        yield
 
     def founder_b(n):
         ts(("sm16", n + 2, n + 3), ("cl", n + 3, n + 4), ("cl", n + 2, n + 3), ALU.mult, ("cl", n, n + 1), ALU.add)
         return ("sm16", n + 2, n + 3)
 
     def chain1(land):
-        J = JL[0]
-        ts(("ci", 16, 17), J, 240.0, ALU.add)
-        ts(("cl", 16, 17), J, 0.0625, ALU.mult, 15.0, ALU.add)
-        ts(("ci", 17, 18), ("ci", 16, 17), 15, ALU.bitwise_and)
-        ts(("sm16", 16, 17), ("ci", 17, 18), 191.9375, ALU.mult, ("cl", 16, 17), ALU.add)
+        count(0, 1536, 8, KX)
+        yield
+        yield
+        ts(("off16", 0, 16), ("i16", 0, 16), KX, ALU.add, 16.0, ALU.mult)
+        yield
+        tt(("mk", 0, 256), (WIN2, ("off16", 0, 16)), ("nmx", 0, 256), ALU.add)
+        yield
+        red(RX, ("mk", 0, 256), ALU.max)
+        yield
+        ts(CX, RX, ("tmp", 1535, 1536), ALU.subtract, -64.0 * 192, ALU.mult)
+        yield
+        ts(("sm16", 16, 17), CX, KX, ALU.add, 15.0 * 192, ALU.add)
+        yield
         tt(("lk", 0, 16), (("trI", 0, 3072), ("sm16", 16, 17)), ("dmo", 0, 16), ALU.mult)
+        yield
         red(("cl", 17, 18), ("lk", 0, 16))
-        tt(("lk", 16, 32), (("W", 8, WW), founder_a(("cl", 17, 18), 20)), ("dmo", 0, 16), ALU.mult)
+        yield
+        yield from founder_a(("cl", 17, 18), 20)
+        tt(("lk", 16, 32), (("W", 8, WW), ("sm16", 20, 21)), ("dmo", 0, 16), ALU.mult)
+        yield
         red(("cl", 23, 24), ("lk", 16, 32))
-        tt(("lk", 32, 48), (("y1", 0, 3072), founder_b(20)), ("dmh", 0, 16), ALU.mult)
+        yield
+        f = founder_b(20)
+        yield
+        tt(("lk", 32, 48), (("y1", 0, 3072), f), ("dmh", 0, 16), ALU.mult)
+        yield
         red((land, 4 * rank, 4 * rank + 1), ("lk", 32, 48))
-
-    def best_lines_a():
-        copy(("bg2", 0, 16), (("W", 8, WW), founder_a(("bsc", 15, 16), 32)))
-        mm(("pM", 288, 304), ("bs1", 0, 128), ("bg2", 0, 16))
-
-    def best_lines_b():
-        tt(("bm2", 0, 16), ("pM", 288, 304), ("dmj", 0, 16), ALU.mult)
-        red(("cl", 35, 36), ("bm2", 0, 16))
-        copy(("yt16", 0, 16), (("y1", 0, 3072), founder_b(32)))
-
-    def chain2(land):
-        copy(("sm16", 40, 41), JL[1])
-        tt(("lk", 48, 64), (("sy", 0, 1024), ("sm16", 40, 41)), ("dmh", 0, 16), ALU.mult)
-        red((land, 4 * rank, 4 * rank + 1), ("lk", 48, 64))
-
-    chain1("land1")
-    share_aim("land1", "a_aim1")
-    tt(("key", KP, 1024), ((tab, Z0, X3), ("UD16", KP // 16, 64)), ("T3", KP, 1024), ALU.add)
-
-    def rows_a(k, between):
-        turn(("D2", 1024 + k, 2048), ("key", k, 1024))
-        if k:
-            turn(("D2", 1024, 1024 + k), ("pC", 0, k))
-        between()
-        scan(("D2", 0, 1024), ("seg", 0, 1024), ("D2", 1024, 2048), 0.0, ALU.mult, ALU.max)
-
-    def rows_b():
-        ts(("ri", 0, 64), ("D2", 15, 1024, 16), 64.0, ALU.mult)
-        ts(("rb", 0, 64), ("ri", 0, 64), 15, ALU.bitwise_and)
-        copy(("rbf", 0, 64), ("rb", 0, 64))
-        for y in range(2):
-            for h in range(2):
-                mm(("pM", 32 * y, 32 * y + 32), ("R%d%d" % (y, h), 0, 128), ("rbf", h, 64, 2), h == 0, h == 1)
-
-    def rows_c(c0):
-        for y in range(2):
-            ts(("row16", c0 + y, c0 + 64, 2), ("pM", 32 * y, 32 * y + 32), -1.0, ALU.mult, 15.0, ALU.add)
 
     def best_a(r):
         k = 16 * (r - 1)
-        ts(("bR", k, k + 16), ("dmj", 0, 16), JB[r - 1], ALU.mult, -1.0, ALU.mult)
+        ts(("bR", k, k + 16), ("dmj", 0, 16), JB[r - 1], ALU.mult)
         mm(("pY", 128 + k, 144 + k), ("blk", 0, 128), ("bR", k, k + 16))
 
-    def best_b(r):
-        k = 16 * (r - 1)
-        copy(("bT", k, k + 16), ("pY", 128 + k, 144 + k))
+    BS, BD = ("sm16", 52, 53), ("sm16", 54, 55)
 
-    def sire_act(r, a=0, b=1024):
-        k = 64 * (r - 1)
-        act(("sf", 16 * k + a, 16 * k + b), (("bT", 16 * (r - 1), 16 * r), ("row16", k + a // 16, k + b // 16)), AF.Identity)
+    def best1():
+        ts(("off16", 16, 32), ("i16", 0, 16), KN, ALU.subtract, 16.0, ALU.mult)
+        tt(("mk", 256, 512), (WIN2, ("off16", 16, 32)), ("nmn", 0, 256), ALU.add)
+        red(RN, ("mk", 256, 512), ALU.min)
+        ts(CN, RN, ("tmp", 3071, 3072), ALU.subtract, 64.0, ALU.mult)
+        ts(("sm16", 48, 49), CN, 192.0, ALU.mult, KN, ALU.subtract)
+        ts(JB[0], KN, -16.0, ALU.mult, CN, ALU.add)
+        copy(("bg", 0, 16), (("W", 8, WW), ("sm16", 48, 49)))
+        mm(("pM", 256, 272), ("bs2", 0, 128), ("bg", 0, 16))
+        mm(("pM", 272, 288), ("bd2", 0, 128), ("bg", 0, 16))
+        best_a(1)
+        turn_keys(("T4", "T3"), 4, 8)
+        tt(("bm", 0, 32), ("pM", 256, 288), ("dmj", 0, 32), ALU.mult)
+        ts(("bT", 0, 16), ("pY", 128, 144), PS2, ALU.mult)
+        scan(("bsc", 0, 32), ("seg", 0, 32), ("bm", 0, 32), 0.0, ALU.mult, ALU.add)
+        copy(("sm16", 52, 56, 2), ("bsc", 15, 32, 16))
 
-    def sire_cols(r):
-        to_list("pE", "ZS", "sf", 1024 * (r - 1), 64 * (r - 1))
-
-    BH = [("cl", 4, 5), ("cl", 5, 6)]
-
-    def outputs(r, first):
-        ts(("yso", 64 * (r - 1), 64 * r), ("pE", 64 * (r - 1), 64 * r), float(first), ALU.add)
-        ts(("yto", r - 1, r), BH[r - 1], 2.0, ALU.mult, T1, ALU.add)
+    def best_lines():
+        yield from founder_a(("bsc", 15, 16), 32)
+        copy(("bg2", 0, 16), (("W", 8, WW), ("sm16", 32, 33)))
+        mm(("pM", 288, 304), ("bs1", 0, 128), ("bg2", 0, 16))
+        yield
+        tt(("bm2", 0, 16), ("pM", 288, 304), ("dmj", 0, 16), ALU.mult)
+        yield
+        red(("cl", 35, 36), ("bm2", 0, 16))
+        yield
+        f = founder_b(32)
+        yield
+        ts(("yt16", 16, 32), (("y1", 0, 3072), f), OWN, ALU.mult)
+        yield
+        tt(("yt16", 0, 16), ("yt16", 16, 32), ("bT", 0, 16), ALU.add)
+        yield
 
     def aims(r, land):
-        op("V", lambda: g.vector.tensor_reduce(ap(BH[r - 1]), T[land][:, 0:16:4], AxisListType.X, ALU.add),
-           [(land, 0, 16)], [BH[r - 1]])
+        act(("lk", 96, 100), (land, 0, 16, 4), AF.Identity, accum=BH[r - 1])
 
-    rows_a(KP, lambda: aims(1, "land1"))
-    rows_b()
-    n = 48
-    best_a(1)
-    copy(("ci", n, n + 1), JB[0])
-    ts(("cl", n + 1, n + 2), JB[0], -0.0625, ALU.mult)
-    ts(("ci", n + 2, n + 3), ("ci", n, n + 1), -1.0, ALU.mult)
-    rows_c(0)
-    ts(("ci", n + 1, n + 2), ("ci", n + 2, n + 3), 15, ALU.bitwise_and)
-    ts(("sm16", n, n + 1), ("ci", n + 1, n + 2), 191.9375, ALU.mult, ("cl", n + 1, n + 2), ALU.add)
-    copy(("bg", 0, 16), (("W", 8, WW), ("sm16", n, n + 1)))
-    mm(("pM", 256, 272), ("bs2", 0, 128), ("bg", 0, 16))
-    mm(("pM", 272, 288), ("bd2", 0, 128), ("bg", 0, 16))
-    list_s(1)
-    best_b(1)
-    tt(("bm", 0, 32), ("pM", 256, 288), ("dmj", 0, 32), ALU.mult)
-    scan(("bsc", 0, 32), ("seg", 0, 32), ("bm", 0, 32), 0.0, ALU.mult, ALU.add)
-    copy(("sm16", n + 4, n + 8, 2), ("bsc", 15, 32, 16))
-    BS, BD = ("sm16", n + 4, n + 5), ("sm16", n + 6, n + 7)
+    def founders(r):
+        for k in range(4):
+            act(("FH", 800 * k, 800 * k + 800), ("y1", 800 * k, 800 * k + 800), AF.Abs, BH[r - 2], -0.5)
 
-    def begin(r, tab):
-        bias = BH[r - 2]
+    def aim_out(r):
+        ts(("yto", r - 1, r), BH[r - 1], 2.0, ALU.mult, T1, ALU.add)
+
+    act(("dmo", 0, 16), ("dmj", 0, 16), AF.Identity, 0.0, OWN)
+    act(("dmh", 0, 16), ("dmj", 0, 16), AF.Identity, 0.0, HOWN)
+    act(("i16", 0, 16), ("io", 0, 16), AF.Identity, 0.0, 0.0625)
+    act(("nmn", 0, 256), ("cix", 0, 256), AF.Abs, PM, -1.0 / 64)
+    act(("nmx", 0, 256), ("nmn", 0, 256), AF.Identity, 15.0 / 64, -1.0)
+    keys_s(tab, 0)
+    run(running(0, "tabB", D2, 1536, ALU.max, 1536))
+    least = running(1536, "tabB", D2, 1536, ALU.min, 128)
+    weave(chain1("land1"), least)
+    share_aim("land1", "a_aim1")
+    run(least)
+    act(("T3", 0, 1024), ((tab, Z0, X3), ("UD16", 0, 64)), AF.Identity)
+    turn_keys(("T4", "T3"), 0, 4)
+    flat(1)
+    count(1536, 1536, 8, KN)
+    aims(1, "land1")
+    founders(2)
+    best1()
+    first_rows = rows(0)
+    lines = best_lines()
+    run(lines, 3)
+    run(first_rows, 1)
+
+    def generation1(r, tab, filler=iter(()), steps=(0, 0, 0, 0)):
+        nv = VD[r - 1]
+        for a in range(0, nv, 800):
+            double(tab, a, a + 800)
+        ghosts1(r, tab)
         for k in range(4):
-            act(("FH", 800 * k, 800 * k + 800), ("y1", 800 * k, 800 * k + 800), AF.Abs, bias, -0.5)
-        nv = 2 if r == 2 else 3
-        for k in range(nv):
-            ts((tab, Z0 + 800 * k, Z0 + 800 * k + 800), ("FH", 800 * k, 800 * k + 800), 2.0, ALU.mult)
-        for k in range(4):
+            run(filler, steps[k])
             sires1(k)
             dams1(tab, k)
-            if k == 0:
-                ghosts1_act(r)
-                ghosts1(r, tab)
-                if r == 2:
-                    best_lines_a()
-                    list_d(1)
-        act((tab, Z0 + 800 * nv, Z0 + 3200), ("FH", 800 * nv, 3200), AF.Identity, 0.0, 2.0)
-        if r == 3:
-            sire_act(2, 0, 512)
-        ghosts2_act(r, tab)
-        copy(("ub1", 0, 16), ((tab, Z0, OWN1), BS))
+            if r == 2 and k == 2:
+                list_s(1)
+                list_d(1)
+        act((tab, Z0 + nv, Z0 + 3200), ("FH", nv, 3200), AF.Identity, 0.0, 2.0)
+        ghosts2(r, tab, lambda: copy(("ub1", 0, 16), ((tab, Z0, OWN1), BS)))
         tt(("Ub", 0, 16), ((tab, Z0, E1), BD), ("ub1", 0, 16), ALU.add)
-        ghosts2(r, tab)
-        if r == 2:
-            best_lines_b()
-        else:
-            outputs(1, 6400)
-        for k in range(2):
-            a, b = 512 * k, 512 * k + 512
-            act(("tmp2", a, b), (("Ub", 0, 16), ("row16", 32 * k, 32 * k + 32)), AF.Identity)
-            tt(("T3", a, b), ((tab, 0, E1), ("US16", 32 * k, 32 * k + 32)), ("tmp2", a, b), ALU.add)
-        if r == 2:
-            u_lists(1)
-            act(("sy", 0, 1024), (("yt16", 0, 16), ("row16", 0, 64)), AF.Identity)
-        else:
-            sire_act(2, 512, 1024)
-            sire_cols(2)
-        act(("T4", 0, 1024), ((tab, 0, E1), ("US16", 64, 128)), AF.Identity, KB if r == 2 else 0.0)
-        tt(("G3", 0, 1024), ((tab, Z0, X3), ("UD16", 0, 64)), ("T3", 0, 1024), ALU.add)
+
+    def generation3(tab, k):
+        a, b = 512 * k, 512 * k + 512
+        act(("tmp2", a, b), ((tab, 0, E1), ("US16", 32 * k, 32 * k + 32)), AF.Identity)
+        tt(("T3", a, b), (("Ub", 0, 16), ("row16", 32 * k, 32 * k + 32)), ("tmp2", a, b), ALU.add)
+
+    def generation3_end(tab, k):
+        a, b = 512 * k, 512 * k + 512
+        tt(("G3", a, b), ((tab, Z0, X3), ("UD16", 32 * k, 32 * k + 32)), ("T3", a, b), ALU.add)
+
+    def extreme3(o, K, U2, n, dm, cmp, out):
+        sign = 2.0 if cmp == ALU.is_lt else -2.0
+        ts(("sm16", n, n + 1), K, sign, ALU.mult)
+        ts(U2, K, sign, ALU.mult)
+        tt(("lk", n + 24, n + 40), (("G3", 0, 1024), ("sm16", n, n + 1)), dm, ALU.mult)
+        red(("cl", n, n + 1), ("lk", n + 24, n + 40))
+        ts(out, ("cl", n, n + 1), ("tmp", o + 511, o + 512), cmp, U2, ALU.add)
 
     tab = "tabB"
-    begin(2, tab)
+    generation1(2, tab, both(first_rows, lines), (2, 2, 1, 1))
+    generation3(tab, 0)
+    generation3(tab, 1)
+    act(("sy", 0, 1024), (("yt16", 0, 16), ("row16", 0, 64)), AF.Identity)
+    generation3_end(tab, 0)
+    double3(tab, 0, 512)
+    generation3_end(tab, 1)
+    run(running(0, "G3", 0, 512, ALU.max, 512))
+    count(0, 512, 1, KX)
     ghosts3(2, tab)
-    scan(("tmp", 0, 1024), ("G3", 0, 1024), ("G3", 0, 1024), 0.0, ALU.max, ALU.max)
-    double3(tab)
-    act(("junk", 0, 1024), ("tmp", 0, 1024), AF.Sign, ("tmp", 1023, 1024), -1.0, JL[1])
-    scan(("FH", 0, 1024), ("G3", 0, 1024), ("G3", 0, 1024), 1.0e9, ALU.min, ALU.min)
-    act(("junk", 0, 1024), ("FH", 0, 1024), AF.Sign, ("FH", 1023, 1024), -1.0, JB[1])
-    sire_act(1)
-    chain2("land2")
+    u_s(1)
+    run(running(512, "G3", 0, 512, ALU.min, 512))
+    extreme3(0, KX, RX, 40, ("dmo", 0, 16), ALU.is_lt, ("sm16", 42, 43))
+    tt(("lk", 48, 64), (("sy", 0, 1024), ("sm16", 42, 43)), ("dmh", 0, 16), ALU.mult)
+    red(("land2", 4 * rank, 4 * rank + 1), ("lk", 48, 64))
     share_aim("land2", "a_aim2")
-    tt(("key", 0, 1024), ((tab, Z0, TW), ("UD16", 64, 128)), ("T4", 0, 1024), ALU.add)
-    rows_a(0, lambda: aims(2, "land2"))
-    rows_b()
+    count(512, 512, 1, KN)
+    keys_s(tab, 1)
+    extreme3(512, KN, RN, 56, ("dmj", 0, 16), ALU.is_gt, JB[1])
     best_a(2)
-    sire_cols(1)
-    ts(("sm16", 58, 59), JB[1], -1.0, ALU.mult)
-    rows_c(64)
-    best_b(2)
+    copy(("sm16", 58, 59), JB[1])
+    u_d(1)
+    ts((tab, X3 + 512, X3 + 1024), ("G3", 512, 1024), 0.5, ALU.mult)
+    tt(("key", 0, 1024), ((tab, Z0, TW), ("UD16", 64, 128)), ("T4", 0, 1024), ALU.add)
+    turn_keys(("key",))
+    to_list("pE", 0, "ZS", "sy", 0)
+    aims(2, "land2")
+    founders(3)
 
     tab = "tabA"
-    begin(3, tab)
-    double3(tab)
+    generation1(3, tab)
+    last_rows = rows(64)
+    run(last_rows, 2)
+    ts(("bH", 0, 16), ("pY", 144, 160), SGN, ALU.mult)
+    ts(("bR", 0, 16), ("pY", 144, 160), PD2, ALU.mult)
+    run(last_rows, 1)
+    tt(("bT", 16, 32), ("bR", 0, 16), ("bH", 0, 16), ALU.add)
+    run(last_rows, 1)
+    ts(("yso", 0, 64), ("pE", 0, 64), 6400.0, ALU.add)
+    aim_out(1)
+    aim_out(2)
+    dma("S", [(T.yt[:], T.yto[:])], "o_yt", [("yto", 0, 2)], [])
+    run(last_rows, 1)
+    generation3(tab, 0)
+    run(last_rows, 1)
+    generation3(tab, 1)
+    run(last_rows, 1)
+    act(("T4", 0, 1024), ((tab, 0, E1), ("US16", 64, 128)), AF.Identity)
+    act(("sf", 0, 1024), (("bT", 16, 32), ("row16", 64, 128)), AF.Identity)
+    to_list("pE", 64, "ZB", "sf", 0)
+    for k in range(2):
+        a, b = 512 * k, 512 * k + 512
+        generation3_end(tab, k)
+        act(("yo", a, b), ("G3", a, b), AF.Identity, 65535.0, -0.25)
+        dma("S", [(T.yf[:, a:b], T.yo[:, a:b])], "o_f3" + "ab"[k], [("yo", a, b)], [])
     ghosts3(3, tab)
+    double3(tab)
     ts(("HB", 0, 16), (("G3", 0, 1024), ("sm16", 58, 59)), 0.5, ALU.mult)
     tt(("T3", 0, 1024), (("HB", 0, 16), ("row16", 64, 128)), ("T4", 0, 1024), ALU.add)
-    act(("yo", 0, 1024), ("G3", 0, 1024), AF.Identity, 65535.0, -0.25)
-    dma("S", [(T.yf[:, 0:1024], T.yo[:, 0:1024])], "o_f3", [("yo", 0, 1024)], [])
+    ts(("yso", 64, 128), ("pE", 64, 128), 9600.0, ALU.add)
+    dma("S", [(T.ys[:], T.yso[:])], "o_ys", [("yso", 0, 128)], [])
     b = 0
     for k, n in enumerate((384, 384, 256)):
         a, b = b, b + n
         tt(("key", a, b), ((tab, Z0, TW), ("UD16", 64 + a // 16, 64 + b // 16)), ("T3", a, b), ALU.add)
         act(("yo", 1024 + a, 1024 + b), ("key", a, b), AF.Identity, 65535.0, -0.25)
         dma("S", [(T.yf[:, 1024 + a:1024 + b], T.yo[:, 1024 + a:1024 + b])], "o_f4%s" % "abc"[k], [("yo", 1024 + a, 1024 + b)], [])
-        if k == 1:
-            outputs(2, 9600)
-            dma("S", [(T.ys[:], T.yso[:])], "o_ys", [("yso", 0, 128)], [])
-            dma("S", [(T.yt[:], T.yto[:])], "o_yt", [("yto", 0, 2)], [])
 
     for s in sorted(total):
         if known["G"].get(s, 0) < total[s]:

@@ -13,9 +13,9 @@ X3 = Z0 + 6528
 G3X = Z0 + 7552
 TW = Z0 + 7680
 WW = 3080
-WV = 1700
+WV = 2000
 D2 = Z0 + 3200
-VD = (1024, 1600, 2400)
+VD = (1536, 1600, 2400)
 
 
 def _sb(n, d=F32):
@@ -24,15 +24,15 @@ def _sb(n, d=F32):
 
 SCRATCH = {
     "sireI": _sb(384, I32), "damI": _sb(528, I32), "mgI": _sb(32, I32), "aimI": _sb(1, I32),
-    "trI": _sb(3072, I32), "W": _sb(WW, I32),
-    "y1": _sb(3200), "FH": _sb(3200), "tabA": _sb(TW), "tabB": _sb(TW),
+    "trI": _sb(3200, I32), "W": _sb(WW, I32), "W2": _sb(3072, I32), "gI": _sb(128, I32),
+    "FH": _sb(3200), "tabA": _sb(TW), "tabB": _sb(TW),
     "tmp": _sb(3072), "tmp2": _sb(1024), "CF": _sb(2304),
     "T3": _sb(1024), "T4": _sb(1024), "key": _sb(1024), "G3": _sb(1024), "sg": _sb(1024),
     "yo": _sb(2048), "sf": _sb(1024, B16), "sy": _sb(1024), "seg": _sb(512),
-    "io": _sb(512), "dmj": _sb(512), "mk": _sb(512), "msc": _sb(512), "junk": _sb(512, B16),
-    "blk": _sb(128), "bs1": _sb(128), "bd1": _sb(128), "bs2": _sb(128), "bd2": _sb(128),
-    "ident": _sb(128), "idm": _sb(128), "id8": _sb(128), "ZS": _sb(144), "ZD": _sb(144), "zero": _sb(144), "one": _sb(128),
-    "w1": _sb(512), "w3": _sb(128), "cix": _sb(256), "nmx": _sb(256), "nmn": _sb(256),
+    "io": _sb(256), "dmj": _sb(32), "mk": _sb(512), "xt": _sb(512), "junk": _sb(512, B16),
+    "blk": _sb(128), "bs1": _sb(128), "bs2": _sb(128), "bd2": _sb(128), "SEL": _sb(32),
+    "ident": _sb(128), "idm": _sb(128), "id8": _sb(128), "ZS": _sb(144), "zero": _sb(144), "one": _sb(128),
+    "w1": _sb(32), "w3": _sb(128), "cix": _sb(256), "nmx": _sb(256), "nmn": _sb(256),
     "zerob": _sb(144, B16), "idb": _sb(128, B16), "perm0": _sb(128, B16), "perm1": _sb(128, B16), "rT": _sb(128, B16),
     "ZSb": _sb(144, B16), "ZB": _sb(144, B16), "bH": _sb(16, B16),
     "pI": _sb(8, I32), "cc": _sb(32), "dmo": _sb(16), "dmh": _sb(16),
@@ -162,7 +162,7 @@ def rank_program(g, core, T, topo):
         op("P", lambda: g.tensor.matmul(ap(out, m), ap(lhsT, k), ap(rhs, k), start, stop), [lhsT, rhs], [out], acc=True)
 
     def iota(out, pattern, base, cm):
-        if out[0] in ("pI", "W"):
+        if out[0] in ("pI", "W", "W2"):
             op("G", lambda: g.iota(ap(out), pattern, base, cm), [], [out])
         else:
             op("G", lambda: g.iota(ap(out), pattern, base, cm, allow_small_or_imprecise_dtypes=True), [], [out])
@@ -232,19 +232,23 @@ def rank_program(g, core, T, topo):
     for k in range(4):
         a, b = 768 * k, 768 * k + 768
         dma("A", [(T.trI[:, a:b], T.trait[:, a:b])], "l_t%d" % k, [], [("trI", a, b)])
-    PM, OWN, KB, PS2, PD2, T1, HOWN, HT1, NT1, SGN = [("cc", k, k + 1) for k in range(10)]
+    PM, OWN, KB, PS2, PD2, HOWN, HT1, SGN = [("cc", k, k + 1) for k in range(8)]
     iota(("pI", 0, 1), [[0, 1]], 0, 1)
-    iota(("io", 0, 512), [[0, 32], [1, 16]], 0, 0)
+    iota(("io", 0, 256), [[0, 16], [1, 16]], 0, 0)
     iota(("W", WV, WW), [[0, WW - WV]], 0, 0)
-    iota(("tabA", 0, Z0), [[0, Z0]], 0, 0)
-    iota(("tabB", 0, Z0), [[0, Z0]], 0, 0)
     iota(("zero", 0, 144), [[0, 144]], 0, 0)
     ts(("pI", 1, 2), ("pI", 0, 1), 15, ALU.bitwise_and)
-    fill(("W", 0, WV), 0)
+    fill(("W", 0, 200), 0)
     copy(PM, ("pI", 1, 2))
-    act(("seg", 0, 512), ("io", 0, 512), AF.Sign)
-    act(("w1", 0, 512), ("io", 0, 512), AF.Abs, PM, -1.0)
-    act(("dmj", 0, 512), ("w1", 0, 512), AF.Relu, 1.0, -1.0)
+    fill(("W", 200, 1300), 0)
+    ts(HT1, ("aimI", 0, 1), 0.5, ALU.mult)
+    copy(("mg16", 0, 32), ("mgI", 0, 32))
+    fill(("W", 1300, WV), 0)
+    act(("w1", 0, 32), ("io", 0, 32), AF.Abs, PM, -1.0)
+    act(("seg", 0, 256), ("io", 0, 256), AF.Sign)
+    act(("dmj", 0, 32), ("w1", 0, 32), AF.Relu, 1.0, -1.0)
+    act(("seg", 256, 512), ("io", 0, 256), AF.Sign)
+    act(("i16", 0, 16), ("io", 0, 16), AF.Identity, 0.0, 0.0625)
     own = [4 * rank + k for k in range(4)]
     d1, s2, d2 = [(4 * rank + 4 + k) % 16 for k in range(3)]
     wp = [(T.W[own[0]:128:16, 8:WW], T.sire[:, 0:192])]
@@ -256,10 +260,6 @@ def rank_program(g, core, T, topo):
     dma("S", [(T.damI[:, 0:192], T.dam[:, 0:192])], "l_dam0", [], [("damI", 0, 192)])
     dma("S", [(T.sireI[:, 192:384], T.sire[:, 192:384])], "l_sire2", [], [("sireI", 192, 384)])
     dma("S", [(T.damI[:, 192:384], T.dam[:, 192:384])], "l_dam2", [], [("damI", 192, 384)])
-    copy(("mg16", 0, 32), ("mgI", 0, 32))
-    copy(T1, ("aimI", 0, 1))
-    ts(HT1, ("aimI", 0, 1), 0.5, ALU.mult)
-    ts(NT1, ("aimI", 0, 1), -1.0, ALU.mult)
 
     def places():
         v = lambda n: (n, 0, 144)
@@ -274,6 +274,7 @@ def rank_program(g, core, T, topo):
         ts(v("AI"), v("EI"), 15, ALU.bitwise_and)
         ts(v("qq"), c, 9472.0, ALU.is_ge)
         ts(v("EF"), v("AI"), 3071.0, ALU.mult, 128.0, ALU.add)
+        yield
         tt(v("is2"), v("pp"), v("qq"), ALU.subtract)
         tt(v("EG"), v("EF"), v("EI"), ALU.add)
         ts(("mn", 0, 128), ("damI", 384, 512), 6400.0, ALU.min)
@@ -284,54 +285,67 @@ def rank_program(g, core, T, topo):
         ts(HOWN, ("pI", 2, 3), float(rank), ALU.is_equal, 0.5, ALU.mult)
         ts(KB, PM, -1.0 / 64, ALU.mult, 15.0 / 64, ALU.add)
         ts(SGN, PD2, -1.0, ALU.mult, PS2, ALU.add)
+        yield
 
-    def y_chunk(k):
+    def founders1(k):
         a, b = 768 * k, 768 * k + 768
-        ts(("y1", a, b), ("trI", a, b), T1, ALU.subtract)
-        act(("FH", a, b), ("y1", a, b), AF.Abs, 0.0, 0.5)
+        act(("FH", a, b), ("trI", a, b), AF.Abs, HT1, -0.5)
 
     def double(tab, a, b):
         ts((tab, Z0 + a, Z0 + b), ("FH", a, b), 2.0, ALU.mult)
 
     def ghosts0():
         act(("gt", 0, 128), (("trI", 0, 3072), ("mg16", 0, 8)), AF.Abs, HT1, -0.5)
-        act(("gs", 0, 128), (("trI", 0, 3072), ("mg16", 0, 8)), AF.Identity, NT1)
-        ship_two(("gs", 0, 128), ("y1", 3072, 3200), ("gt", 0, 128), ("FH", 3072, 3200), "a_g0")
+        copy(("gI", 0, 128), (("trI", 0, 3072), ("mg16", 0, 8)))
+        ship_two(("gI", 0, 128), ("trI", 3072, 3200), ("gt", 0, 128), ("FH", 3072, 3200), "a_g0")
 
     tab = "tabA"
-    y_chunk(0)
-    y_chunk(1)
+    for c, r0, r1 in ((0, s2, d2), (16, own[0], d1)):
+        select(("SEL", c, c + 16), ("zero", 0, 16), [[r0 - r1, 2], [-16, 8]], ALU.not_equal, 1.0, -r0, 1)
+    pl = places()
+    run(pl, 1)
+    founders1(0)
+    founders1(1)
     ghosts0()
-    y_chunk(2)
-    y_chunk(3)
+    founders1(2)
+    founders1(3)
     copy(("sire16", 0, 192), ("sireI", 0, 192))
-    places()
-    dma("S", [(T.trI[r:128:16, 0:3072], T.sire[:, 192:384]) for r in own], "l_tr", [], [("trI", 0, 3072)])
-    for b, r in (("bs1", own[0]), ("bd1", d1), ("bs2", s2), ("bd2", d2)):
-        mark((b, 0, 128), [[-16, 8], [0, 16]], -r)
+    run(pl)
     ROW = [[-16, 9], [1000, 16]]
-    mark(("ZS", 0, 144), ROW, -s2 - 15000)
     mark(("ident", 0, 128), [[-1, 128]], 0)
     mark(("idm", 0, 128), [[-1, 128]], 0, -6400.0)
     mark(("id8", 0, 128), [[-1, 128]], 0, -float(Z0))
-    mark(("ZD", 0, 144), ROW, -d2 - 15000)
+    mark(("ZS", 0, 144), ROW, -s2 - 15000)
+    for b, r in (("bs1", own[0]), ("bs2", s2), ("bd2", d2)):
+        mark((b, 0, 128), [[-16, 8], [0, 16]], -r)
 
-    def to_list(pb, o0, z, flat, f0, x0=0, more=()):
+    def to_list(pb, o0, z, flat):
         for i in range(16):
-            mm((pb, o0, o0 + 64), (z, 15 - i, 143 - i), (flat, f0 + i, f0 + 1024, 16), i == 0, i == 15 and not more)
-        for k, (w, x) in enumerate(more):
-            mm((pb, o0, o0 + 64), (w, 0, 128), (x, x0, x0 + 64), False, k == len(more) - 1)
+            mm((pb, o0, o0 + 64), (z, 15 - i, 143 - i), (flat, i, 1024, 16), i == 0, i == 15)
 
     def flat(h):
         act(("CF", 1024 * h, 1024 * h + 1024), (("W", 0, WW), ("pos16", 64 * h, 64 * h + 64)), AF.Identity)
 
     SB, DB = (("pS", 0), ("pD", 0)), (("pS", 64), ("pE", 128))
 
-    def list_s(h):
-        to_list(*SB[h], "ZS", "CF", 1024 * h, 64 * h, (("ident", "mn"), ("idm", "pp"), ("id8", "qq")))
+    def turn_flat(pb, f0, m, n):
+        for i in range(16):
+            mm((pb, i, 16 * n, 16), ("CF", f0 + i, f0 + 16 * m, 16), ("SEL", 0, n), m=m)
 
-    def list_d(h):
-        to_list(*DB[h], "ZD", "CF", 1024 * h, 64 * h, (("ident", "mn"), ("ident", "x1"), ("idm", "is2")))
+    def take(e, pb, m, n):
+        o, a = ("xt", 0, n), (pb, 0, n)
+        if e == "A":
+            op("A", lambda: g.scalar.activation(ap(o, m), ap(a, m), AF.Identity), [a], [o])
+        else:
+            op("V", lambda: g.vector.tensor_copy(ap(o, m), ap(a, m)), [a], [o])
+
+    SELF = ((("ident", "mn"), ("idm", "pp"), ("id8", "qq")), (("ident", "mn"), ("ident", "x1"), ("idm", "is2")))
+
+    def turn_back(h):
+        for r, (pb, o) in enumerate((SB[h], DB[h])):
+            for k, (w, x) in enumerate(SELF[r]):
+                mm((pb, o, o + 64), (w, 0, 128), (x, 64 * h, 64 * h + 64), k == 0, False)
+            mm((pb, o, o + 64), ("xt", 128 * r, 128 * r + 128), ("ident", 0, 64), False, True, k=64)
 
     def u_s(h):
         ts(("US16", 64 * h, 64 * h + 64), (SB[h][0], SB[h][1], SB[h][1] + 64), float(Z0), ALU.add)
@@ -339,16 +353,15 @@ def rank_program(g, core, T, topo):
     def u_d(h):
         copy(("UD16", 64 * h, 64 * h + 64), (DB[h][0], DB[h][1], DB[h][1] + 64))
 
-    PART = [0]
-    for n in (512, 768, 896, 896):
-        PART.append(PART[-1] + n)
+    PART = (0, 512, 1280, 2176, 3072)
+    EVEN = tuple(range(0, 3073, 512))
 
-    def sires1(k):
-        a, b = PART[k], PART[k + 1]
+    def sires1(k, part=PART):
+        a, b = part[k], part[k + 1]
         act(("tmp", a, b), (("FH", 0, 3072), ("sire16", a // 16, b // 16)), AF.Identity)
 
-    def dams1(tab, k):
-        a, b = PART[k], PART[k + 1]
+    def dams1(tab, k, part=PART):
+        a, b = part[k], part[k + 1]
         tt((tab, Z0 + 3200 + a, Z0 + 3200 + b), (("FH", 0, 3200), ("dam16", a // 16, b // 16)), ("tmp", a, b), ALU.add)
 
     MS1, MD1, MS2, MD2 = [("ms16", 8 * k, 8 * k + 8) for k in range(4)]
@@ -374,37 +387,39 @@ def rank_program(g, core, T, topo):
         ts(("gs", o, o + 128), (("G3", 0, 1024), ("mg16", 24, 32)), 0.5, ALU.mult)
         ship("gs", o, o + 128, tab, G3X, G3X + 128, "a_g3%d" % r)
 
+    copy(("CF", 2048, 2304), (("W", 0, WW), ("pos16", 128, 144)))
+    turn_flat("pA", 2048, 16, 32)
     sires1(0)
     double(tab, 0, VD[0])
-    act(("CF", 2048, 2304), (("W", 0, WW), ("pos16", 128, 144)), AF.Identity)
-    mm(("pC", 0, 128), ("bs1", 0, 128), ("CF", 2176, 2304))
-    mm(("pC", 128, 256), ("bd1", 0, 128), ("CF", 2176, 2304))
-    mm(("pC", 256, 384), ("bs2", 0, 128), ("CF", 2048, 2176))
-    mm(("pC", 384, 512), ("bd2", 0, 128), ("CF", 2048, 2176))
     sires1(1)
     flat(0)
-    list_s(0)
-    list_d(0)
     sires1(2)
     sires1(3)
     copy(("dam16", 0, 192), ("damI", 0, 192))
     dams1(tab, 0)
-    tt(("mk", 0, 512), ("pC", 0, 512), ("dmj", 0, 512), ALU.mult)
+    take("V", "pA", 16, 512)
+    for n, (r, c) in enumerate(((2, 8), (3, 8), (0, 0), (1, 0))):
+        mm(("pC", 8 * n, 8 * n + 8), ("xt", 128 * r, 128 * r + 128), ("ident", c, c + 8), k=16)
     copy(("sire16", 192, 384), ("sireI", 192, 384))
-    scan(("msc", 0, 512), ("seg", 0, 512), ("mk", 0, 512), 0.0, ALU.mult, ALU.add)
     copy(("dam16", 192, 384), ("damI", 192, 384))
-    copy(("ms16", 0, 32), ("msc", 15, 512, 16))
-    ghosts1(1, tab)
-    iota(("cix", 0, 256), [[1, 16], [64, 16]], 0, 0)
-    iota(("one", 0, 128), [[0, 128]], 1, 0)
-    select(("w3", 0, 128), ("one", 0, 128), [[-16, 8], [0, 16]], ALU.is_ge, 0.0, 0, 1)
-    select(("blk", 0, 128), ("w3", 0, 128), [[16, 8], [0, 16]], ALU.is_ge, 0.0, 15, -1)
     dams1(tab, 1)
-    act((tab, Z0 + VD[0], Z0 + 3200), ("y1", VD[0], 3200), AF.Abs)
+    turn_flat("pB", 0, 64, 16)
+    copy(("ms16", 0, 32), ("pC", 0, 32))
+    ghosts1(1, tab)
+    iota(("tabA", 0, Z0), [[0, Z0]], 0, 0)
+    iota(("tabB", 0, Z0), [[0, Z0]], 0, 0)
+    iota(("cix", 0, 256), [[1, 16], [64, 16]], 0, 0)
+    iota(("W2", 0, 900), [[0, 900]], 0, 0)
+    act((tab, Z0 + VD[0], Z0 + 3200), ("FH", VD[0], 3200), AF.Identity, 0.0, 2.0)
     dma("S", [(T.W[q:128:16, 8:WW], T.sire[:, 0:192]) for q in own[1:]], "l_w2", [], [("W", 8, WW)])
     dams1(tab, 2)
     dams1(tab, 3)
     ghosts2(1, tab)
+    iota(("W2", 900, 3072), [[0, 2172]], 0, 0)
+    dma("S", [(T.W2[r:128:16, 0:3072], T.sire[:, 192:384]) for r in own], "l_tr", [], [("W2", 0, 3072)])
+    iota(("one", 0, 128), [[0, 128]], 1, 0)
+    select(("w3", 0, 128), ("one", 0, 128), [[-16, 8], [0, 16]], ALU.is_ge, 0.0, 0, 1)
+    select(("blk", 0, 128), ("w3", 0, 128), [[16, 8], [0, 16]], ALU.is_ge, 0.0, 15, -1)
     iota(("zerob", 0, 144), [[0, 144]], 0, 0)
     mark(("idb", 0, 128), [[-1, 128]], 0, on="zerob")
     for h in range(2):
@@ -414,13 +429,16 @@ def rank_program(g, core, T, topo):
     for a in range(0, 3072, 512):
         b = a + 512
         act(("tmp", a, b), ((tab, Z0, OWN1), ("sire16", 192 + a // 16, 192 + b // 16)), AF.Identity)
+        if a == 1024:
+            take("A", "pB", 64, 256)
+            turn_back(0)
         if a == 2560:
             u_s(0)
-            u_d(0)
         tt(("tabB", D2 + a, D2 + b), ((tab, Z0, E1), ("dam16", 192 + a // 16, 192 + b // 16)), ("tmp", a, b), ALU.add)
 
     def keys_s(tab, h):
-        act(("T4", 0, 1024), ((tab, 0, E1), ("US16", 64 * h, 64 * h + 64)), AF.Identity, KB)
+        for a in (0, 512):
+            act(("T4", a, a + 512), ((tab, 0, E1), ("US16", 64 * h + a // 16, 64 * h + a // 16 + 32)), AF.Identity, KB)
 
     def turn_keys(parts, i0=0, i1=8):
         for i in range(i0, i1):
@@ -428,10 +446,11 @@ def rank_program(g, core, T, topo):
             for k, b in enumerate(parts):
                 mm(o, (b, i, 1024, 8), ("ident", 0, 128), k == 0, k == len(parts) - 1)
 
-    def rows(c0):
-        for k, pb in enumerate(("pA", "pB")):
-            scan(("sg", 512 * k, 512 * k + 512), ("seg", 0, 512), (pb, 0, 512), 0.0, ALU.mult, ALU.max)
-            yield
+    def rows(c0, piece=512):
+        for k, (pb, n) in enumerate((("pA", piece), ("pB", 512))):
+            for a in range(0, 512, n):
+                scan(("sg", 512 * k + a, 512 * k + a + n), ("seg", 0, n), (pb, a, a + n), 0.0, ALU.mult, ALU.max)
+                yield
         ts(("ri", 0, 64), ("sg", 15, 1024, 16), 64.0, ALU.mult)
         yield
         ts(("rb", 0, 64), ("ri", 0, 64), 15, ALU.bitwise_and)
@@ -491,7 +510,7 @@ def rank_program(g, core, T, topo):
         yield
         ts(("sm16", 16, 17), CX, KX, ALU.add, 15.0 * 192, ALU.add)
         yield
-        tt(("lk", 0, 16), (("trI", 0, 3072), ("sm16", 16, 17)), ("dmo", 0, 16), ALU.mult)
+        tt(("lk", 0, 16), (("W2", 0, 3072), ("sm16", 16, 17)), ("dmo", 0, 16), ALU.mult)
         yield
         red(("cl", 17, 18), ("lk", 0, 16))
         yield
@@ -502,7 +521,7 @@ def rank_program(g, core, T, topo):
         yield
         f = founder_b(20)
         yield
-        tt(("lk", 32, 48), (("y1", 0, 3072), f), ("dmh", 0, 16), ALU.mult)
+        tt(("lk", 32, 48), (("trI", 0, 3072), f), ("dmh", 0, 16), ALU.mult)
         yield
         red((land, 4 * rank, 4 * rank + 1), ("lk", 32, 48))
 
@@ -517,7 +536,9 @@ def rank_program(g, core, T, topo):
         ts(("off16", 16, 32), ("i16", 0, 16), KN, ALU.subtract, 16.0, ALU.mult)
         tt(("mk", 256, 512), (WIN2, ("off16", 16, 32)), ("nmn", 0, 256), ALU.add)
         red(RN, ("mk", 256, 512), ALU.min)
+        yield
         ts(CN, RN, ("tmp", 3071, 3072), ALU.subtract, 64.0, ALU.mult)
+        yield
         ts(("sm16", 48, 49), CN, 192.0, ALU.mult, KN, ALU.subtract)
         ts(JB[0], KN, -16.0, ALU.mult, CN, ALU.add)
         copy(("bg", 0, 16), (("W", 8, WW), ("sm16", 48, 49)))
@@ -525,9 +546,12 @@ def rank_program(g, core, T, topo):
         mm(("pM", 272, 288), ("bd2", 0, 128), ("bg", 0, 16))
         best_a(1)
         turn_keys(("T4", "T3"), 4, 8)
+        yield
+        yield
         tt(("bm", 0, 32), ("pM", 256, 288), ("dmj", 0, 32), ALU.mult)
         ts(("bT", 0, 16), ("pY", 128, 144), PS2, ALU.mult)
         scan(("bsc", 0, 32), ("seg", 0, 32), ("bm", 0, 32), 0.0, ALU.mult, ALU.add)
+        yield
         copy(("sm16", 52, 56, 2), ("bsc", 15, 32, 16))
 
     def best_lines():
@@ -541,7 +565,7 @@ def rank_program(g, core, T, topo):
         yield
         f = founder_b(32)
         yield
-        ts(("yt16", 16, 32), (("y1", 0, 3072), f), OWN, ALU.mult)
+        ts(("yt16", 16, 32), (("trI", 0, 3072), f), OWN, ALU.mult)
         yield
         tt(("yt16", 0, 16), ("yt16", 16, 32), ("bT", 0, 16), ALU.add)
         yield
@@ -551,18 +575,18 @@ def rank_program(g, core, T, topo):
 
     def founders(r):
         for k in range(4):
-            act(("FH", 800 * k, 800 * k + 800), ("y1", 800 * k, 800 * k + 800), AF.Abs, BH[r - 2], -0.5)
+            act(("FH", 800 * k, 800 * k + 800), ("trI", 800 * k, 800 * k + 800), AF.Abs, BH[r - 2], -0.5)
 
     def aim_out(r):
-        ts(("yto", r - 1, r), BH[r - 1], 2.0, ALU.mult, T1, ALU.add)
+        ts(("yto", r - 1, r), BH[r - 1], 2.0, ALU.mult)
 
     act(("dmo", 0, 16), ("dmj", 0, 16), AF.Identity, 0.0, OWN)
     act(("dmh", 0, 16), ("dmj", 0, 16), AF.Identity, 0.0, HOWN)
-    act(("i16", 0, 16), ("io", 0, 16), AF.Identity, 0.0, 0.0625)
     act(("nmn", 0, 256), ("cix", 0, 256), AF.Abs, PM, -1.0 / 64)
     act(("nmx", 0, 256), ("nmn", 0, 256), AF.Identity, 15.0 / 64, -1.0)
     keys_s(tab, 0)
     run(running(0, "tabB", D2, 1536, ALU.max, 1536))
+    u_d(0)
     least = running(1536, "tabB", D2, 1536, ALU.min, 128)
     weave(chain1("land1"), least)
     share_aim("land1", "a_aim1")
@@ -573,24 +597,23 @@ def rank_program(g, core, T, topo):
     count(1536, 1536, 8, KN)
     aims(1, "land1")
     founders(2)
-    best1()
-    first_rows = rows(0)
-    lines = best_lines()
-    run(lines, 3)
-    run(first_rows, 1)
+    first_best, first_rows, lines = best1(), rows(0, 128), best_lines()
+    doubling = (double("tabB", a, a + 200) for a in range(0, 800, 200))
+    run(both(first_best, first_rows), 4)
+    weave(first_best, doubling)
+    run(both(doubling, lines))
 
-    def generation1(r, tab, filler=iter(()), steps=(0, 0, 0, 0)):
+    def generation1(r, tab, done, part, filler, steps):
         nv = VD[r - 1]
-        for a in range(0, nv, 800):
+        for a in range(done, nv, 800):
             double(tab, a, a + 800)
         ghosts1(r, tab)
-        for k in range(4):
+        for k in range(len(part) - 1):
             run(filler, steps[k])
-            sires1(k)
-            dams1(tab, k)
+            sires1(k, part)
+            dams1(tab, k, part)
             if r == 2 and k == 2:
-                list_s(1)
-                list_d(1)
+                turn_flat("pA", 1024, 64, 16)
         act((tab, Z0 + nv, Z0 + 3200), ("FH", nv, 3200), AF.Identity, 0.0, 2.0)
         ghosts2(r, tab, lambda: copy(("ub1", 0, 16), ((tab, Z0, OWN1), BS)))
         tt(("Ub", 0, 16), ((tab, Z0, E1), BD), ("ub1", 0, 16), ALU.add)
@@ -609,13 +632,18 @@ def rank_program(g, core, T, topo):
         ts(("sm16", n, n + 1), K, sign, ALU.mult)
         ts(U2, K, sign, ALU.mult)
         tt(("lk", n + 24, n + 40), (("G3", 0, 1024), ("sm16", n, n + 1)), dm, ALU.mult)
+        yield
         red(("cl", n, n + 1), ("lk", n + 24, n + 40))
+        yield
         ts(out, ("cl", n, n + 1), ("tmp", o + 511, o + 512), cmp, U2, ALU.add)
+        yield
 
     tab = "tabB"
-    generation1(2, tab, both(first_rows, lines), (2, 2, 1, 1))
+    generation1(2, tab, 800, PART, both(first_rows, lines), (2, 2, 1, 1))
     generation3(tab, 0)
     generation3(tab, 1)
+    take("A", "pA", 64, 256)
+    turn_back(1)
     act(("sy", 0, 1024), (("yt16", 0, 16), ("row16", 0, 64)), AF.Identity)
     generation3_end(tab, 0)
     double3(tab, 0, 512)
@@ -625,27 +653,29 @@ def rank_program(g, core, T, topo):
     ghosts3(2, tab)
     u_s(1)
     run(running(512, "G3", 0, 512, ALU.min, 512))
-    extreme3(0, KX, RX, 40, ("dmo", 0, 16), ALU.is_lt, ("sm16", 42, 43))
+    halves = (ts((tab, X3 + a, X3 + a + 128), ("G3", a, a + 128), 0.5, ALU.mult) for a in range(512, 1024, 128))
+    weave(extreme3(0, KX, RX, 40, ("dmo", 0, 16), ALU.is_lt, ("sm16", 42, 43)), halves)
     tt(("lk", 48, 64), (("sy", 0, 1024), ("sm16", 42, 43)), ("dmh", 0, 16), ALU.mult)
+    run(halves)
     red(("land2", 4 * rank, 4 * rank + 1), ("lk", 48, 64))
     share_aim("land2", "a_aim2")
     count(512, 512, 1, KN)
     keys_s(tab, 1)
-    extreme3(512, KN, RN, 56, ("dmj", 0, 16), ALU.is_gt, JB[1])
+    run(extreme3(512, KN, RN, 56, ("dmj", 0, 16), ALU.is_gt, JB[1]))
     best_a(2)
     copy(("sm16", 58, 59), JB[1])
     u_d(1)
-    ts((tab, X3 + 512, X3 + 1024), ("G3", 512, 1024), 0.5, ALU.mult)
-    tt(("key", 0, 1024), ((tab, Z0, TW), ("UD16", 64, 128)), ("T4", 0, 1024), ALU.add)
+    for a in (0, 512):
+        tt(("key", a, a + 512), ((tab, Z0, TW), ("UD16", 64 + a // 16, 96 + a // 16)), ("T4", a, a + 512), ALU.add)
     turn_keys(("key",))
-    to_list("pE", 0, "ZS", "sy", 0)
+    to_list("pE", 0, "ZS", "sy")
     aims(2, "land2")
     founders(3)
 
     tab = "tabA"
-    generation1(3, tab)
     last_rows = rows(64)
-    run(last_rows, 2)
+    generation1(3, tab, 0, EVEN, last_rows, (1, 0, 0, 0, 0, 0))
+    run(last_rows, 1)
     ts(("bH", 0, 16), ("pY", 144, 160), SGN, ALU.mult)
     ts(("bR", 0, 16), ("pY", 144, 160), PD2, ALU.mult)
     run(last_rows, 1)
@@ -662,7 +692,7 @@ def rank_program(g, core, T, topo):
     run(last_rows, 1)
     act(("T4", 0, 1024), ((tab, 0, E1), ("US16", 64, 128)), AF.Identity)
     act(("sf", 0, 1024), (("bT", 16, 32), ("row16", 64, 128)), AF.Identity)
-    to_list("pE", 64, "ZB", "sf", 0)
+    to_list("pE", 64, "ZB", "sf")
     for k in range(2):
         a, b = 512 * k, 512 * k + 512
         generation3_end(tab, k)

@@ -8,14 +8,17 @@ Z0 = 8
 OWN1 = Z0 + 6272
 G1 = Z0 + 6272
 E1 = Z0 + 6400
+D2 = Z0 + 6400
+G21 = Z0 + 9472
+E2 = Z0 + 9600
 G2X = Z0 + 6400
 X3 = Z0 + 6528
 G3X = Z0 + 7552
 TW = Z0 + 7680
 WW = 3080
-WV = 2000
-D2 = Z0 + 3200
-VD = (1536, 1600, 2400)
+WV = 2300
+VD = (1920, 1600, 2400)
+GS1, GS2, GS3 = 0, 384, 816
 
 
 def _sb(n, d=F32):
@@ -23,25 +26,26 @@ def _sb(n, d=F32):
 
 
 SCRATCH = {
-    "sireI": _sb(384, I32), "damI": _sb(528, I32), "mgI": _sb(32, I32), "aimI": _sb(1, I32),
+    "sireI": _sb(384, I32), "damI": _sb(512, I32), "mgI": _sb(32, I32), "aimI": _sb(1, I32),
     "trI": _sb(3200, I32), "W": _sb(WW, I32), "W2": _sb(3072, I32), "gI": _sb(128, I32),
-    "FH": _sb(3200), "tabA": _sb(TW), "tabB": _sb(TW),
+    "FH": _sb(3200), "tabA": _sb(E2), "tabB": _sb(TW),
     "tmp": _sb(3072), "tmp2": _sb(1024), "CF": _sb(2304),
     "T3": _sb(1024), "T4": _sb(1024), "key": _sb(1024), "G3": _sb(1024), "sg": _sb(1024),
     "yo": _sb(2048), "sf": _sb(1024, B16), "sy": _sb(1024), "seg": _sb(512),
     "io": _sb(256), "dmj": _sb(32), "mk": _sb(512), "xt": _sb(512), "junk": _sb(512, B16),
     "blk": _sb(128), "bs1": _sb(128), "bs2": _sb(128), "bd2": _sb(128), "SEL": _sb(32),
-    "ident": _sb(128), "idm": _sb(128), "id8": _sb(128), "ZS": _sb(144), "zero": _sb(144), "one": _sb(128),
+    "ident": _sb(128), "idm": _sb(128), "id4": _sb(128), "idn": _sb(128), "idp": _sb(128), "idl": _sb(128), "idh": _sb(128),
+    "ZS": _sb(144), "zero": _sb(144), "one": _sb(128),
     "w1": _sb(32), "w3": _sb(128), "cix": _sb(256), "nmx": _sb(256), "nmn": _sb(256),
     "zerob": _sb(144, B16), "idb": _sb(128, B16), "perm0": _sb(128, B16), "perm1": _sb(128, B16), "rT": _sb(128, B16),
     "ZSb": _sb(144, B16), "ZB": _sb(144, B16), "bH": _sb(16, B16),
     "pI": _sb(8, I32), "cc": _sb(32), "dmo": _sb(16), "dmh": _sb(16),
-    "sire16": _sb(384, U16), "dam16": _sb(384, U16), "mg16": _sb(32, U16), "ms16": _sb(32, U16),
+    "sire16": _sb(384, U16), "dam16": _sb(384, U16), "mg16": _sb(34, U16), "ms16": _sb(40, U16), "c16": _sb(64, U16),
     "pos16": _sb(144, U16), "US16": _sb(128, U16), "UD16": _sb(128, U16), "row16": _sb(128, U16), "sm16": _sb(64, U16),
-    "EI": _sb(144, I32), "AI": _sb(144, I32), "EF": _sb(144), "EG": _sb(144), "EM": _sb(144),
-    "pp": _sb(144), "qq": _sb(144), "is2": _sb(144), "mn": _sb(128), "x1": _sb(128),
-    "gs": _sb(1152), "gt": _sb(384), "ri": _sb(64, I32), "rb": _sb(64, I32), "rbf": _sb(64, B16),
-    "bT": _sb(32), "bR": _sb(32), "bg": _sb(16), "bm": _sb(32), "bsc": _sb(32), "Ub": _sb(16), "ub1": _sb(16), "HB": _sb(16),
+    "AI": _sb(144, I32), "EF": _sb(16), "EG": _sb(16),
+    "cf": _sb(128), "lo": _sb(128), "s1": _sb(128), "s2": _sb(128), "r1": _sb(128), "r2": _sb(128),
+    "gs": _sb(1104), "gt": _sb(400), "ri": _sb(64, I32), "rb": _sb(64, I32), "rbf": _sb(64, B16),
+    "bT": _sb(32), "bR": _sb(32), "bg": _sb(16), "bm": _sb(32), "bsc": _sb(32),
     "cl": _sb(64), "ci": _sb(64, I32), "lk": _sb(128), "land1": _sb(16), "land2": _sb(16),
     "off16": _sb(32, U16), "i16": _sb(16), "bg2": _sb(16), "bm2": _sb(16), "yt16": _sb(32),
     "yso": _sb(128), "yto": _sb(2),
@@ -50,8 +54,9 @@ BANKS = ("pC", "pS", "pD", "pM", "pY", "pA", "pB", "pE")
 for _b in BANKS:
     SCRATCH[_b] = ("psum", [128, 512], F32)
 SEMAPHORES = ["qV", "qA", "qP", "qG", "sent", "l_sire", "l_sire2", "l_dam0", "l_dam1", "l_dam2", "l_mg", "l_aim",
-              "l_t0", "l_t1", "l_t2", "l_t3", "l_w", "l_w2", "l_tr", "o_ys", "o_yt", "o_f3a", "o_f3b", "o_f4a", "o_f4b", "o_f4c",
-              "a_g0", "a_g11", "a_g12", "a_g13", "a_g21", "a_g22", "a_g23", "a_g32", "a_g33", "a_aim1", "a_aim2"]
+              "l_t0", "l_t1", "l_t2", "l_t3", "l_w", "l_w2", "l_tr", "o_ys", "o_yt", "o_f30", "o_f31",
+              "o_f40", "o_f41", "o_f42", "o_f43",
+              "a_g0", "a_g0t", "a_g11", "a_g12", "a_g13", "a_g21", "a_g22", "a_g23", "a_g32", "a_g33", "a_aim1", "a_aim2"]
 
 
 def rank_program(g, core, T, topo):
@@ -101,10 +106,10 @@ def rank_program(g, core, T, topo):
     def reg(x):
         return (x[0], 0, 512) if x[0] in BANKS else (x[0], x[1], x[2])
 
-    def ap(x, rows=128):
+    def ap(x, rows=128, first=0):
         if len(x) == 4:
-            return T[x[0]][0:rows, x[1]:x[2]:x[3]]
-        return T[x[0]][0:rows, x[1]:x[2]]
+            return T[x[0]][first:first + rows, x[1]:x[2]:x[3]]
+        return T[x[0]][first:first + rows, x[1]:x[2]]
 
     def op(e, fn, reads, writes, acc=False):
         rd, wr = [reg(x) for x in reads], [reg(x) for x in writes]
@@ -158,8 +163,14 @@ def rank_program(g, core, T, topo):
         else:
             op("A", lambda: g.scalar.activation(ap(out), s, func, bias=bv, scale=sv, accum_out=ap(accum)), rd, [out, accum])
 
-    def mm(out, lhsT, rhs, start=True, stop=True, k=128, m=128):
-        op("P", lambda: g.tensor.matmul(ap(out, m), ap(lhsT, k), ap(rhs, k), start, stop), [lhsT, rhs], [out], acc=True)
+    def take(e, o, a, m):
+        if e == "A":
+            op("A", lambda: g.scalar.activation(ap(o, m), ap(a, m), AF.Identity), [a], [o])
+        else:
+            op("V", lambda: g.vector.tensor_copy(ap(o, m), ap(a, m)), [a], [o])
+
+    def mm(out, lhsT, rhs, start=True, stop=True, k=128, m=128, k0=0):
+        op("P", lambda: g.tensor.matmul(ap(out, m), ap(lhsT, k, k0), ap(rhs, k, k0), start, stop), [lhsT, rhs], [out], acc=True)
 
     def iota(out, pattern, base, cm):
         if out[0] in ("pI", "W", "W2"):
@@ -171,7 +182,7 @@ def rank_program(g, core, T, topo):
         op("G", lambda: g.affine_select(ap(out), ap(a), pattern, cmp, v, base, cm), [a], [out])
 
     def mark(out, pattern, base, v=1.0, on="zero"):
-        select(out, (on, 0, out[2]), pattern, ALU.not_equal, v, base, 1)
+        select(out, (on, 0, out[2] - out[1]), pattern, ALU.not_equal, v, base, 1)
 
     def dma(e, pairs, sem, reads, writes):
         need(e, reads, writes)
@@ -179,40 +190,25 @@ def rank_program(g, core, T, topo):
             Q[e].dma_start(o, i).then_inc(T.sem[sem], 16)
         note("D" + sem, reads, writes, sem, 16 * len(pairs))
 
-    def weave(main, filler):
-        for _ in main:
-            next(filler, None)
-
     def run(steps, n=1000):
         for _ in zip(range(n), steps):
             pass
 
-    def both(a, b):
-        while next(a, 0) is None:
-            next(b, None)
-            yield
+    def weave(main, filler):
+        for _ in main:
+            next(filler, None)
 
     engs = [e for e in topo.engines(core, nxt) if all(e in topo.engines(core, c) for c in T.cores if c != core)]
     mask = sum(1 << e for e in engs)
     sent = [0]
 
-    def ship(buf, a, b, out, oa, ob, sem):
-        need("G", [(buf, a, b)], [])
+    def ship(buf, a, out, o, sem, by=engs):
+        need("G", [(buf, a, a + 128)], [])
         rid, pid, _ = topo.addr(nxt)
-        g.remote_dma(out_ap=T[out][:, oa:ob], in_ap=T[buf][:, a:b], remote_sem=T.sem[sem], local_sem=T.sem.sent,
-                     pid=pid, routing_id=rid, dma_engine_mask=mask)
-        sent[0] += len(engs)
-        note("R", [], [(out, oa, ob)], sem, len(engs))
-
-    def ship_two(a, oa, b, ob, sem):
-        need("G", [a, b], [])
-        rid, pid, _ = topo.addr(nxt)
-        halves = [sum(1 << e for e in engs[k::2]) for k in range(2)]
-        g.remote_dma_fused([RemoteDMATransfer(dst_ids=[DstId(rid=rid, pnc=pid)], dma_engine_mask=m, remote_sem=T.sem[sem],
-                                              srcs=[ap(x)], dsts=[ap(o)]) for m, x, o in zip(halves, (a, b), (oa, ob))],
-                           local_sem=T.sem.sent)
-        sent[0] += len(engs)
-        note("R", [], [oa, ob], sem, len(engs))
+        g.remote_dma(out_ap=T[out][:, o:o + 128], in_ap=T[buf][:, a:a + 128], remote_sem=T.sem[sem], local_sem=T.sem.sent,
+                     pid=pid, routing_id=rid, dma_engine_mask=sum(1 << e for e in by))
+        sent[0] += len(by)
+        note("R", [], [(out, o, o + 128)], sem, len(by))
 
     def share_aim(land, sem):
         need("G", [(land, 4 * rank, 4 * rank + 1)], [])
@@ -228,7 +224,6 @@ def rank_program(g, core, T, topo):
 
     dma("S", [(T.aimI[:], T.aim0[:])], "l_aim", [], [("aimI", 0, 1)])
     dma("A", [(T.mgI[:], T.mg[:])], "l_mg", [], [("mgI", 0, 32)])
-    dma("S", [(T.damI[:, 384:512], T.dam[:, 384:512])], "l_dam1", [], [("damI", 384, 512)])
     for k in range(4):
         a, b = 768 * k, 768 * k + 768
         dma("A", [(T.trI[:, a:b], T.trait[:, a:b])], "l_t%d" % k, [], [("trI", a, b)])
@@ -255,103 +250,93 @@ def rank_program(g, core, T, topo):
     wp.append((T.W[d1:128:16, 8:WW], T.dam[:, 0:192]))
     wp.append((T.W[s2:128:16, 8:WW], T.sire[:, 192:384]))
     wp.append((T.W[d2:128:16, 8:WW], T.dam[:, 192:384]))
-    dma("S", [(T.sireI[:, 0:192], T.sire[:, 0:192])], "l_sire", [("trI", 0, 768)], [("sireI", 0, 192)])
-    dma("S", wp, "l_w", [], [("W", 8, WW)])
+    dma("S", wp, "l_w", [("trI", 768, 1536)], [("W", 8, WW)])
+    dma("S", [(T.sireI[:, 0:192], T.sire[:, 0:192])], "l_sire", [], [("sireI", 0, 192)])
     dma("S", [(T.damI[:, 0:192], T.dam[:, 0:192])], "l_dam0", [], [("damI", 0, 192)])
     dma("S", [(T.sireI[:, 192:384], T.sire[:, 192:384])], "l_sire2", [], [("sireI", 192, 384)])
     dma("S", [(T.damI[:, 192:384], T.dam[:, 192:384])], "l_dam2", [], [("damI", 192, 384)])
+    dma("S", [(T.damI[:, 384:512], T.dam[:, 384:512])], "l_dam1", [], [("damI", 384, 512)])
+    for c, r0, r1 in ((0, s2, d2), (16, own[0], d1)):
+        mark(("SEL", c, c + 16), [[r0 - r1, 2], [-16, 8]], -r0)
+    ts(("AI", 128, 144), ("mgI", 8, 24), 15, ALU.bitwise_and)
+    ts(("pI", 2, 3), ("pI", 1, 2), 2, ALU.logical_shift_right)
+    ts(PS2, PM, float(s2), ALU.is_equal)
+    ts(("EF", 0, 16), ("AI", 128, 144), 3071.0, ALU.mult, 128.0, ALU.add)
+    ts(PD2, PM, float(d2), ALU.is_equal)
+    ts(OWN, ("pI", 2, 3), float(rank), ALU.is_equal)
+    tt(("EG", 0, 16), ("EF", 0, 16), ("mgI", 8, 24), ALU.add)
+    ts(HOWN, ("pI", 2, 3), float(rank), ALU.is_equal, 0.5, ALU.mult)
+    ts(KB, PM, -1.0 / 32, ALU.mult, 15.0 / 32, ALU.add)
+    ts(("pos16", 128, 144), ("EG", 0, 16), 0.0625, ALU.mult)
+    ts(SGN, PD2, -1.0, ALU.mult, PS2, ALU.add)
 
-    def places():
-        v = lambda n: (n, 0, 144)
-        c = ("damI", 384, 528)
-        ts(("damI", 512, 520), ("mgI", 16, 24), 6400.0, ALU.add)
-        ts(("damI", 520, 528), ("mgI", 8, 16), 6400.0, ALU.add)
-        ts(("pI", 2, 3), ("pI", 1, 2), 2, ALU.logical_shift_right)
-        ts(PS2, PM, float(s2), ALU.is_equal)
-        ts(PD2, PM, float(d2), ALU.is_equal)
-        ts(v("EI"), c, -6400.0, ALU.add, 0.0, ALU.max)
-        ts(v("pp"), c, 6400.0, ALU.is_ge)
-        ts(v("AI"), v("EI"), 15, ALU.bitwise_and)
-        ts(v("qq"), c, 9472.0, ALU.is_ge)
-        ts(v("EF"), v("AI"), 3071.0, ALU.mult, 128.0, ALU.add)
-        yield
-        tt(v("is2"), v("pp"), v("qq"), ALU.subtract)
-        tt(v("EG"), v("EF"), v("EI"), ALU.add)
-        ts(("mn", 0, 128), ("damI", 384, 512), 6400.0, ALU.min)
-        tt(v("EM"), v("EG"), v("is2"), ALU.mult)
-        ts(("x1", 0, 128), ("damI", 384, 512), -9472.0, ALU.add, 0.0, ALU.max)
-        ts(v("pos16"), v("EM"), 0.0625, ALU.mult)
-        ts(OWN, ("pI", 2, 3), float(rank), ALU.is_equal)
-        ts(HOWN, ("pI", 2, 3), float(rank), ALU.is_equal, 0.5, ALU.mult)
-        ts(KB, PM, -1.0 / 64, ALU.mult, 15.0 / 64, ALU.add)
-        ts(SGN, PD2, -1.0, ALU.mult, PS2, ALU.add)
-        yield
-
-    def founders1(k):
-        a, b = 768 * k, 768 * k + 768
-        act(("FH", a, b), ("trI", a, b), AF.Abs, HT1, -0.5)
+    def founders(bias, width):
+        for a in range(0, 4 * width, width):
+            act(("FH", a, a + width), ("trI", a, a + width), AF.Abs, bias, -0.5)
+            yield
 
     def double(tab, a, b):
         ts((tab, Z0 + a, Z0 + b), ("FH", a, b), 2.0, ALU.mult)
 
-    def ghosts0():
-        act(("gt", 0, 128), (("trI", 0, 3072), ("mg16", 0, 8)), AF.Abs, HT1, -0.5)
-        copy(("gI", 0, 128), (("trI", 0, 3072), ("mg16", 0, 8)))
-        ship_two(("gI", 0, 128), ("trI", 3072, 3200), ("gt", 0, 128), ("FH", 3072, 3200), "a_g0")
+    def double_rest(r, tab):
+        act((tab, Z0 + VD[r - 1], Z0 + 3200), ("FH", VD[r - 1], 3200), AF.Identity, 0.0, 2.0)
 
     tab = "tabA"
-    for c, r0, r1 in ((0, s2, d2), (16, own[0], d1)):
-        select(("SEL", c, c + 16), ("zero", 0, 16), [[r0 - r1, 2], [-16, 8]], ALU.not_equal, 1.0, -r0, 1)
-    pl = places()
-    run(pl, 1)
-    founders1(0)
-    founders1(1)
-    ghosts0()
-    founders1(2)
-    founders1(3)
-    copy(("sire16", 0, 192), ("sireI", 0, 192))
-    run(pl)
-    ROW = [[-16, 9], [1000, 16]]
     mark(("ident", 0, 128), [[-1, 128]], 0)
-    mark(("idm", 0, 128), [[-1, 128]], 0, -6400.0)
-    mark(("id8", 0, 128), [[-1, 128]], 0, -float(Z0))
-    mark(("ZS", 0, 144), ROW, -s2 - 15000)
-    for b, r in (("bs1", own[0]), ("bs2", s2), ("bd2", d2)):
-        mark((b, 0, 128), [[-16, 8], [0, 16]], -r)
+    first_founders = founders(HT1, 768)
+    run(first_founders, 2)
+    act(("gt", 0, 128), (("trI", 0, 3072), ("mg16", 0, 8)), AF.Abs, HT1, -0.5)
+    ship("gt", 0, "FH", 3072, "a_g0", engs[0::2])
+    copy(("gI", 0, 128), (("trI", 0, 3072), ("mg16", 0, 8)))
+    iota(("cix", 0, 256), [[1, 16], [64, 16]], 0, 0)
+    ship("gI", 0, "trI", 3072, "a_g0t", engs[1::2])
+    run(first_founders)
+    ROW = [[-16, 9], [1000, 16]]
+    for b, v in (("idh", 0.0625), ("idl", 191.9375), ("idp", 3200.0), ("idm", -3200.0), ("idn", -1.0), ("id4", -4.0)):
+        mark((b, 0, 128), [[-1, 128]], 0, v)
 
     def to_list(pb, o0, z, flat):
         for i in range(16):
             mm((pb, o0, o0 + 64), (z, 15 - i, 143 - i), (flat, i, 1024, 16), i == 0, i == 15)
 
-    def flat(h):
-        act(("CF", 1024 * h, 1024 * h + 1024), (("W", 0, WW), ("pos16", 64 * h, 64 * h + 64)), AF.Identity)
+    def parents(a, b):
+        act(("CF", a, b), (("W", 0, WW), ("pos16", a // 16, b // 16)), AF.Identity)
 
-    SB, DB = (("pS", 0), ("pD", 0)), (("pS", 64), ("pE", 128))
-
-    def turn_flat(pb, f0, m, n):
-        for i in range(16):
+    def turn_flat(pb, f0, m, n, i0=0, i1=16):
+        for i in range(i0, i1):
             mm((pb, i, 16 * n, 16), ("CF", f0 + i, f0 + 16 * m, 16), ("SEL", 0, n), m=m)
 
-    def take(e, pb, m, n):
-        o, a = ("xt", 0, n), (pb, 0, n)
-        if e == "A":
-            op("A", lambda: g.scalar.activation(ap(o, m), ap(a, m), AF.Identity), [a], [o])
-        else:
-            op("V", lambda: g.vector.tensor_copy(ap(o, m), ap(a, m)), [a], [o])
+    def dam_terms():
+        v = lambda n: (n, 0, 128)
+        c = ("damI", 384, 512)
+        act(v("cf"), c, AF.Identity)
+        act(v("lo"), v("AI"), AF.Identity)
+        act(v("s1"), c, AF.Sign, -6399.5)
+        act(v("s2"), c, AF.Sign, -9471.5)
+        for k, (w, x) in enumerate((("idh", "cf"), ("idl", "lo"), ("idp", "s1"), ("idm", "s2"))):
+            mm(("pM", 0, 128), v(w), v(x), k == 0, k == 3)
+        act(v("r1"), c, AF.Relu, -6400.0)
+        act(v("r2"), c, AF.Relu, -9472.0)
 
-    SELF = ((("ident", "mn"), ("idm", "pp"), ("id8", "qq")), (("ident", "mn"), ("ident", "x1"), ("idm", "is2")))
+    SELF = ((("ident", "cf"), ("idn", "r1"), ("idm", "s1"), ("id4", "s2")),
+            (("ident", "cf"), ("idn", "r1"), ("ident", "r2"), ("idm", "s1"), ("idp", "s2")))
+    LISTS = (("pD", 0), ("pE", 128))
 
     def turn_back(h):
-        for r, (pb, o) in enumerate((SB[h], DB[h])):
+        pb, o0 = LISTS[h]
+        for r in range(2):
+            o = (pb, o0 + 64 * r, o0 + 64 * r + 64)
             for k, (w, x) in enumerate(SELF[r]):
-                mm((pb, o, o + 64), (w, 0, 128), (x, 64 * h, 64 * h + 64), k == 0, False)
-            mm((pb, o, o + 64), ("xt", 128 * r, 128 * r + 128), ("ident", 0, 64), False, True, k=64)
+                mm(o, (w, 0, 128), (x, 64 * h, 64 * h + 64), k == 0, False)
+            mm(o, ("xt", 128 * r, 128 * r + 128), ("ident", 64 * h, 64 * h + 64), False, True, k=64, k0=64 * h)
 
     def u_s(h):
-        ts(("US16", 64 * h, 64 * h + 64), (SB[h][0], SB[h][1], SB[h][1] + 64), float(Z0), ALU.add)
+        pb, o = LISTS[h]
+        ts(("US16", 64 * h, 64 * h + 64), (pb, o, o + 64), float(Z0 - 3204), ALU.add)
 
     def u_d(h):
-        copy(("UD16", 64 * h, 64 * h + 64), (DB[h][0], DB[h][1], DB[h][1] + 64))
+        pb, o = LISTS[h]
+        copy(("UD16", 64 * h, 64 * h + 64), (pb, o + 64, o + 128))
 
     PART = (0, 512, 1280, 2176, 3072)
     EVEN = tuple(range(0, 3073, 512))
@@ -364,101 +349,83 @@ def rank_program(g, core, T, topo):
         a, b = part[k], part[k + 1]
         tt((tab, Z0 + 3200 + a, Z0 + 3200 + b), (("FH", 0, 3200), ("dam16", a // 16, b // 16)), ("tmp", a, b), ALU.add)
 
-    MS1, MD1, MS2, MD2 = [("ms16", 8 * k, 8 * k + 8) for k in range(4)]
-
-    def ghosts1(r, tab):
-        o = 128 * r
-        copy(("gt", 128, 256), (("FH", 0, 3072), MS1))
-        tt(("gs", o, o + 128), (("FH", 0, 3200), MD1), ("gt", 128, 256), ALU.add)
-        ship("gs", o, o + 128, tab, G1, G1 + 128, "a_g1%d" % r)
-
-    def ghosts2(r, tab, between=lambda: None):
-        o = 384 + 128 * r
-        copy(("gt", 256, 384), ((tab, Z0, OWN1), MS2))
+    def ghosts1(r, tab, between):
+        o = GS1 + 128 * (r - 1)
+        copy(("gt", 128, 256), (("FH", 0, 3072), ("ms16", 0, 8)))
         between()
-        tt(("gs", o, o + 128), ((tab, Z0, E1), MD2), ("gt", 256, 384), ALU.add)
-        ship("gs", o, o + 128, tab, G2X, G2X + 128, "a_g2%d" % r)
+        tt(("gs", o, o + 128), (("FH", 0, 3200), ("ms16", 8, 16)), ("gt", 128, 256), ALU.add)
+        ship("gs", o, tab, G1, "a_g1%d" % r)
 
-    def double3(tab, a=0, b=1024):
-        act((tab, X3 + a, X3 + b), ("G3", a, b), AF.Identity, 0.0, 0.5)
+    def ghosts2(r, tab, between):
+        o, n = GS2 + 144 * (r - 1), 8 if r == 1 else 9
+        copy(("gt", 256, 256 + 16 * n), ((tab, Z0, OWN1), ("ms16", 16, 16 + n)))
+        between()
+        tt(("gs", o, o + 16 * n), ((tab, Z0, E1), ("ms16", 26, 26 + n)), ("gt", 256, 256 + 16 * n), ALU.add)
+        ship("gs", o, tab, G21 if r == 1 else G2X, "a_g2%d" % r)
 
-    def ghosts3(r, tab):
-        o = 896 + 128 * (r - 2)
-        ts(("gs", o, o + 128), (("G3", 0, 1024), ("mg16", 24, 32)), 0.5, ALU.mult)
-        ship("gs", o, o + 128, tab, G3X, G3X + 128, "a_g3%d" % r)
-
+    double(tab, 0, 768)
     copy(("CF", 2048, 2304), (("W", 0, WW), ("pos16", 128, 144)))
     turn_flat("pA", 2048, 16, 32)
+    dma("S", [(T.W[q:128:16, 8:WW], T.sire[:, 0:192]) for q in own[1:]], "l_w2", [], [("W", 8, WW)])
+    copy(("sire16", 0, 192), ("sireI", 0, 192))
     sires1(0)
-    double(tab, 0, VD[0])
-    sires1(1)
-    flat(0)
-    sires1(2)
-    sires1(3)
+    double(tab, 768, 1536)
     copy(("dam16", 0, 192), ("damI", 0, 192))
-    dams1(tab, 0)
-    take("V", "pA", 16, 512)
-    for n, (r, c) in enumerate(((2, 8), (3, 8), (0, 0), (1, 0))):
-        mm(("pC", 8 * n, 8 * n + 8), ("xt", 128 * r, 128 * r + 128), ("ident", c, c + 8), k=16)
     copy(("sire16", 192, 384), ("sireI", 192, 384))
     copy(("dam16", 192, 384), ("damI", 192, 384))
+    ts(("AI", 0, 128), ("damI", 384, 512), 15, ALU.bitwise_and)
+    copy(("c16", 0, 64), ("damI", 384, 448))
+    sires1(1)
+    take("A", ("xt", 0, 512), ("pA", 0, 512), 16)
+    for n, (r, c) in enumerate(((2, 0), (3, 0), (0, 8), (1, 8))):
+        mm(("pC", 8 * n, 8 * n + 8), ("xt", 128 * r, 128 * r + 128), ("ident", c, c + 8), k=16)
+    double(tab, 1536, VD[0])
+    sires1(2)
+    dams1(tab, 0)
     dams1(tab, 1)
-    turn_flat("pB", 0, 64, 16)
-    copy(("ms16", 0, 32), ("pC", 0, 32))
-    ghosts1(1, tab)
+    sires1(3)
+    copy(("ms16", 0, 24), ("pC", 0, 24))
+    ghosts1(1, tab, lambda: copy(("ms16", 26, 34), ("pC", 24, 32)))
     iota(("tabA", 0, Z0), [[0, Z0]], 0, 0)
     iota(("tabB", 0, Z0), [[0, Z0]], 0, 0)
-    iota(("cix", 0, 256), [[1, 16], [64, 16]], 0, 0)
     iota(("W2", 0, 900), [[0, 900]], 0, 0)
-    act((tab, Z0 + VD[0], Z0 + 3200), ("FH", VD[0], 3200), AF.Identity, 0.0, 2.0)
-    dma("S", [(T.W[q:128:16, 8:WW], T.sire[:, 0:192]) for q in own[1:]], "l_w2", [], [("W", 8, WW)])
+    double_rest(1, tab)
+    act(("dmo", 0, 16), ("dmj", 0, 16), AF.Identity, 0.0, OWN)
+    act(("dmh", 0, 16), ("dmj", 0, 16), AF.Identity, 0.0, HOWN)
+    act(("nmn", 0, 256), ("cix", 0, 256), AF.Abs, PM, -1.0 / 64)
     dams1(tab, 2)
     dams1(tab, 3)
-    ghosts2(1, tab)
+    ghosts2(1, tab, lambda: None)
     iota(("W2", 900, 3072), [[0, 2172]], 0, 0)
     dma("S", [(T.W2[r:128:16, 0:3072], T.sire[:, 192:384]) for r in own], "l_tr", [], [("W2", 0, 3072)])
+    for b, r in (("bs2", s2), ("bd2", d2), ("bs1", own[0])):
+        mark((b, 0, 128), [[-16, 8], [0, 16]], -r)
     iota(("one", 0, 128), [[0, 128]], 1, 0)
     select(("w3", 0, 128), ("one", 0, 128), [[-16, 8], [0, 16]], ALU.is_ge, 0.0, 0, 1)
     select(("blk", 0, 128), ("w3", 0, 128), [[16, 8], [0, 16]], ALU.is_ge, 0.0, 15, -1)
     iota(("zerob", 0, 144), [[0, 144]], 0, 0)
-    mark(("idb", 0, 128), [[-1, 128]], 0, on="zerob")
-    for h in range(2):
-        mark(("perm%d" % h, 0, 128), [[-1, 8], [1000, 2], [-8, 8]], -1000 * h, on="zerob")
-    mark(("ZSb", 0, 144), ROW, -s2 - 15000, on="zerob")
-    mark(("ZB", 0, 144), ROW, -d2 - 15000, on="ZSb")
     for a in range(0, 3072, 512):
         b = a + 512
         act(("tmp", a, b), ((tab, Z0, OWN1), ("sire16", 192 + a // 16, 192 + b // 16)), AF.Identity)
-        if a == 1024:
-            take("A", "pB", 64, 256)
-            turn_back(0)
-        if a == 2560:
-            u_s(0)
-        tt(("tabB", D2 + a, D2 + b), ((tab, Z0, E1), ("dam16", 192 + a // 16, 192 + b // 16)), ("tmp", a, b), ALU.add)
+        tt((tab, D2 + a, D2 + b), ((tab, Z0, E1), ("dam16", 192 + a // 16, 192 + b // 16)), ("tmp", a, b), ALU.add)
 
-    def keys_s(tab, h):
-        for a in (0, 512):
-            act(("T4", a, a + 512), ((tab, 0, E1), ("US16", 64 * h + a // 16, 64 * h + a // 16 + 32)), AF.Identity, KB)
+    def turn_keys(b):
+        for i in range(8):
+            mm(("pA" if i < 4 else "pB", 128 * (i % 4), 128 * (i % 4) + 128), (b, i, 1024, 8), ("ident", 0, 128))
 
-    def turn_keys(parts, i0=0, i1=8):
-        for i in range(i0, i1):
-            o = ("pA" if i < 4 else "pB", 128 * (i % 4), 128 * (i % 4) + 128)
-            for k, b in enumerate(parts):
-                mm(o, (b, i, 1024, 8), ("ident", 0, 128), k == 0, k == len(parts) - 1)
-
-    def rows(c0, piece=512):
+    def rows(c0, piece):
         for k, (pb, n) in enumerate((("pA", piece), ("pB", 512))):
             for a in range(0, 512, n):
                 scan(("sg", 512 * k + a, 512 * k + a + n), ("seg", 0, n), (pb, a, a + n), 0.0, ALU.mult, ALU.max)
                 yield
-        ts(("ri", 0, 64), ("sg", 15, 1024, 16), 64.0, ALU.mult)
+        ts(("ri", 0, 64), ("sg", 15, 1024, 16), 32.0, ALU.mult)
         yield
         ts(("rb", 0, 64), ("ri", 0, 64), 15, ALU.bitwise_and)
         yield
         copy(("rbf", 0, 64), ("rb", 0, 64))
         mm(("pC", 0, 128), ("rbf", 0, 64), ("idb", 0, 128), m=64)
         yield
-        op("V", lambda: g.vector.tensor_copy(ap(("rT", 0, 128), 64), ap(("pC", 0, 128), 64)), [("pC", 0, 128)], [("rT", 0, 128)])
+        take("V", ("rT", 0, 128), ("pC", 0, 128), 64)
         for h in range(2):
             mm(("pC", 128, 192), ("perm%d" % h, 0, 128), ("rT", h, 128, 2), h == 0, h == 1, k=64)
         yield
@@ -478,18 +445,16 @@ def rank_program(g, core, T, topo):
     KX, KN, RX, RN, CX, CN = [("cl", k, k + 1) for k in range(8, 14)]
     JB = [("cl", k, k + 1) for k in (2, 3)]
     BH = [("cl", 4, 5), ("cl", 5, 6)]
-    WIN2 = ("tabB", D2, D2 + 3072)
+    WIN2, WIN3 = ("tabA", D2, D2 + 3072), ("tabB", X3, X3 + 1024)
 
     def founder_a(s, n):
         b = lambda k: ("cl", n + k, n + k + 1)
         ib = lambda k: ("ci", n + k, n + k + 1)
-        ts(ib(0), s, -3200.0, ALU.add, 0.0, ALU.max)
+        ts(ib(0), s, 0.0625, ALU.mult, -15.0 / 32, ALU.add)
+        ts(b(1), s, 192.0, ALU.mult, -200.0, ALU.add)
         ts(b(0), s, 3200.0, ALU.is_lt, s, ALU.mult)
         ts(b(2), s, 3200.0, ALU.is_ge)
-        ts(ib(1), ib(0), 15, ALU.bitwise_and)
-        ts(b(1), ib(0), 0.0625, ALU.mult)
-        yield
-        ts(("sm16", n, n + 1), ib(1), 191.9375, ALU.mult, b(1), ALU.add)
+        ts(("sm16", n, n + 1), ib(0), -3071.0, ALU.mult, b(1), ALU.add)
         yield
 
     def founder_b(n):
@@ -530,8 +495,6 @@ def rank_program(g, core, T, topo):
         ts(("bR", k, k + 16), ("dmj", 0, 16), JB[r - 1], ALU.mult)
         mm(("pY", 128 + k, 144 + k), ("blk", 0, 128), ("bR", k, k + 16))
 
-    BS, BD = ("sm16", 52, 53), ("sm16", 54, 55)
-
     def best1():
         ts(("off16", 16, 32), ("i16", 0, 16), KN, ALU.subtract, 16.0, ALU.mult)
         tt(("mk", 256, 512), (WIN2, ("off16", 16, 32)), ("nmn", 0, 256), ALU.add)
@@ -545,14 +508,13 @@ def rank_program(g, core, T, topo):
         mm(("pM", 256, 272), ("bs2", 0, 128), ("bg", 0, 16))
         mm(("pM", 272, 288), ("bd2", 0, 128), ("bg", 0, 16))
         best_a(1)
-        turn_keys(("T4", "T3"), 4, 8)
-        yield
         yield
         tt(("bm", 0, 32), ("pM", 256, 288), ("dmj", 0, 32), ALU.mult)
         ts(("bT", 0, 16), ("pY", 128, 144), PS2, ALU.mult)
         scan(("bsc", 0, 32), ("seg", 0, 32), ("bm", 0, 32), 0.0, ALU.mult, ALU.add)
         yield
-        copy(("sm16", 52, 56, 2), ("bsc", 15, 32, 16))
+        copy(("ms16", 24, 35, 10), ("bsc", 15, 32, 16))
+        yield
 
     def best_lines():
         yield from founder_a(("bsc", 15, 16), 32)
@@ -573,143 +535,149 @@ def rank_program(g, core, T, topo):
     def aims(r, land):
         act(("lk", 96, 100), (land, 0, 16, 4), AF.Identity, accum=BH[r - 1])
 
-    def founders(r):
-        for k in range(4):
-            act(("FH", 800 * k, 800 * k + 800), ("trI", 800 * k, 800 * k + 800), AF.Abs, BH[r - 2], -0.5)
+    def keys1(a):
+        act(("T4", a, a + 512), ((tab, Z0, E2), ("c16", a // 16, a // 16 + 32)), AF.Identity, KB)
 
-    def aim_out(r):
-        ts(("yto", r - 1, r), BH[r - 1], 2.0, ALU.mult)
-
-    act(("dmo", 0, 16), ("dmj", 0, 16), AF.Identity, 0.0, OWN)
-    act(("dmh", 0, 16), ("dmj", 0, 16), AF.Identity, 0.0, HOWN)
-    act(("nmn", 0, 256), ("cix", 0, 256), AF.Abs, PM, -1.0 / 64)
+    dam_terms()
     act(("nmx", 0, 256), ("nmn", 0, 256), AF.Identity, 15.0 / 64, -1.0)
-    keys_s(tab, 0)
-    run(running(0, "tabB", D2, 1536, ALU.max, 1536))
-    u_d(0)
-    least = running(1536, "tabB", D2, 1536, ALU.min, 128)
-    weave(chain1("land1"), least)
+    keys1(0)
+    run(running(0, tab, D2, 1536, ALU.max, 1536))
+    least = running(1536, tab, D2, 1536, ALU.min, 128)
+    first_chain = chain1("land1")
+    run(first_chain, 1)
+    run(least, 1)
+    ts(("pos16", 0, 128), ("pM", 0, 128), -392.0 - 6400.0, ALU.add)
+    keys1(512)
+    turn_keys("T4")
+    parents(0, 1024)
+    weave(first_chain, least)
     share_aim("land1", "a_aim1")
+    mark(("idb", 0, 128), [[-1, 128]], 0, on="zerob")
+    for h in range(2):
+        mark(("perm%d" % h, 0, 128), [[-1, 8], [1000, 2], [-8, 8]], -1000 * h, on="zerob")
+    mark(("ZS", 0, 144), ROW, -s2 - 15000)
+    mark(("ZSb", 0, 144), ROW, -s2 - 15000, on="zerob")
+    mark(("ZB", 0, 144), ROW, -d2 - 15000, on="ZSb")
     run(least)
-    act(("T3", 0, 1024), ((tab, Z0, X3), ("UD16", 0, 64)), AF.Identity)
-    turn_keys(("T4", "T3"), 0, 4)
-    flat(1)
+    parents(1024, 1536)
     count(1536, 1536, 8, KN)
+    parents(1536, 2048)
+    turn_flat("pS", 0, 128, 16, 0, 4)
     aims(1, "land1")
-    founders(2)
-    first_best, first_rows, lines = best1(), rows(0, 128), best_lines()
-    doubling = (double("tabB", a, a + 200) for a in range(0, 800, 200))
-    run(both(first_best, first_rows), 4)
-    weave(first_best, doubling)
-    run(both(doubling, lines))
+    run(founders(BH[0], 800))
+    lines = best_lines()
+    step = {"best": best1(), "rows": rows(0, 256), "line": lines,
+            "double": (double("tabB", a, a + 200) for a in range(0, 800, 200))}
+    for name in "best rows best rows best rows rows best rows best line rows line rows".split():
+        run(step[name], 1)
+    turn_flat("pS", 0, 128, 16, 4, 16)
+    weave(step["double"], lines)
+    run(step["rows"])
 
-    def generation1(r, tab, done, part, filler, steps):
-        nv = VD[r - 1]
-        for a in range(done, nv, 800):
+    def generation1(r, tab, done, part, filler, after, last):
+        for a in range(done, VD[r - 1], 800):
             double(tab, a, a + 800)
-        ghosts1(r, tab)
+        ghosts1(r, tab, lambda: run(filler, 1))
         for k in range(len(part) - 1):
-            run(filler, steps[k])
             sires1(k, part)
             dams1(tab, k, part)
-            if r == 2 and k == 2:
-                turn_flat("pA", 1024, 64, 16)
-        act((tab, Z0 + nv, Z0 + 3200), ("FH", nv, 3200), AF.Identity, 0.0, 2.0)
-        ghosts2(r, tab, lambda: copy(("ub1", 0, 16), ((tab, Z0, OWN1), BS)))
-        tt(("Ub", 0, 16), ((tab, Z0, E1), BD), ("ub1", 0, 16), ALU.add)
+            if k in after:
+                after[k]()
+        double_rest(r, tab)
+        ghosts2(r, tab, last)
 
-    def generation3(tab, k):
-        a, b = 512 * k, 512 * k + 512
+    def generation3(r, tab, k):
+        a, b, o = 512 * k, 512 * k + 512, GS2 + 144 * (r - 1) + 128
         act(("tmp2", a, b), ((tab, 0, E1), ("US16", 32 * k, 32 * k + 32)), AF.Identity)
-        tt(("T3", a, b), (("Ub", 0, 16), ("row16", 32 * k, 32 * k + 32)), ("tmp2", a, b), ALU.add)
+        tt(("T3", a, b), (("gs", o, o + 16), ("row16", 32 * k, 32 * k + 32)), ("tmp2", a, b), ALU.add)
 
-    def generation3_end(tab, k):
+    def generation3_end(tab, k, out, o):
         a, b = 512 * k, 512 * k + 512
-        tt(("G3", a, b), ((tab, Z0, X3), ("UD16", 32 * k, 32 * k + 32)), ("T3", a, b), ALU.add)
+        tt((out, o + a, o + b), ((tab, Z0, X3), ("UD16", 32 * k, 32 * k + 32)), ("T3", a, b), ALU.add)
 
     def extreme3(o, K, U2, n, dm, cmp, out):
         sign = 2.0 if cmp == ALU.is_lt else -2.0
         ts(("sm16", n, n + 1), K, sign, ALU.mult)
         ts(U2, K, sign, ALU.mult)
-        tt(("lk", n + 24, n + 40), (("G3", 0, 1024), ("sm16", n, n + 1)), dm, ALU.mult)
+        tt(("lk", n + 24, n + 40), (WIN3, ("sm16", n, n + 1)), dm, ALU.mult)
         yield
         red(("cl", n, n + 1), ("lk", n + 24, n + 40))
         yield
         ts(out, ("cl", n, n + 1), ("tmp", o + 511, o + 512), cmp, U2, ALU.add)
         yield
 
+    def both_lists():
+        take("V", ("xt", 0, 256), ("pS", 0, 256), 128)
+        turn_back(0)
+        turn_back(1)
+
     tab = "tabB"
-    generation1(2, tab, 800, PART, both(first_rows, lines), (2, 2, 1, 1))
-    generation3(tab, 0)
-    generation3(tab, 1)
-    take("A", "pA", 64, 256)
-    turn_back(1)
+    generation1(2, tab, 800, PART, lines, {0: lambda: run(lines), 1: both_lists, 3: lambda: u_s(0)}, lambda: u_d(0))
+    generation3(2, tab, 0)
+    generation3(2, tab, 1)
     act(("sy", 0, 1024), (("yt16", 0, 16), ("row16", 0, 64)), AF.Identity)
-    generation3_end(tab, 0)
-    double3(tab, 0, 512)
-    generation3_end(tab, 1)
-    run(running(0, "G3", 0, 512, ALU.max, 512))
-    count(0, 512, 1, KX)
-    ghosts3(2, tab)
     u_s(1)
-    run(running(512, "G3", 0, 512, ALU.min, 512))
-    halves = (ts((tab, X3 + a, X3 + a + 128), ("G3", a, a + 128), 0.5, ALU.mult) for a in range(512, 1024, 128))
-    weave(extreme3(0, KX, RX, 40, ("dmo", 0, 16), ALU.is_lt, ("sm16", 42, 43)), halves)
+    act(("T4", 0, 1024), ((tab, 0, E1), ("US16", 64, 128)), AF.Identity, KB)
+    generation3_end(tab, 0, tab, X3)
+    generation3_end(tab, 1, tab, X3)
+    run(running(0, tab, X3, 512, ALU.max, 512))
+    count(0, 512, 1, KX)
+    copy(("gs", GS3, GS3 + 128), (WIN3, ("mg16", 24, 32)))
+    ship("gs", GS3, tab, G3X, "a_g32")
+    u_d(1)
+    run(running(512, tab, X3, 512, ALU.min, 512))
+    run(extreme3(0, KX, RX, 40, ("dmo", 0, 16), ALU.is_lt, ("sm16", 42, 43)))
     tt(("lk", 48, 64), (("sy", 0, 1024), ("sm16", 42, 43)), ("dmh", 0, 16), ALU.mult)
-    run(halves)
     red(("land2", 4 * rank, 4 * rank + 1), ("lk", 48, 64))
     share_aim("land2", "a_aim2")
     count(512, 512, 1, KN)
-    keys_s(tab, 1)
-    run(extreme3(512, KN, RN, 56, ("dmj", 0, 16), ALU.is_gt, JB[1]))
+    keys = (tt(("key", a, a + 256), ((tab, Z0, TW), ("UD16", 64 + a // 16, 80 + a // 16)), ("T4", a, a + 256), ALU.add)
+            for a in range(0, 1024, 256))
+    weave(extreme3(512, KN, RN, 56, ("dmj", 0, 16), ALU.is_gt, JB[1]), keys)
     best_a(2)
-    copy(("sm16", 58, 59), JB[1])
-    u_d(1)
-    for a in (0, 512):
-        tt(("key", a, a + 512), ((tab, Z0, TW), ("UD16", 64 + a // 16, 96 + a // 16)), ("T4", a, a + 512), ALU.add)
-    turn_keys(("key",))
+    copy(("mg16", 32, 33), JB[1])
+    run(keys)
+    turn_keys("key")
     to_list("pE", 0, "ZS", "sy")
     aims(2, "land2")
-    founders(3)
-
-    tab = "tabA"
-    last_rows = rows(64)
-    generation1(3, tab, 0, EVEN, last_rows, (1, 0, 0, 0, 0, 0))
-    run(last_rows, 1)
+    run(founders(BH[1], 800))
     ts(("bH", 0, 16), ("pY", 144, 160), SGN, ALU.mult)
     ts(("bR", 0, 16), ("pY", 144, 160), PD2, ALU.mult)
-    run(last_rows, 1)
+    for r in range(2):
+        ts(("yto", r, r + 1), BH[r], 2.0, ALU.mult)
     tt(("bT", 16, 32), ("bR", 0, 16), ("bH", 0, 16), ALU.add)
+    dma("S", [(T.yt[:], T.yto[:])], "o_yt", [("yto", 0, 2)], [])
+
+    tab = "tabA"
+    last_rows = rows(64, 512)
+    generation1(3, tab, 0, EVEN, last_rows, {}, lambda: run(last_rows, 1))
     run(last_rows, 1)
     ts(("yso", 0, 64), ("pE", 0, 64), 6400.0, ALU.add)
-    aim_out(1)
-    aim_out(2)
-    dma("S", [(T.yt[:], T.yto[:])], "o_yt", [("yto", 0, 2)], [])
-    run(last_rows, 1)
-    generation3(tab, 0)
-    run(last_rows, 1)
-    generation3(tab, 1)
-    run(last_rows, 1)
+    run(last_rows, 2)
+    for k in range(2):
+        generation3(3, tab, k)
+        run(last_rows, 1)
     act(("T4", 0, 1024), ((tab, 0, E1), ("US16", 64, 128)), AF.Identity)
     act(("sf", 0, 1024), (("bT", 16, 32), ("row16", 64, 128)), AF.Identity)
     to_list("pE", 64, "ZB", "sf")
     for k in range(2):
         a, b = 512 * k, 512 * k + 512
-        generation3_end(tab, k)
+        generation3_end(tab, k, "G3", 0)
         act(("yo", a, b), ("G3", a, b), AF.Identity, 65535.0, -0.25)
-        dma("S", [(T.yf[:, a:b], T.yo[:, a:b])], "o_f3" + "ab"[k], [("yo", a, b)], [])
-    ghosts3(3, tab)
-    double3(tab)
-    ts(("HB", 0, 16), (("G3", 0, 1024), ("sm16", 58, 59)), 0.5, ALU.mult)
-    tt(("T3", 0, 1024), (("HB", 0, 16), ("row16", 64, 128)), ("T4", 0, 1024), ALU.add)
-    ts(("yso", 64, 128), ("pE", 64, 128), 9600.0, ALU.add)
+        dma("S", [(T.yf[:, a:b], T.yo[:, a:b])], "o_f3%d" % k, [("yo", a, b)], [])
+    o = GS3 + 144
+    ts(("gs", o, o + 144), (("G3", 0, 1024), ("mg16", 24, 33)), 0.5, ALU.mult)
+    ship("gs", o, tab, G3X, "a_g33")
+    act((tab, X3, X3 + 1024), ("G3", 0, 1024), AF.Identity, 0.0, 0.5)
+    tt(("T3", 0, 1024), (("gs", o + 128, o + 144), ("row16", 64, 128)), ("T4", 0, 1024), ALU.add)
+    act(("yso", 64, 128), ("pE", 64, 128), AF.Identity, 9600.0)
     dma("S", [(T.ys[:], T.yso[:])], "o_ys", [("yso", 0, 128)], [])
     b = 0
-    for k, n in enumerate((384, 384, 256)):
+    for k, n in enumerate((320, 320, 192, 192)):
         a, b = b, b + n
         tt(("key", a, b), ((tab, Z0, TW), ("UD16", 64 + a // 16, 64 + b // 16)), ("T3", a, b), ALU.add)
         act(("yo", 1024 + a, 1024 + b), ("key", a, b), AF.Identity, 65535.0, -0.25)
-        dma("S", [(T.yf[:, 1024 + a:1024 + b], T.yo[:, 1024 + a:1024 + b])], "o_f4%s" % "abc"[k], [("yo", 1024 + a, 1024 + b)], [])
+        dma("S", [(T.yf[:, 1024 + a:1024 + b], T.yo[:, 1024 + a:1024 + b])], "o_f4%d" % k, [("yo", 1024 + a, 1024 + b)], [])
 
     for s in sorted(total):
         if known["G"].get(s, 0) < total[s]:

from concourse.bass import DstId, RemoteDMATransfer
from concourse.mybir import AluOpType, AxisListType, ActivationFunctionType

ALU = AluOpType
AF = ActivationFunctionType
F32, I32, U16, B16 = "float32", "int32", "uint16", "bfloat16"
Z0 = 8
OWN1 = Z0 + 6272
G1 = Z0 + 6272
E1 = Z0 + 6400
D2 = Z0 + 6400
G21 = Z0 + 9472
E2 = Z0 + 9600
G2X = Z0 + 6400
X3 = Z0 + 6528
G3X = Z0 + 7552
TW = Z0 + 7680
WW = 3080
WV = 2300
VD = (1920, 1600, 2400)
GS1, GS2, GS3 = 0, 384, 816


def _sb(n, d=F32):
    return ("sbuf", [128, n], d)


SCRATCH = {
    "sireI": _sb(384, I32), "damI": _sb(512, I32), "mgI": _sb(32, I32), "aimI": _sb(1, I32),
    "trI": _sb(3200, I32), "W": _sb(WW, I32), "W2": _sb(3072, I32), "gI": _sb(128, I32),
    "FH": _sb(3200), "tabA": _sb(E2), "tabB": _sb(TW),
    "tmp": _sb(3072), "tmp2": _sb(1024), "CF": _sb(2304),
    "T3": _sb(1024), "T4": _sb(1024), "key": _sb(1024), "G3": _sb(1024), "sg": _sb(1024),
    "yo": _sb(2048), "sf": _sb(1024, B16), "sy": _sb(1024), "seg": _sb(512),
    "io": _sb(256), "dmj": _sb(32), "mk": _sb(512), "xt": _sb(512), "junk": _sb(512, B16),
    "blk": _sb(128), "bs1": _sb(128), "bs2": _sb(128), "bd2": _sb(128), "SEL": _sb(32),
    "ident": _sb(128), "idm": _sb(128), "id4": _sb(128), "idn": _sb(128), "idp": _sb(128), "idl": _sb(128), "idh": _sb(128),
    "ZS": _sb(144), "zero": _sb(144), "one": _sb(128),
    "w1": _sb(32), "w3": _sb(128), "cix": _sb(256), "nmx": _sb(256), "nmn": _sb(256),
    "zerob": _sb(144, B16), "idb": _sb(128, B16), "perm0": _sb(128, B16), "perm1": _sb(128, B16), "rT": _sb(128, B16),
    "ZSb": _sb(144, B16), "ZB": _sb(144, B16), "bH": _sb(16, B16),
    "pI": _sb(8, I32), "cc": _sb(32), "dmo": _sb(16), "dmh": _sb(16),
    "sire16": _sb(384, U16), "dam16": _sb(384, U16), "mg16": _sb(34, U16), "ms16": _sb(40, U16), "c16": _sb(64, U16),
    "pos16": _sb(144, U16), "US16": _sb(128, U16), "UD16": _sb(128, U16), "row16": _sb(128, U16), "sm16": _sb(64, U16),
    "AI": _sb(144, I32), "EF": _sb(16), "EG": _sb(16),
    "cf": _sb(128), "lo": _sb(128), "s1": _sb(128), "s2": _sb(128), "r1": _sb(128), "r2": _sb(128),
    "gs": _sb(1104), "gt": _sb(400), "ri": _sb(64, I32), "rb": _sb(64, I32), "rbf": _sb(64, B16),
    "bT": _sb(32), "bR": _sb(32), "bg": _sb(16), "bm": _sb(32), "bsc": _sb(32),
    "cl": _sb(64), "ci": _sb(64, I32), "lk": _sb(128), "land1": _sb(16), "land2": _sb(16),
    "off16": _sb(32, U16), "i16": _sb(16), "bg2": _sb(16), "bm2": _sb(16), "yt16": _sb(32),
    "yso": _sb(128), "yto": _sb(2),
}
BANKS = ("pC", "pS", "pD", "pM", "pY", "pA", "pB", "pE")
for _b in BANKS:
    SCRATCH[_b] = ("psum", [128, 512], F32)
SEMAPHORES = ["qV", "qA", "qP", "qG", "sent", "l_sire", "l_sire2", "l_dam0", "l_dam1", "l_dam2", "l_mg", "l_aim",
              "l_t0", "l_t1", "l_t2", "l_t3", "l_w", "l_w2", "l_tr", "o_ys", "o_yt", "o_f30", "o_f31",
              "o_f40", "o_f41", "o_f42", "o_f43",
              "a_g0", "a_g0t", "a_g11", "a_g12", "a_g13", "a_g21", "a_g22", "a_g23", "a_g32", "a_g33", "a_aim1", "a_aim2"]


def rank_program(g, core, T, topo):
    rank = T.rank_of(core)
    if rank is None:
        return
    N = len(T.cores)
    nxt = T.cores[(rank + 1) % N]
    Q = {"V": g.vector, "A": g.scalar, "P": g.tensor, "G": g, "S": g.sync}
    SEM = {"V": "qV", "A": "qA", "P": "qP", "G": "qG"}
    cnt = {"V": 0, "A": 0, "P": 0, "G": 0}
    known = {e: {} for e in Q}
    recs = {}
    clocks = {}
    total = {}

    def need(e, reads, writes, acc=False):
        req = {}
        for kind, regs in ((0, reads), (1, writes)):
            for b, c0, c1 in regs:
                for o0, o1, ow, sem, val, oe in recs.get(b, []):
                    if o1 <= c0 or o0 >= c1 or (kind == 0 and not ow) or (oe == e and acc):
                        continue
                    req[sem] = max(req.get(sem, 0), val)
        live = {s: v for s, v in req.items() if known[e].get(s, 0) < v}
        for s in sorted(live):
            if any(o != s and clocks.get((o, live[o]), {}).get(s, 0) >= live[s] for o in live):
                continue
            Q[e].wait_ge(T.sem[s], live[s])
        for s, v in live.items():
            known[e][s] = max(known[e].get(s, 0), v)
            for o, w in clocks.get((s, v), {}).items():
                known[e][o] = max(known[e].get(o, 0), w)

    def note(e, reads, writes, sem, val):
        clocks[(sem, val)] = dict(known[e]) if e in known else {}
        total[sem] = val
        for b, c0, c1 in writes:
            keep = [r for r in recs.get(b, []) if not (c0 <= r[0] and r[1] <= c1)]
            keep.append((c0, c1, True, sem, val, e))
            recs[b] = keep
        for b, c0, c1 in reads:
            keep = [r for r in recs.get(b, []) if not (not r[2] and r[5] == e and c0 <= r[0] and r[1] <= c1)]
            keep.append((c0, c1, False, sem, val, e))
            recs[b] = keep

    def reg(x):
        return (x[0], 0, 512) if x[0] in BANKS else (x[0], x[1], x[2])

    def ap(x, rows=128, first=0):
        if len(x) == 4:
            return T[x[0]][first:first + rows, x[1]:x[2]:x[3]]
        return T[x[0]][first:first + rows, x[1]:x[2]]

    def op(e, fn, reads, writes, acc=False):
        rd, wr = [reg(x) for x in reads], [reg(x) for x in writes]
        wr = wr + [r for r in rd if r[0] in BANKS]
        need(e, rd, wr, acc)
        cnt[e] += 1
        fn().then_inc(T.sem[SEM[e]], 1)
        note(e, rd, wr, SEM[e], cnt[e])

    def src(x):
        if len(x) == 2:
            return ap(x[0]).indirect(ap(x[1])), [x[0], x[1]]
        return ap(x), [x]

    def copy(out, a):
        s, rd = src(a)
        op("V", lambda: g.vector.tensor_copy(ap(out), s), rd, [out])

    def tt(out, a, b, alu):
        s, rd = src(a)
        op("V", lambda: g.vector.tensor_tensor(ap(out), s, ap(b), alu), rd + [b], [out])

    def ts(out, a, s1, o1, s2=None, o2=None):
        s, rd = src(a)
        v1 = ap(s1) if isinstance(s1, tuple) else s1
        v2 = ap(s2) if isinstance(s2, tuple) else s2
        rd = rd + [x for x in (s1, s2) if isinstance(x, tuple)]
        if o2 is None:
            op("V", lambda: g.vector.tensor_scalar(ap(out), s, v1, None, o1), rd, [out])
        else:
            op("V", lambda: g.vector.tensor_scalar(ap(out), s, v1, v2, o1, o2), rd, [out])

    def red(out, a, alu=ALU.add):
        op("V", lambda: g.vector.tensor_reduce(ap(out), ap(a), AxisListType.X, alu), [a], [out])

    def fill(a, v):
        op("V", lambda: g.vector.memset(ap(a), v), [], [a])

    def scan(out, d0, d1, init, o0, o1):
        iv = ap(init) if isinstance(init, tuple) else init
        rd = [d0, d1] + ([init] if isinstance(init, tuple) else [])
        op("V", lambda: g.vector.tensor_tensor_scan(ap(out), ap(d0), ap(d1), iv, o0, o1), rd, [out])

    def act(out, a, func, bias=0.0, scale=1.0, accum=None):
        s, rd = src(a)
        bv = ap(bias) if isinstance(bias, tuple) else bias
        sv = ap(scale) if isinstance(scale, tuple) else scale
        rd = rd + [x for x in (bias, scale) if isinstance(x, tuple)]
        if accum is None:
            op("A", lambda: g.scalar.activation(ap(out), s, func, bias=bv, scale=sv), rd, [out])
        else:
            op("A", lambda: g.scalar.activation(ap(out), s, func, bias=bv, scale=sv, accum_out=ap(accum)), rd, [out, accum])

    def take(e, o, a, m):
        if e == "A":
            op("A", lambda: g.scalar.activation(ap(o, m), ap(a, m), AF.Identity), [a], [o])
        else:
            op("V", lambda: g.vector.tensor_copy(ap(o, m), ap(a, m)), [a], [o])

    def mm(out, lhsT, rhs, start=True, stop=True, k=128, m=128, k0=0):
        op("P", lambda: g.tensor.matmul(ap(out, m), ap(lhsT, k, k0), ap(rhs, k, k0), start, stop), [lhsT, rhs], [out], acc=True)

    def iota(out, pattern, base, cm):
        if out[0] in ("pI", "W", "W2"):
            op("G", lambda: g.iota(ap(out), pattern, base, cm), [], [out])
        else:
            op("G", lambda: g.iota(ap(out), pattern, base, cm, allow_small_or_imprecise_dtypes=True), [], [out])

    def select(out, a, pattern, cmp, v, base, cm):
        op("G", lambda: g.affine_select(ap(out), ap(a), pattern, cmp, v, base, cm), [a], [out])

    def mark(out, pattern, base, v=1.0, on="zero"):
        select(out, (on, 0, out[2] - out[1]), pattern, ALU.not_equal, v, base, 1)

    def dma(e, pairs, sem, reads, writes):
        need(e, reads, writes)
        for o, i in pairs:
            Q[e].dma_start(o, i).then_inc(T.sem[sem], 16)
        note("D" + sem, reads, writes, sem, 16 * len(pairs))

    def run(steps, n=1000):
        for _ in zip(range(n), steps):
            pass

    def weave(main, filler):
        for _ in main:
            next(filler, None)

    engs = [e for e in topo.engines(core, nxt) if all(e in topo.engines(core, c) for c in T.cores if c != core)]
    mask = sum(1 << e for e in engs)
    sent = [0]

    def ship(buf, a, out, o, sem, by=engs):
        need("G", [(buf, a, a + 128)], [])
        rid, pid, _ = topo.addr(nxt)
        g.remote_dma(out_ap=T[out][:, o:o + 128], in_ap=T[buf][:, a:a + 128], remote_sem=T.sem[sem], local_sem=T.sem.sent,
                     pid=pid, routing_id=rid, dma_engine_mask=sum(1 << e for e in by))
        sent[0] += len(by)
        note("R", [], [(out, o, o + 128)], sem, len(by))

    def share_aim(land, sem):
        need("G", [(land, 4 * rank, 4 * rank + 1)], [])
        others = [c for c in T.cores if c != core]
        ids = [DstId(rid=topo.addr(c)[0], pnc=topo.addr(c)[1]) for c in others]
        a = T[land][:, 4 * rank:4 * rank + 1]
        g.remote_dma_fused([RemoteDMATransfer(dst_ids=ids, dma_engine_mask=mask, remote_sem=T.sem[sem], srcs=[a],
                                              dsts=[a for c in others])], local_sem=T.sem.sent)
        sent[0] += len(engs)
        for k in range(N):
            if k != rank:
                note("R", [], [(land, 4 * k, 4 * k + 1)], sem, len(engs) * (N - 1))

    dma("S", [(T.aimI[:], T.aim0[:])], "l_aim", [], [("aimI", 0, 1)])
    dma("A", [(T.mgI[:], T.mg[:])], "l_mg", [], [("mgI", 0, 32)])
    for k in range(4):
        a, b = 768 * k, 768 * k + 768
        dma("A", [(T.trI[:, a:b], T.trait[:, a:b])], "l_t%d" % k, [], [("trI", a, b)])
    PM, OWN, KB, PS2, PD2, HOWN, HT1, SGN = [("cc", k, k + 1) for k in range(8)]
    iota(("pI", 0, 1), [[0, 1]], 0, 1)
    iota(("io", 0, 256), [[0, 16], [1, 16]], 0, 0)
    iota(("W", WV, WW), [[0, WW - WV]], 0, 0)
    iota(("zero", 0, 144), [[0, 144]], 0, 0)
    ts(("pI", 1, 2), ("pI", 0, 1), 15, ALU.bitwise_and)
    fill(("W", 0, 200), 0)
    copy(PM, ("pI", 1, 2))
    fill(("W", 200, 1300), 0)
    ts(HT1, ("aimI", 0, 1), 0.5, ALU.mult)
    copy(("mg16", 0, 32), ("mgI", 0, 32))
    fill(("W", 1300, WV), 0)
    act(("w1", 0, 32), ("io", 0, 32), AF.Abs, PM, -1.0)
    act(("seg", 0, 256), ("io", 0, 256), AF.Sign)
    act(("dmj", 0, 32), ("w1", 0, 32), AF.Relu, 1.0, -1.0)
    act(("seg", 256, 512), ("io", 0, 256), AF.Sign)
    act(("i16", 0, 16), ("io", 0, 16), AF.Identity, 0.0, 0.0625)
    own = [4 * rank + k for k in range(4)]
    d1, s2, d2 = [(4 * rank + 4 + k) % 16 for k in range(3)]
    wp = [(T.W[own[0]:128:16, 8:WW], T.sire[:, 0:192])]
    wp.append((T.W[d1:128:16, 8:WW], T.dam[:, 0:192]))
    wp.append((T.W[s2:128:16, 8:WW], T.sire[:, 192:384]))
    wp.append((T.W[d2:128:16, 8:WW], T.dam[:, 192:384]))
    dma("S", wp, "l_w", [("trI", 768, 1536)], [("W", 8, WW)])
    dma("S", [(T.sireI[:, 0:192], T.sire[:, 0:192])], "l_sire", [], [("sireI", 0, 192)])
    dma("S", [(T.damI[:, 0:192], T.dam[:, 0:192])], "l_dam0", [], [("damI", 0, 192)])
    dma("S", [(T.sireI[:, 192:384], T.sire[:, 192:384])], "l_sire2", [], [("sireI", 192, 384)])
    dma("S", [(T.damI[:, 192:384], T.dam[:, 192:384])], "l_dam2", [], [("damI", 192, 384)])
    dma("S", [(T.damI[:, 384:512], T.dam[:, 384:512])], "l_dam1", [], [("damI", 384, 512)])
    for c, r0, r1 in ((0, s2, d2), (16, own[0], d1)):
        mark(("SEL", c, c + 16), [[r0 - r1, 2], [-16, 8]], -r0)
    ts(("AI", 128, 144), ("mgI", 8, 24), 15, ALU.bitwise_and)
    ts(("pI", 2, 3), ("pI", 1, 2), 2, ALU.logical_shift_right)
    ts(PS2, PM, float(s2), ALU.is_equal)
    ts(("EF", 0, 16), ("AI", 128, 144), 3071.0, ALU.mult, 128.0, ALU.add)
    ts(PD2, PM, float(d2), ALU.is_equal)
    ts(OWN, ("pI", 2, 3), float(rank), ALU.is_equal)
    tt(("EG", 0, 16), ("EF", 0, 16), ("mgI", 8, 24), ALU.add)
    ts(HOWN, ("pI", 2, 3), float(rank), ALU.is_equal, 0.5, ALU.mult)
    ts(KB, PM, -1.0 / 32, ALU.mult, 15.0 / 32, ALU.add)
    ts(("pos16", 128, 144), ("EG", 0, 16), 0.0625, ALU.mult)
    ts(SGN, PD2, -1.0, ALU.mult, PS2, ALU.add)

    def founders(bias, width):
        for a in range(0, 4 * width, width):
            act(("FH", a, a + width), ("trI", a, a + width), AF.Abs, bias, -0.5)
            yield

    def double(tab, a, b):
        ts((tab, Z0 + a, Z0 + b), ("FH", a, b), 2.0, ALU.mult)

    def double_rest(r, tab):
        act((tab, Z0 + VD[r - 1], Z0 + 3200), ("FH", VD[r - 1], 3200), AF.Identity, 0.0, 2.0)

    tab = "tabA"
    mark(("ident", 0, 128), [[-1, 128]], 0)
    first_founders = founders(HT1, 768)
    run(first_founders, 2)
    act(("gt", 0, 128), (("trI", 0, 3072), ("mg16", 0, 8)), AF.Abs, HT1, -0.5)
    ship("gt", 0, "FH", 3072, "a_g0", engs[0::2])
    copy(("gI", 0, 128), (("trI", 0, 3072), ("mg16", 0, 8)))
    iota(("cix", 0, 256), [[1, 16], [64, 16]], 0, 0)
    ship("gI", 0, "trI", 3072, "a_g0t", engs[1::2])
    run(first_founders)
    ROW = [[-16, 9], [1000, 16]]
    for b, v in (("idh", 0.0625), ("idl", 191.9375), ("idp", 3200.0), ("idm", -3200.0), ("idn", -1.0), ("id4", -4.0)):
        mark((b, 0, 128), [[-1, 128]], 0, v)

    def to_list(pb, o0, z, flat):
        for i in range(16):
            mm((pb, o0, o0 + 64), (z, 15 - i, 143 - i), (flat, i, 1024, 16), i == 0, i == 15)

    def parents(a, b):
        act(("CF", a, b), (("W", 0, WW), ("pos16", a // 16, b // 16)), AF.Identity)

    def turn_flat(pb, f0, m, n, i0=0, i1=16):
        for i in range(i0, i1):
            mm((pb, i, 16 * n, 16), ("CF", f0 + i, f0 + 16 * m, 16), ("SEL", 0, n), m=m)

    def dam_terms():
        v = lambda n: (n, 0, 128)
        c = ("damI", 384, 512)
        act(v("cf"), c, AF.Identity)
        act(v("lo"), v("AI"), AF.Identity)
        act(v("s1"), c, AF.Sign, -6399.5)
        act(v("s2"), c, AF.Sign, -9471.5)
        for k, (w, x) in enumerate((("idh", "cf"), ("idl", "lo"), ("idp", "s1"), ("idm", "s2"))):
            mm(("pM", 0, 128), v(w), v(x), k == 0, k == 3)
        act(v("r1"), c, AF.Relu, -6400.0)
        act(v("r2"), c, AF.Relu, -9472.0)

    SELF = ((("ident", "cf"), ("idn", "r1"), ("idm", "s1"), ("id4", "s2")),
            (("ident", "cf"), ("idn", "r1"), ("ident", "r2"), ("idm", "s1"), ("idp", "s2")))
    LISTS = (("pD", 0), ("pE", 128))

    def turn_back(h):
        pb, o0 = LISTS[h]
        for r in range(2):
            o = (pb, o0 + 64 * r, o0 + 64 * r + 64)
            for k, (w, x) in enumerate(SELF[r]):
                mm(o, (w, 0, 128), (x, 64 * h, 64 * h + 64), k == 0, False)
            mm(o, ("xt", 128 * r, 128 * r + 128), ("ident", 64 * h, 64 * h + 64), False, True, k=64, k0=64 * h)

    def u_s(h):
        pb, o = LISTS[h]
        ts(("US16", 64 * h, 64 * h + 64), (pb, o, o + 64), float(Z0 - 3204), ALU.add)

    def u_d(h):
        pb, o = LISTS[h]
        copy(("UD16", 64 * h, 64 * h + 64), (pb, o + 64, o + 128))

    PART = (0, 512, 1280, 2176, 3072)
    EVEN = tuple(range(0, 3073, 512))

    def sires1(k, part=PART):
        a, b = part[k], part[k + 1]
        act(("tmp", a, b), (("FH", 0, 3072), ("sire16", a // 16, b // 16)), AF.Identity)

    def dams1(tab, k, part=PART):
        a, b = part[k], part[k + 1]
        tt((tab, Z0 + 3200 + a, Z0 + 3200 + b), (("FH", 0, 3200), ("dam16", a // 16, b // 16)), ("tmp", a, b), ALU.add)

    def ghosts1(r, tab, between):
        o = GS1 + 128 * (r - 1)
        copy(("gt", 128, 256), (("FH", 0, 3072), ("ms16", 0, 8)))
        between()
        tt(("gs", o, o + 128), (("FH", 0, 3200), ("ms16", 8, 16)), ("gt", 128, 256), ALU.add)
        ship("gs", o, tab, G1, "a_g1%d" % r)

    def ghosts2(r, tab, between):
        o, n = GS2 + 144 * (r - 1), 8 if r == 1 else 9
        copy(("gt", 256, 256 + 16 * n), ((tab, Z0, OWN1), ("ms16", 16, 16 + n)))
        between()
        tt(("gs", o, o + 16 * n), ((tab, Z0, E1), ("ms16", 26, 26 + n)), ("gt", 256, 256 + 16 * n), ALU.add)
        ship("gs", o, tab, G21 if r == 1 else G2X, "a_g2%d" % r)

    double(tab, 0, 768)
    copy(("CF", 2048, 2304), (("W", 0, WW), ("pos16", 128, 144)))
    turn_flat("pA", 2048, 16, 32)
    dma("S", [(T.W[q:128:16, 8:WW], T.sire[:, 0:192]) for q in own[1:]], "l_w2", [], [("W", 8, WW)])
    copy(("sire16", 0, 192), ("sireI", 0, 192))
    sires1(0)
    double(tab, 768, 1536)
    copy(("dam16", 0, 192), ("damI", 0, 192))
    copy(("sire16", 192, 384), ("sireI", 192, 384))
    copy(("dam16", 192, 384), ("damI", 192, 384))
    ts(("AI", 0, 128), ("damI", 384, 512), 15, ALU.bitwise_and)
    copy(("c16", 0, 64), ("damI", 384, 448))
    sires1(1)
    take("A", ("xt", 0, 512), ("pA", 0, 512), 16)
    for n, (r, c) in enumerate(((2, 0), (3, 0), (0, 8), (1, 8))):
        mm(("pC", 8 * n, 8 * n + 8), ("xt", 128 * r, 128 * r + 128), ("ident", c, c + 8), k=16)
    double(tab, 1536, VD[0])
    sires1(2)
    dams1(tab, 0)
    dams1(tab, 1)
    sires1(3)
    copy(("ms16", 0, 24), ("pC", 0, 24))
    ghosts1(1, tab, lambda: copy(("ms16", 26, 34), ("pC", 24, 32)))
    iota(("tabA", 0, Z0), [[0, Z0]], 0, 0)
    iota(("tabB", 0, Z0), [[0, Z0]], 0, 0)
    iota(("W2", 0, 900), [[0, 900]], 0, 0)
    double_rest(1, tab)
    act(("dmo", 0, 16), ("dmj", 0, 16), AF.Identity, 0.0, OWN)
    act(("dmh", 0, 16), ("dmj", 0, 16), AF.Identity, 0.0, HOWN)
    act(("nmn", 0, 256), ("cix", 0, 256), AF.Abs, PM, -1.0 / 64)
    dams1(tab, 2)
    dams1(tab, 3)
    ghosts2(1, tab, lambda: None)
    iota(("W2", 900, 3072), [[0, 2172]], 0, 0)
    dma("S", [(T.W2[r:128:16, 0:3072], T.sire[:, 192:384]) for r in own], "l_tr", [], [("W2", 0, 3072)])
    for b, r in (("bs2", s2), ("bd2", d2), ("bs1", own[0])):
        mark((b, 0, 128), [[-16, 8], [0, 16]], -r)
    iota(("one", 0, 128), [[0, 128]], 1, 0)
    select(("w3", 0, 128), ("one", 0, 128), [[-16, 8], [0, 16]], ALU.is_ge, 0.0, 0, 1)
    select(("blk", 0, 128), ("w3", 0, 128), [[16, 8], [0, 16]], ALU.is_ge, 0.0, 15, -1)
    iota(("zerob", 0, 144), [[0, 144]], 0, 0)
    for a in range(0, 3072, 512):
        b = a + 512
        act(("tmp", a, b), ((tab, Z0, OWN1), ("sire16", 192 + a // 16, 192 + b // 16)), AF.Identity)
        tt((tab, D2 + a, D2 + b), ((tab, Z0, E1), ("dam16", 192 + a // 16, 192 + b // 16)), ("tmp", a, b), ALU.add)

    def turn_keys(b):
        for i in range(8):
            mm(("pA" if i < 4 else "pB", 128 * (i % 4), 128 * (i % 4) + 128), (b, i, 1024, 8), ("ident", 0, 128))

    def rows(c0, piece):
        for k, (pb, n) in enumerate((("pA", piece), ("pB", 512))):
            for a in range(0, 512, n):
                scan(("sg", 512 * k + a, 512 * k + a + n), ("seg", 0, n), (pb, a, a + n), 0.0, ALU.mult, ALU.max)
                yield
        ts(("ri", 0, 64), ("sg", 15, 1024, 16), 32.0, ALU.mult)
        yield
        ts(("rb", 0, 64), ("ri", 0, 64), 15, ALU.bitwise_and)
        yield
        copy(("rbf", 0, 64), ("rb", 0, 64))
        mm(("pC", 0, 128), ("rbf", 0, 64), ("idb", 0, 128), m=64)
        yield
        take("V", ("rT", 0, 128), ("pC", 0, 128), 64)
        for h in range(2):
            mm(("pC", 128, 192), ("perm%d" % h, 0, 128), ("rT", h, 128, 2), h == 0, h == 1, k=64)
        yield
        ts(("row16", c0, c0 + 64), ("pC", 128, 192), -1.0, ALU.mult, 15.0, ALU.add)
        yield

    def running(o, buf, a, n, alu, piece):
        for k in range(0, n, piece):
            init = ("tmp", o + k - 1, o + k) if k else (0.0 if alu == ALU.max else 1.0e9)
            scan(("tmp", o + k, o + k + piece), (buf, a + 2 * k, a + 2 * k + 2 * piece, 2),
                 (buf, a + 2 * k + 1, a + 2 * k + 2 * piece, 2), init, alu, alu)
            yield

    def count(o, n, step, out):
        act(("junk", 0, n // step), ("tmp", o + step - 1, o + n, step), AF.Sign, ("tmp", o + n - 1, o + n), -1.0, out)

    KX, KN, RX, RN, CX, CN = [("cl", k, k + 1) for k in range(8, 14)]
    JB = [("cl", k, k + 1) for k in (2, 3)]
    BH = [("cl", 4, 5), ("cl", 5, 6)]
    WIN2, WIN3 = ("tabA", D2, D2 + 3072), ("tabB", X3, X3 + 1024)

    def founder_a(s, n):
        b = lambda k: ("cl", n + k, n + k + 1)
        ib = lambda k: ("ci", n + k, n + k + 1)
        ts(ib(0), s, 0.0625, ALU.mult, -15.0 / 32, ALU.add)
        ts(b(1), s, 192.0, ALU.mult, -200.0, ALU.add)
        ts(b(0), s, 3200.0, ALU.is_lt, s, ALU.mult)
        ts(b(2), s, 3200.0, ALU.is_ge)
        ts(("sm16", n, n + 1), ib(0), -3071.0, ALU.mult, b(1), ALU.add)
        yield

    def founder_b(n):
        ts(("sm16", n + 2, n + 3), ("cl", n + 3, n + 4), ("cl", n + 2, n + 3), ALU.mult, ("cl", n, n + 1), ALU.add)
        return ("sm16", n + 2, n + 3)

    def chain1(land):
        count(0, 1536, 8, KX)
        yield
        yield
        ts(("off16", 0, 16), ("i16", 0, 16), KX, ALU.add, 16.0, ALU.mult)
        yield
        tt(("mk", 0, 256), (WIN2, ("off16", 0, 16)), ("nmx", 0, 256), ALU.add)
        yield
        red(RX, ("mk", 0, 256), ALU.max)
        yield
        ts(CX, RX, ("tmp", 1535, 1536), ALU.subtract, -64.0 * 192, ALU.mult)
        yield
        ts(("sm16", 16, 17), CX, KX, ALU.add, 15.0 * 192, ALU.add)
        yield
        tt(("lk", 0, 16), (("W2", 0, 3072), ("sm16", 16, 17)), ("dmo", 0, 16), ALU.mult)
        yield
        red(("cl", 17, 18), ("lk", 0, 16))
        yield
        yield from founder_a(("cl", 17, 18), 20)
        tt(("lk", 16, 32), (("W", 8, WW), ("sm16", 20, 21)), ("dmo", 0, 16), ALU.mult)
        yield
        red(("cl", 23, 24), ("lk", 16, 32))
        yield
        f = founder_b(20)
        yield
        tt(("lk", 32, 48), (("trI", 0, 3072), f), ("dmh", 0, 16), ALU.mult)
        yield
        red((land, 4 * rank, 4 * rank + 1), ("lk", 32, 48))

    def best_a(r):
        k = 16 * (r - 1)
        ts(("bR", k, k + 16), ("dmj", 0, 16), JB[r - 1], ALU.mult)
        mm(("pY", 128 + k, 144 + k), ("blk", 0, 128), ("bR", k, k + 16))

    def best1():
        ts(("off16", 16, 32), ("i16", 0, 16), KN, ALU.subtract, 16.0, ALU.mult)
        tt(("mk", 256, 512), (WIN2, ("off16", 16, 32)), ("nmn", 0, 256), ALU.add)
        red(RN, ("mk", 256, 512), ALU.min)
        yield
        ts(CN, RN, ("tmp", 3071, 3072), ALU.subtract, 64.0, ALU.mult)
        yield
        ts(("sm16", 48, 49), CN, 192.0, ALU.mult, KN, ALU.subtract)
        ts(JB[0], KN, -16.0, ALU.mult, CN, ALU.add)
        copy(("bg", 0, 16), (("W", 8, WW), ("sm16", 48, 49)))
        mm(("pM", 256, 272), ("bs2", 0, 128), ("bg", 0, 16))
        mm(("pM", 272, 288), ("bd2", 0, 128), ("bg", 0, 16))
        best_a(1)
        yield
        tt(("bm", 0, 32), ("pM", 256, 288), ("dmj", 0, 32), ALU.mult)
        ts(("bT", 0, 16), ("pY", 128, 144), PS2, ALU.mult)
        scan(("bsc", 0, 32), ("seg", 0, 32), ("bm", 0, 32), 0.0, ALU.mult, ALU.add)
        yield
        copy(("ms16", 24, 35, 10), ("bsc", 15, 32, 16))
        yield

    def best_lines():
        yield from founder_a(("bsc", 15, 16), 32)
        copy(("bg2", 0, 16), (("W", 8, WW), ("sm16", 32, 33)))
        mm(("pM", 288, 304), ("bs1", 0, 128), ("bg2", 0, 16))
        yield
        tt(("bm2", 0, 16), ("pM", 288, 304), ("dmj", 0, 16), ALU.mult)
        yield
        red(("cl", 35, 36), ("bm2", 0, 16))
        yield
        f = founder_b(32)
        yield
        ts(("yt16", 16, 32), (("trI", 0, 3072), f), OWN, ALU.mult)
        yield
        tt(("yt16", 0, 16), ("yt16", 16, 32), ("bT", 0, 16), ALU.add)
        yield

    def aims(r, land):
        act(("lk", 96, 100), (land, 0, 16, 4), AF.Identity, accum=BH[r - 1])

    def keys1(a):
        act(("T4", a, a + 512), ((tab, Z0, E2), ("c16", a // 16, a // 16 + 32)), AF.Identity, KB)

    dam_terms()
    act(("nmx", 0, 256), ("nmn", 0, 256), AF.Identity, 15.0 / 64, -1.0)
    keys1(0)
    run(running(0, tab, D2, 1536, ALU.max, 1536))
    least = running(1536, tab, D2, 1536, ALU.min, 128)
    first_chain = chain1("land1")
    run(first_chain, 1)
    run(least, 1)
    ts(("pos16", 0, 128), ("pM", 0, 128), -392.0 - 6400.0, ALU.add)
    keys1(512)
    turn_keys("T4")
    parents(0, 1024)
    weave(first_chain, least)
    share_aim("land1", "a_aim1")
    mark(("idb", 0, 128), [[-1, 128]], 0, on="zerob")
    for h in range(2):
        mark(("perm%d" % h, 0, 128), [[-1, 8], [1000, 2], [-8, 8]], -1000 * h, on="zerob")
    mark(("ZS", 0, 144), ROW, -s2 - 15000)
    mark(("ZSb", 0, 144), ROW, -s2 - 15000, on="zerob")
    mark(("ZB", 0, 144), ROW, -d2 - 15000, on="ZSb")
    run(least)
    parents(1024, 1536)
    count(1536, 1536, 8, KN)
    parents(1536, 2048)
    turn_flat("pS", 0, 128, 16, 0, 4)
    aims(1, "land1")
    run(founders(BH[0], 800))
    lines = best_lines()
    step = {"best": best1(), "rows": rows(0, 256), "line": lines,
            "double": (double("tabB", a, a + 200) for a in range(0, 800, 200))}
    for name in "best rows best rows best rows rows best rows best line rows line rows".split():
        run(step[name], 1)
    turn_flat("pS", 0, 128, 16, 4, 16)
    weave(step["double"], lines)
    run(step["rows"])

    def generation1(r, tab, done, part, filler, after, last):
        for a in range(done, VD[r - 1], 800):
            double(tab, a, a + 800)
        ghosts1(r, tab, lambda: run(filler, 1))
        for k in range(len(part) - 1):
            sires1(k, part)
            dams1(tab, k, part)
            if k in after:
                after[k]()
        double_rest(r, tab)
        ghosts2(r, tab, last)

    def generation3(r, tab, k):
        a, b, o = 512 * k, 512 * k + 512, GS2 + 144 * (r - 1) + 128
        act(("tmp2", a, b), ((tab, 0, E1), ("US16", 32 * k, 32 * k + 32)), AF.Identity)
        tt(("T3", a, b), (("gs", o, o + 16), ("row16", 32 * k, 32 * k + 32)), ("tmp2", a, b), ALU.add)

    def generation3_end(tab, k, out, o):
        a, b = 512 * k, 512 * k + 512
        tt((out, o + a, o + b), ((tab, Z0, X3), ("UD16", 32 * k, 32 * k + 32)), ("T3", a, b), ALU.add)

    def extreme3(o, K, U2, n, dm, cmp, out):
        sign = 2.0 if cmp == ALU.is_lt else -2.0
        ts(("sm16", n, n + 1), K, sign, ALU.mult)
        ts(U2, K, sign, ALU.mult)
        tt(("lk", n + 24, n + 40), (WIN3, ("sm16", n, n + 1)), dm, ALU.mult)
        yield
        red(("cl", n, n + 1), ("lk", n + 24, n + 40))
        yield
        ts(out, ("cl", n, n + 1), ("tmp", o + 511, o + 512), cmp, U2, ALU.add)
        yield

    def both_lists():
        take("V", ("xt", 0, 256), ("pS", 0, 256), 128)
        turn_back(0)
        turn_back(1)

    tab = "tabB"
    generation1(2, tab, 800, PART, lines, {0: lambda: run(lines), 1: both_lists, 3: lambda: u_s(0)}, lambda: u_d(0))
    generation3(2, tab, 0)
    generation3(2, tab, 1)
    act(("sy", 0, 1024), (("yt16", 0, 16), ("row16", 0, 64)), AF.Identity)
    u_s(1)
    act(("T4", 0, 1024), ((tab, 0, E1), ("US16", 64, 128)), AF.Identity, KB)
    generation3_end(tab, 0, tab, X3)
    generation3_end(tab, 1, tab, X3)
    run(running(0, tab, X3, 512, ALU.max, 512))
    count(0, 512, 1, KX)
    copy(("gs", GS3, GS3 + 128), (WIN3, ("mg16", 24, 32)))
    ship("gs", GS3, tab, G3X, "a_g32")
    u_d(1)
    run(running(512, tab, X3, 512, ALU.min, 512))
    run(extreme3(0, KX, RX, 40, ("dmo", 0, 16), ALU.is_lt, ("sm16", 42, 43)))
    tt(("lk", 48, 64), (("sy", 0, 1024), ("sm16", 42, 43)), ("dmh", 0, 16), ALU.mult)
    red(("land2", 4 * rank, 4 * rank + 1), ("lk", 48, 64))
    share_aim("land2", "a_aim2")
    count(512, 512, 1, KN)
    keys = (tt(("key", a, a + 256), ((tab, Z0, TW), ("UD16", 64 + a // 16, 80 + a // 16)), ("T4", a, a + 256), ALU.add)
            for a in range(0, 1024, 256))
    weave(extreme3(512, KN, RN, 56, ("dmj", 0, 16), ALU.is_gt, JB[1]), keys)
    best_a(2)
    copy(("mg16", 32, 33), JB[1])
    run(keys)
    turn_keys("key")
    to_list("pE", 0, "ZS", "sy")
    aims(2, "land2")
    run(founders(BH[1], 800))
    ts(("bH", 0, 16), ("pY", 144, 160), SGN, ALU.mult)
    ts(("bR", 0, 16), ("pY", 144, 160), PD2, ALU.mult)
    for r in range(2):
        ts(("yto", r, r + 1), BH[r], 2.0, ALU.mult)
    tt(("bT", 16, 32), ("bR", 0, 16), ("bH", 0, 16), ALU.add)
    dma("S", [(T.yt[:], T.yto[:])], "o_yt", [("yto", 0, 2)], [])

    tab = "tabA"
    last_rows = rows(64, 512)
    generation1(3, tab, 0, EVEN, last_rows, {}, lambda: run(last_rows, 1))
    run(last_rows, 1)
    ts(("yso", 0, 64), ("pE", 0, 64), 6400.0, ALU.add)
    run(last_rows, 2)
    for k in range(2):
        generation3(3, tab, k)
        run(last_rows, 1)
    act(("T4", 0, 1024), ((tab, 0, E1), ("US16", 64, 128)), AF.Identity)
    act(("sf", 0, 1024), (("bT", 16, 32), ("row16", 64, 128)), AF.Identity)
    to_list("pE", 64, "ZB", "sf")
    for k in range(2):
        a, b = 512 * k, 512 * k + 512
        generation3_end(tab, k, "G3", 0)
        act(("yo", a, b), ("G3", a, b), AF.Identity, 65535.0, -0.25)
        dma("S", [(T.yf[:, a:b], T.yo[:, a:b])], "o_f3%d" % k, [("yo", a, b)], [])
    o = GS3 + 144
    ts(("gs", o, o + 144), (("G3", 0, 1024), ("mg16", 24, 33)), 0.5, ALU.mult)
    ship("gs", o, tab, G3X, "a_g33")
    act((tab, X3, X3 + 1024), ("G3", 0, 1024), AF.Identity, 0.0, 0.5)
    tt(("T3", 0, 1024), (("gs", o + 128, o + 144), ("row16", 64, 128)), ("T4", 0, 1024), ALU.add)
    act(("yso", 64, 128), ("pE", 64, 128), AF.Identity, 9600.0)
    dma("S", [(T.ys[:], T.yso[:])], "o_ys", [("yso", 0, 128)], [])
    b = 0
    for k, n in enumerate((320, 320, 192, 192)):
        a, b = b, b + n
        tt(("key", a, b), ((tab, Z0, TW), ("UD16", 64 + a // 16, 64 + b // 16)), ("T3", a, b), ALU.add)
        act(("yo", 1024 + a, 1024 + b), ("key", a, b), AF.Identity, 65535.0, -0.25)
        dma("S", [(T.yf[:, 1024 + a:1024 + b], T.yo[:, 1024 + a:1024 + b])], "o_f4%d" % k, [("yo", 1024 + a, 1024 + b)], [])

    for s in sorted(total):
        if known["G"].get(s, 0) < total[s]:
            g.wait_ge(T.sem[s], total[s])
    g.wait_ge(T.sem.sent, sent[0])
